import numpy as np
import ml_dtypes


def mxq(x, axis, fmt="e4m3"):
    dtype, down = {"e4m3": (ml_dtypes.float8_e4m3fn, 7), "e5m2": (ml_dtypes.float8_e5m2, 14)}[fmt]
    v = np.moveaxis(np.asarray(x, np.float32).astype(ml_dtypes.bfloat16).astype(np.float64), axis, -1)
    blocks = v.reshape(v.shape[:-1] + (-1, 32))
    amax = np.abs(blocks).max(-1, keepdims=True)
    byte = np.maximum(np.where(amax > 0, np.frexp(amax)[1] - 1 + 127, 0) - down, 1)
    scale = np.exp2(byte - 127.0)
    codes = (blocks / scale).astype(np.float32).astype(dtype).astype(np.float64)
    return np.moveaxis((codes * scale).reshape(v.shape), -1, axis)


WIDE = False


def mx_kscale(k):
    if not WIDE:
        return np.ones(k)
    levels = np.array([24, -24, 12, -12, 0])
    if k % 512:
        return np.exp2(np.random.permutation(np.resize(levels, k // 32))).repeat(32)
    a = np.empty((k // 512, 16))
    for p in range(k // 512):
        a[p, :8] = np.random.permutation(np.resize(levels, 8))
        for g in range(8):
            far = levels[np.abs(levels - a[p, g]) >= 10]
            a[p, g + 8] = far[np.random.randint(len(far))]
    return np.exp2(a.ravel()).repeat(32)


def f64(x):
    return np.asarray(x).astype(np.float64)


def striped(idx):
    return np.tile(idx.reshape(-1, 16).T, (8, 1)).astype(np.uint16)


def unstriped(offs):
    return offs[:16].T.reshape(-1).astype(np.int64)


E2M1 = np.array([0.0, 0.5, 1.0, 1.5, 2.0, 3.0, 4.0, 6.0, -0.0, -0.5, -1.0, -1.5, -2.0, -3.0, -4.0, -6.0])


def pack_weight(w, fmt):
    k, n = w.shape
    w = f64(np.asarray(w, np.float32).astype(ml_dtypes.bfloat16)).reshape(k // 32, 32, n)
    amax = np.abs(w).max(1)
    if fmt == "e4m3":
        byte = np.frexp(amax)[1] - 1 + 127 - 7
    else:
        mant, ex = np.frexp(amax / 6.0)
        byte = np.where(mant > 0.5, ex, ex - 1) + 127
    byte = np.clip(np.where(amax > 0, byte, 1), 1, 254)
    scaled = (w * np.exp2(127.0 - byte)[:, None, :]).reshape(k, n).astype(np.float32)
    by_word = np.ascontiguousarray(scaled.reshape(k // 512, 128, 4, n).transpose(0, 1, 3, 2))
    if fmt == "e4m3":
        words = by_word.astype(ml_dtypes.float8_e4m3fn).view(np.uint8)
    else:
        c = by_word.astype(ml_dtypes.float4_e2m1fn).view(np.uint8) & 0xF
        words = (c[..., 0::2] | (c[..., 1::2] << 4)).reshape(k // 512, 128, 2 * n)
    return np.ascontiguousarray(words), np.ascontiguousarray(byte.astype(np.uint8).reshape(k // 512, 16, n))


def unpack_weight(words, scales, fmt):
    g, _, n = scales.shape
    words = np.ascontiguousarray(words).reshape(g, 128, n, -1)
    if fmt == "e4m3":
        vals = words.view(ml_dtypes.float8_e4m3fn).astype(np.float64)
    else:
        nib = np.empty((g, 128, n, 4), np.uint8)
        nib[..., 0::2] = words & 0xF
        nib[..., 1::2] = words >> 4
        vals = E2M1[nib]
    vals = vals * np.repeat(np.exp2(scales.astype(np.float64) - 127.0), 8, axis=1)[..., None]
    return vals.transpose(0, 1, 3, 2).reshape(g * 512, n)


def pack_table4(v):
    words, scales = pack_weight(v, "e2m1")
    g, t = words.shape[0] // 2, v.shape[1]
    return np.ascontiguousarray(words.reshape(g, 2, 128, t, 2).transpose(0, 2, 3, 1, 4).reshape(g, 128, t, 4)), scales


def unpack_table4(words, scales):
    g, _, t, _ = words.shape
    return unpack_weight(words.reshape(g, 128, t, 2, 2).transpose(0, 3, 1, 2, 4).reshape(2 * g, 128, 2 * t), scales, "e2m1")


K, L, R, N, T, J = 1024, 512, 1024, 1024, 4096, 1024


def setup_inputs():
    n = np.random.standard_normal
    s = mx_kscale(K)[:, None]
    s2 = mx_kscale(L)[:, None]
    u = mx_kscale(R)[:, None]
    p_tab = pack_table4(n((K, T)) * s)
    p_tab2 = pack_weight(n((L, T)) * s2, "e4m3")
    p_wa = pack_weight(n((K, R)) / np.sqrt(K) / s * u.T, "e4m3")
    p_en = pack_weight(n((R, N)) / np.sqrt(R) / u, "e2m1")
    return {
        "tab_words": p_tab[0],
        "tab_scales": p_tab[1],
        "tab2_words": p_tab2[0],
        "tab2_scales": p_tab2[1],
        "wa_words": p_wa[0],
        "wa_scales": p_wa[1],
        "wb": (n((L, R)) / np.sqrt(L) / s2 * u.T).astype(np.float32),
        "en_words": p_en[0],
        "en_scales": p_en[1],
        "b": (0.3 * n(N)).astype(np.float32),
        "offs": striped(np.random.permutation(T)[:J]),
        "offs2": striped(np.random.permutation(T)[:J]),
    }


def reference(tab_words, tab_scales, tab2_words, tab2_scales, wa_words, wa_scales, wb, en_words, en_scales, b, offs, offs2):
    idx = unstriped(offs)
    idx2 = unstriped(offs2)
    tab_ = unpack_table4(tab_words, tab_scales)[:, idx]
    tab2_ = unpack_weight(tab2_words, tab2_scales, "e4m3")[:, idx2]
    wa_ = unpack_weight(wa_words, wa_scales, "e4m3")
    wb_ = mxq(f64(wb), 0, "e4m3")
    ha = wa_.T @ tab_
    hb = wb_.T @ tab2_
    h = np.maximum(ha, hb)
    h_ = mxq(h, 0, "e4m3")
    en_ = unpack_weight(en_words, en_scales, "e2m1")
    y = en_.T @ h_
    return y + f64(b)[:, None]

@@ -1,0 +1,249 @@
+from contextlib import ExitStack
+
+import concourse.mybir as mybir
+from concourse.masks import make_identity
+
+K, L, R, N, T, J = 1024, 512, 1024, 1024, 4096, 1024
+FLOPS = 2 * J * (K * R + L * R + R * N)
+
+F32 = mybir.dt.float32
+BF16 = mybir.dt.bfloat16
+I32 = mybir.dt.int32
+U32 = mybir.dt.uint32
+U16 = mybir.dt.uint16
+U8 = mybir.dt.uint8
+FP8X4 = mybir.dt.float8_e4m3fn_x4
+FP4X4 = mybir.dt.float4_e2m1fn_x4
+MAX = mybir.AluOpType.max
+IDENTITY = mybir.ActivationFunctionType.Identity
+
+P = 128
+PASS = 512
+HALF = 512
+UNIT = 128
+PARKED = 12
+TAB2_ROW = 8
+LEAD = 10
+
+
+def tile_list_kg_max_bias_kernel(
+    tc, tab_words, tab_scales, tab2_words, tab2_scales, wa_words, wa_scales, wb, en_words, en_scales, b, offs, offs2, out
+):
+    nc = tc.nc
+    with ExitStack() as ctx:
+        lists = ctx.enter_context(tc.tile_pool(name="lists", bufs=1))
+        keep = ctx.enter_context(tc.tile_pool(name="keep", bufs=1))
+        placed = ctx.enter_context(tc.tile_pool(name="placed", bufs=1))
+        stage = ctx.enter_context(tc.tile_pool(name="stage", bufs=6))
+        acc_pool = ctx.enter_context(tc.psum_pool(name="acc", bufs=5))
+        hb_pool = ctx.enter_context(tc.psum_pool(name="hb", bufs=3))
+
+        def held(name, shape, dtype, tag=None):
+            return keep.tile(shape, dtype, name=name, tag=tag or name, align_bytes=64)
+
+        def at(name, shape, dtype, offset):
+            return placed.tile(shape, dtype, name=name, tag=name, align_bytes=64, offset=offset)
+
+        idx = lists.tile([P, J // 16], U16, name="idx")
+        idx2 = lists.tile([P, J // 16], U16, name="idx2")
+        nc.sync.dma_start(idx[:], offs)
+        nc.sync.dma_start(idx2[:], offs2)
+
+        tab_win = held("tab_win", [P, T], U32, tag="slot_h")
+        nc.sync.dma_start(tab_win[:].bitcast(I32), tab_words[0].rearrange("p t i -> p (t i)").bitcast(I32))
+        wa_hbm = wa_words.rearrange("a p r i -> p a (r i)")
+        wa_raw = []
+        for g in range(2):
+            raw = held("wa_raw%d" % g, [P, 2, PASS], I32, tag=("slot_f", "slot_g")[g])
+            nc.sync.dma_start(raw[:], wa_hbm[:, :, 4 * PASS * g : 4 * PASS * (g + 1)].bitcast(I32))
+            wa_raw.append(raw)
+
+        tab_sc_win = at("tab_sc_win", [P, T], U8, 14 * 1024)
+        nc.vector.memset(tab_sc_win[:].bitcast(I32), 0)
+        nc.scalar.dma_start(tab_sc_win[PARKED : PARKED + 16, :].bitcast(I32), tab_scales[1].bitcast(I32))
+        for q in range(4):
+            nc.scalar.dma_start(tab_sc_win[32 * q : 32 * q + 4, :].bitcast(I32), tab_scales[0, 4 * q : 4 * q + 4, :].bitcast(I32))
+
+        wa_sc_raw = held("wa_sc_raw", [P, 2, R], U8, tag="slot_d")
+        nc.gpsimd.memset(wa_sc_raw[:].bitcast(I32), 0)
+        for q in range(4):
+            nc.gpsimd.dma_start(
+                wa_sc_raw[32 * q : 32 * q + 4, :, :].bitcast(I32),
+                wa_scales[:, 4 * q : 4 * q + 4, :].rearrange("a r n -> r a n").bitcast(I32),
+            )
+
+        tab2_sc_win = held("tab2_sc_win", [P, T], U8, tag="slot_e")
+        nc.vector.memset(tab2_sc_win[:].bitcast(I32), 0)
+        for q in range(4):
+            row = 32 * q + TAB2_ROW
+            nc.scalar.dma_start(tab2_sc_win[row : row + 4, :].bitcast(I32), tab2_scales[0, 4 * q : 4 * q + 4, :].bitcast(I32))
+
+        bias_rows = held("bias_rows", [P, P], F32)
+        ident = held("ident", [P, P], F32)
+        bias = held("bias", [P, N // P], F32)
+        nc.vector.memset(bias_rows[:], 0.0)
+        nc.gpsimd.dma_start(bias_rows[0 : N // P, :], b.rearrange("(c p) -> c p", p=P))
+        make_identity(nc, ident[:])
+        bias_ps = acc_pool.tile([P, PASS], F32, name="acc")
+        nc.tensor.transpose(bias_ps[:, 0:P], bias_rows[:], ident[:])
+        nc.scalar.copy(bias[:], bias_ps[:, 0 : N // P])
+
+        tab_sc0 = held("tab_sc0", [P, J], U8)
+        tab_sc1 = held("tab_sc1", [P, J], U8)
+        nc.vector.memset(tab_sc1[:].bitcast(I32), 0)
+        nc.vector.tensor_copy(tab_sc0[:], tab_sc_win[:].indirect(idx[:]))
+        for q in range(4):
+            nc.scalar.dma_start(
+                tab_sc1[32 * q : 32 * q + 4, :].bitcast(I32), tab_sc0[PARKED + 4 * q : PARKED + 4 * q + 4, :].bitcast(I32)
+            )
+        tab_sc = [tab_sc0, tab_sc1]
+
+        tab2_win = at("tab2_win", [P, T], U32, 0)
+        nc.sync.dma_start(tab2_win[:].bitcast(I32), tab2_words[0].rearrange("p t i -> p (t i)").bitcast(I32))
+        wb_hbm = wb.rearrange("(p i) r -> p i r", i=4)
+
+        def list_half(offsets, c):
+            return offsets[:, c * HALF // 16 : (c + 1) * HALF // 16]
+
+        def gather_tab(c, pairs):
+            words = held("tab_g%d" % c, [P, 2, 2 * HALF], U8)
+            nc.vector.tensor_copy(pairs[:], tab_win[:].indirect(list_half(idx, c)))
+            nc.vector.tensor_copy(words[:].bitcast(U16), pairs[:].bitcast(U16).rearrange("p (j d) -> p d j", d=2))
+            return words
+
+        def order_wa_scales(g):
+            scales = held("wa_sc%d" % g, [P, 2, PASS], U8)
+            nc.vector.tensor_copy(
+                scales[:].rearrange("p a (t m) -> p a t m", t=4),
+                wa_sc_raw[:, :, PASS * g : PASS * (g + 1)].rearrange("p a (m t) -> p a t m", t=4),
+            )
+            return scales
+
+        def order_wa_words(g, words):
+            nc.vector.tensor_copy(
+                words[:].rearrange("p a (t m i) -> p a m t i", t=4, i=4),
+                wa_raw[g][:].rearrange("p a (m i t) -> p a m t i", t=4, i=4),
+            )
+            return words
+
+        tab_g = [gather_tab(0, at("tab_pairs0", [P, HALF], U32, 16 * 1024))]
+        wa = [(order_wa_words(0, at("wa0", [P, 2, PASS], I32, 16 * 1024)), order_wa_scales(0))]
+        scales1 = order_wa_scales(1)
+        wa.append((order_wa_words(1, held("wa1", [P, 2, PASS], I32, tag="slot_d")), scales1))
+        tab_g.append(gather_tab(1, held("tab_pairs1", [P, HALF], U32, tag="slot_g")))
+
+        wb_raw = []
+        for g, tag in enumerate(("slot_f", "slot_h")):
+            raw = held("wb_raw%d" % g, [P, 4, PASS], F32, tag=tag)
+            nc.sync.dma_start(raw[:], wb_hbm[:, :, PASS * g : PASS * (g + 1)])
+            wb_raw.append(raw)
+
+        tab2_sc = held("tab2_sc", [P, J], U8, tag="slot_g")
+        nc.vector.tensor_copy(tab2_sc[:], tab2_sc_win[:].indirect(idx2[:]))
+
+        en_sc = held("en_sc", [P, 2, N], U8, tag="slot_e")
+        nc.vector.memset(en_sc[:].bitcast(I32), 0)
+        for q in range(4):
+            nc.sync.dma_start(
+                en_sc[32 * q : 32 * q + 4, :, :].bitcast(I32),
+                en_scales[:, 4 * q : 4 * q + 4, :].rearrange("a r n -> r a n").bitcast(I32),
+            )
+
+        tab2_g = []
+        for c in range(2):
+            words = held("tab2_g%d" % c, [P, HALF], U32)
+            nc.vector.tensor_copy(words[:], tab2_win[:].indirect(list_half(idx2, c)))
+            tab2_g.append(words)
+        en = at("en", [P, 2, 2 * N], U8, 0)
+        nc.sync.dma_start(en[:].bitcast(I32), en_words.rearrange("a p c -> p a c").bitcast(I32))
+
+        def quantise_wb(g, copy, rounded):
+            words = held("wb%d" % g, [P, PASS], U32)
+            scales = held("wb_sc%d" % g, [P, PASS], U8)
+            copy(rounded[:].rearrange("p (t m i) -> p m t i", t=4, i=4), wb_raw[g][:].rearrange("p i (m t) -> p m t i", t=4))
+            nc.vector.quantize_mx(out=words[:].bitcast(FP8X4), scales=scales[:], in_=rounded[:])
+            return words, scales
+
+        def project_a(c, g, u):
+            words, scales = wa[g]
+            bank = acc_pool.tile([P, 4, UNIT], F32, name="acc")
+            for a in range(2):
+                for t in range(4):
+                    nc.tensor.matmul_mx(
+                        out=bank[:, t, :],
+                        lhsT=words[:, a, P * t : P * (t + 1)].bitcast(FP8X4),
+                        lhsT_scale=scales[:, a, P * t : P * (t + 1)],
+                        rhs=tab_g[c][:, a, 2 * UNIT * u : 2 * UNIT * (u + 1)].bitcast(FP4X4),
+                        rhs_scale=tab_sc[a][:, HALF * c + UNIT * u : HALF * c + UNIT * (u + 1)],
+                        start=(a == 0 and t == 0),
+                        stop=(a == 1 and t == 3),
+                    )
+            ha = held("ha%d%d%d" % (c, g, u), [P, 4 * UNIT], F32)
+            nc.scalar.copy(ha[:].rearrange("p (j t) -> p j t", t=4), bank[:].rearrange("p t j -> p j t"))
+            return ha
+
+        def join(c, g, u, ha, wbq, rounded):
+            words, scales = wbq
+            bank = hb_pool.tile([P, 4, UNIT], F32, name="hb")
+            for t in range(4):
+                nc.tensor.matmul_mx(
+                    out=bank[:, t, :],
+                    lhsT=words[:, P * t : P * (t + 1)].bitcast(FP8X4),
+                    lhsT_scale=scales[:, P * t : P * (t + 1)],
+                    rhs=tab2_g[c][:, UNIT * u : UNIT * (u + 1)].bitcast(FP8X4),
+                    rhs_scale=tab2_sc[TAB2_ROW:P, HALF * c + UNIT * u : HALF * c + UNIT * (u + 1)],
+                    start=True,
+                    stop=True,
+                )
+            nc.vector.tensor_tensor(
+                rounded.rearrange("p (j t) -> p j t", t=4),
+                bank[:].rearrange("p t j -> p j t"),
+                ha[:].rearrange("p (j t) -> p j t", t=4),
+                MAX,
+            )
+
+        units = [(c, g, u) for c in range(2) for g in range(2) for u in range(4)]
+        ha = {unit: project_a(*unit) for unit in units[:LEAD]}
+        wbq = {0: quantise_wb(0, nc.vector.tensor_copy, held("wb_bf0", [P, 4 * PASS], BF16))}
+        h = {}
+        for c in range(2):
+            for g in range(2):
+                h[c, g] = (held("h%d%d" % (c, g), [P, HALF], U32), held("h_sc%d%d" % (c, g), [P, HALF], U8))
+        waiting = []
+        for n, (c, g, u) in enumerate(units):
+            if (c, g, u) == (0, 1, 0):
+                wbq[1] = quantise_wb(1, nc.scalar.copy, at("wb_bf1", [P, 4 * PASS], BF16, 16 * 1024))
+            s = u % 2
+            if s == 0:
+                rounded = held("h_bf%d" % n, [P, 8 * UNIT], BF16)
+            join(c, g, u, ha[c, g, u], wbq[g], rounded[:, 4 * UNIT * s : 4 * UNIT * (s + 1)])
+            if s == 0 and waiting:
+                nc.vector.quantize_mx(**waiting.pop())
+            if s == 1:
+                words, scales = h[c, g]
+                cols = slice(UNIT * (u - 1), UNIT * (u + 1))
+                waiting.append(dict(out=words[:, cols].bitcast(FP8X4), scales=scales[:, cols], in_=rounded[:]))
+            if LEAD + n < len(units):
+                ha[units[LEAD + n]] = project_a(*units[LEAD + n])
+        nc.vector.quantize_mx(**waiting.pop())
+
+        for c in range(2):
+            for nt in range(N // P):
+                bank = acc_pool.tile([P, HALF], F32, name="acc")
+                for g in range(2):
+                    words, scales = h[c, g]
+                    nc.tensor.matmul_mx(
+                        out=bank[:],
+                        lhsT=en[:, g, 2 * P * nt : 2 * P * (nt + 1)].bitcast(FP4X4),
+                        lhsT_scale=en_sc[:, g, P * nt : P * (nt + 1)],
+                        rhs=words[:].bitcast(FP8X4),
+                        rhs_scale=scales[:],
+                        start=(g == 0),
+                        stop=(g == 1),
+                    )
+                scores = stage.tile([P, HALF], F32, name="scores")
+                if c == 1 and nt % 2 == 1:
+                    nc.vector.tensor_scalar_add(scores[:], bank[:], bias[:, nt : nt + 1])
+                else:
+                    nc.scalar.activation(scores[:], bank[:], IDENTITY, bias=bias[:, nt : nt + 1])
+                nc.sync.dma_start(out[P * nt : P * (nt + 1), HALF * c : HALF * (c + 1)], scores[:])

@@ -1,7 +1,6 @@
 from contextlib import ExitStack
 
 import concourse.mybir as mybir
-from concourse.masks import make_identity
 
 K, L, R, N, T, J = 1024, 512, 1024, 1024, 4096, 1024
 FLOPS = 2 * J * (K * R + L * R + R * N)
@@ -24,6 +23,8 @@ UNIT = 128
 PARKED = 12
 TAB2_ROW = 8
 LEAD = 10
+KB = 1024
+ACC_BANKS = 5
 
 
 def tile_list_kg_max_bias_kernel(
@@ -35,7 +36,7 @@ def tile_list_kg_max_bias_kernel(
         keep = ctx.enter_context(tc.tile_pool(name="keep", bufs=1))
         placed = ctx.enter_context(tc.tile_pool(name="placed", bufs=1))
         stage = ctx.enter_context(tc.tile_pool(name="stage", bufs=6))
-        acc_pool = ctx.enter_context(tc.psum_pool(name="acc", bufs=5))
+        acc_pool = ctx.enter_context(tc.psum_pool(name="acc", bufs=ACC_BANKS))
         hb_pool = ctx.enter_context(tc.psum_pool(name="hb", bufs=3))
 
         def held(name, shape, dtype, tag=None):
@@ -49,44 +50,48 @@ def tile_list_kg_max_bias_kernel(
         nc.sync.dma_start(idx[:], offs)
         nc.sync.dma_start(idx2[:], offs2)
 
-        tab_win = held("tab_win", [P, T], U32, tag="slot_h")
+        zeros = at("zeros", [P, 544], F32, 16 * KB - 64)
+        ident = held("ident", [P, P], F32)
+        nc.gpsimd.memset(zeros[:, 0:P], 0.0)
+        nc.gpsimd.affine_select(
+            out=ident[:], in_=zeros[:, 0:P], compare_op=mybir.AluOpType.not_equal, fill=1.0, base=0, pattern=[[-1, P]], channel_multiplier=1
+        )
+
+        tab_sc_win = at("tab_sc_win", [P, T], U8, 28 * KB)
+        nc.gpsimd.memset(tab_sc_win[:, 0 : T // 2].bitcast(I32), 0)
+        nc.vector.memset(tab_sc_win[:, T // 2 : T].bitcast(I32), 0)
+        nc.sync.dma_start(tab_sc_win[PARKED : PARKED + 16, :].bitcast(I32), tab_scales[1].bitcast(I32))
+        for q in range(4):
+            nc.sync.dma_start(tab_sc_win[32 * q : 32 * q + 4, :].bitcast(I32), tab_scales[0, 4 * q : 4 * q + 4, :].bitcast(I32))
+
+        tab2_sc_win = at("tab2_sc_win", [P, T], U8, 60 * KB)
+        wa_sc_raw = at("wa_sc_raw", [P, 2, R], U8, 16 * KB)
+        bias_rows = held("bias_rows", [P, P], F32)
+        nc.vector.memset(bias_rows[:], 0.0)
+        nc.vector.memset(tab2_sc_win[:].bitcast(I32), 0)
+        nc.vector.memset(wa_sc_raw[:].bitcast(I32), 0)
+
+        tab_win = at("tab_win", [P, T], U32, 0)
         nc.sync.dma_start(tab_win[:].bitcast(I32), tab_words[0].rearrange("p t i -> p (t i)").bitcast(I32))
         wa_hbm = wa_words.rearrange("a p r i -> p a (r i)")
-        wa_raw = []
-        for g in range(2):
-            raw = held("wa_raw%d" % g, [P, 2, PASS], I32, tag=("slot_f", "slot_g")[g])
-            nc.sync.dma_start(raw[:], wa_hbm[:, :, 4 * PASS * g : 4 * PASS * (g + 1)].bitcast(I32))
-            wa_raw.append(raw)
+        wa_raw = [at("wa_raw0", [P, 2, PASS], I32, 18 * KB)]
+        nc.sync.dma_start(wa_raw[0][:], wa_hbm[:, :, 0 : 4 * PASS].bitcast(I32))
 
-        tab_sc_win = at("tab_sc_win", [P, T], U8, 14 * 1024)
-        nc.vector.memset(tab_sc_win[:].bitcast(I32), 0)
-        nc.scalar.dma_start(tab_sc_win[PARKED : PARKED + 16, :].bitcast(I32), tab_scales[1].bitcast(I32))
         for q in range(4):
-            nc.scalar.dma_start(tab_sc_win[32 * q : 32 * q + 4, :].bitcast(I32), tab_scales[0, 4 * q : 4 * q + 4, :].bitcast(I32))
-
-        wa_sc_raw = held("wa_sc_raw", [P, 2, R], U8, tag="slot_d")
-        nc.gpsimd.memset(wa_sc_raw[:].bitcast(I32), 0)
-        for q in range(4):
-            nc.gpsimd.dma_start(
+            nc.sync.dma_start(
                 wa_sc_raw[32 * q : 32 * q + 4, :, :].bitcast(I32),
                 wa_scales[:, 4 * q : 4 * q + 4, :].rearrange("a r n -> r a n").bitcast(I32),
             )
 
-        tab2_sc_win = held("tab2_sc_win", [P, T], U8, tag="slot_e")
-        nc.vector.memset(tab2_sc_win[:].bitcast(I32), 0)
-        for q in range(4):
-            row = 32 * q + TAB2_ROW
-            nc.scalar.dma_start(tab2_sc_win[row : row + 4, :].bitcast(I32), tab2_scales[0, 4 * q : 4 * q + 4, :].bitcast(I32))
-
-        bias_rows = held("bias_rows", [P, P], F32)
-        ident = held("ident", [P, P], F32)
         bias = held("bias", [P, N // P], F32)
-        nc.vector.memset(bias_rows[:], 0.0)
         nc.gpsimd.dma_start(bias_rows[0 : N // P, :], b.rearrange("(c p) -> c p", p=P))
-        make_identity(nc, ident[:])
         bias_ps = acc_pool.tile([P, PASS], F32, name="acc")
         nc.tensor.transpose(bias_ps[:, 0:P], bias_rows[:], ident[:])
         nc.scalar.copy(bias[:], bias_ps[:, 0 : N // P])
+
+        for q in range(4):
+            row = 32 * q + TAB2_ROW
+            nc.gpsimd.dma_start(tab2_sc_win[row : row + 4, :].bitcast(I32), tab2_scales[0, 4 * q : 4 * q + 4, :].bitcast(I32))
 
         tab_sc0 = held("tab_sc0", [P, J], U8)
         tab_sc1 = held("tab_sc1", [P, J], U8)
@@ -98,9 +103,11 @@ def tile_list_kg_max_bias_kernel(
             )
         tab_sc = [tab_sc0, tab_sc1]
 
-        tab2_win = at("tab2_win", [P, T], U32, 0)
-        nc.sync.dma_start(tab2_win[:].bitcast(I32), tab2_words[0].rearrange("p t i -> p (t i)").bitcast(I32))
         wb_hbm = wb.rearrange("(p i) r -> p i r", i=4)
+        wb_raw = [at("wb_raw0", [P, 4, PASS], F32, 22 * KB)]
+        nc.sync.dma_start(wb_raw[0][:], wb_hbm[:, :, 0:PASS])
+        wa_raw.append(at("wa_raw1", [P, 2, PASS], I32, 30 * KB))
+        nc.sync.dma_start(wa_raw[1][:], wa_hbm[:, :, 4 * PASS : 8 * PASS].bitcast(I32))
 
         def list_half(offsets, c):
             return offsets[:, c * HALF // 16 : (c + 1) * HALF // 16]
@@ -126,22 +133,23 @@ def tile_list_kg_max_bias_kernel(
             )
             return words
 
-        tab_g = [gather_tab(0, at("tab_pairs0", [P, HALF], U32, 16 * 1024))]
-        wa = [(order_wa_words(0, at("wa0", [P, 2, PASS], I32, 16 * 1024)), order_wa_scales(0))]
+        tab_g = [gather_tab(0, at("tab_pairs0", [P, HALF], U32, 34 * KB))]
+        tab2_win = at("tab2_win", [P, T], U32, 34 * KB)
+        nc.sync.dma_start(tab2_win[:].bitcast(I32), tab2_words[0].rearrange("p t i -> p (t i)").bitcast(I32))
+        wa = [(order_wa_words(0, held("wa0", [P, 2, PASS], I32, tag="slot_a")), order_wa_scales(0))]
         scales1 = order_wa_scales(1)
-        wa.append((order_wa_words(1, held("wa1", [P, 2, PASS], I32, tag="slot_d")), scales1))
-        tab_g.append(gather_tab(1, held("tab_pairs1", [P, HALF], U32, tag="slot_g")))
+        tab_g.append(gather_tab(1, at("tab_pairs1", [P, HALF], U32, 16 * KB)))
+        wa.append((order_wa_words(1, held("wa1", [P, 2, PASS], I32)), scales1))
 
-        wb_raw = []
-        for g, tag in enumerate(("slot_f", "slot_h")):
-            raw = held("wb_raw%d" % g, [P, 4, PASS], F32, tag=tag)
-            nc.sync.dma_start(raw[:], wb_hbm[:, :, PASS * g : PASS * (g + 1)])
-            wb_raw.append(raw)
+        wb_raw.append(at("wb_raw1", [P, 4, PASS], F32, 0))
+        nc.sync.dma_start(wb_raw[1][:], wb_hbm[:, :, PASS : 2 * PASS])
+        en = at("en", [P, 2, 2 * N], U8, 30 * KB)
+        nc.sync.dma_start(en[:].bitcast(I32), en_words.rearrange("a p c -> p a c").bitcast(I32))
 
-        tab2_sc = held("tab2_sc", [P, J], U8, tag="slot_g")
+        tab2_sc = at("tab2_sc", [P, J], U8, 16 * KB)
         nc.vector.tensor_copy(tab2_sc[:], tab2_sc_win[:].indirect(idx2[:]))
 
-        en_sc = held("en_sc", [P, 2, N], U8, tag="slot_e")
+        en_sc = at("en_sc", [P, 2, N], U8, 60 * KB)
         nc.vector.memset(en_sc[:].bitcast(I32), 0)
         for q in range(4):
             nc.sync.dma_start(
@@ -149,38 +157,43 @@ def tile_list_kg_max_bias_kernel(
                 en_scales[:, 4 * q : 4 * q + 4, :].rearrange("a r n -> r a n").bitcast(I32),
             )
 
-        tab2_g = []
-        for c in range(2):
-            words = held("tab2_g%d" % c, [P, HALF], U32)
+        def gather_tab2(c, words):
             nc.vector.tensor_copy(words[:], tab2_win[:].indirect(list_half(idx2, c)))
-            tab2_g.append(words)
-        en = at("en", [P, 2, 2 * N], U8, 0)
-        nc.sync.dma_start(en[:].bitcast(I32), en_words.rearrange("a p c -> p a c").bitcast(I32))
+            return words
 
-        def quantise_wb(g, copy, rounded):
-            words = held("wb%d" % g, [P, PASS], U32)
+        def round_wb(g, rounded):
+            nc.scalar.copy(rounded[:].rearrange("p (t m i) -> p m t i", t=4, i=4), wb_raw[g][:].rearrange("p i (m t) -> p m t i", t=4))
+            return rounded
+
+        def quantise_wb(g, rounded, words):
             scales = held("wb_sc%d" % g, [P, PASS], U8)
-            copy(rounded[:].rearrange("p (t m i) -> p m t i", t=4, i=4), wb_raw[g][:].rearrange("p i (m t) -> p m t i", t=4))
             nc.vector.quantize_mx(out=words[:].bitcast(FP8X4), scales=scales[:], in_=rounded[:])
             return words, scales
 
-        def project_a(c, g, u):
+        wbq = {0: quantise_wb(0, round_wb(0, held("wb_bf0", [P, 4 * PASS], BF16)), at("wb0", [P, PASS], U32, 62 * KB))}
+        tab2_g = [gather_tab2(0, at("tab2_g0", [P, HALF], U32, 17 * KB))]
+
+        def ha_pass(bank, a, c, g, u):
             words, scales = wa[g]
-            bank = acc_pool.tile([P, 4, UNIT], F32, name="acc")
-            for a in range(2):
-                for t in range(4):
-                    nc.tensor.matmul_mx(
-                        out=bank[:, t, :],
-                        lhsT=words[:, a, P * t : P * (t + 1)].bitcast(FP8X4),
-                        lhsT_scale=scales[:, a, P * t : P * (t + 1)],
-                        rhs=tab_g[c][:, a, 2 * UNIT * u : 2 * UNIT * (u + 1)].bitcast(FP4X4),
-                        rhs_scale=tab_sc[a][:, HALF * c + UNIT * u : HALF * c + UNIT * (u + 1)],
-                        start=(a == 0 and t == 0),
-                        stop=(a == 1 and t == 3),
-                    )
-            ha = held("ha%d%d%d" % (c, g, u), [P, 4 * UNIT], F32)
-            nc.scalar.copy(ha[:].rearrange("p (j t) -> p j t", t=4), bank[:].rearrange("p t j -> p j t"))
-            return ha
+            for t in range(4):
+                nc.tensor.matmul_mx(
+                    out=bank[:, t, :],
+                    lhsT=words[:, a, P * t : P * (t + 1)].bitcast(FP8X4),
+                    lhsT_scale=scales[:, a, P * t : P * (t + 1)],
+                    rhs=tab_g[c][:, a, 2 * UNIT * u : 2 * UNIT * (u + 1)].bitcast(FP4X4),
+                    rhs_scale=tab_sc[a][:, HALF * c + UNIT * u : HALF * c + UNIT * (u + 1)],
+                    start=(a == 0 and t == 0),
+                    stop=(a == 1 and t == 3),
+                )
+
+        def project_a(group):
+            banks = [acc_pool.tile([P, 4, UNIT], F32, name="acc") for unit in group]
+            for bank, unit in zip(banks, group):
+                ha_pass(bank, 0, *unit)
+            for bank, unit in zip(banks, group):
+                ha_pass(bank, 1, *unit)
+                ha[unit] = held("ha%d%d%d" % unit, [P, 4 * UNIT], F32)
+                nc.scalar.copy(ha[unit][:].rearrange("p (j t) -> p j t", t=4), bank[:].rearrange("p t j -> p j t"))
 
         def join(c, g, u, ha, wbq, rounded):
             words, scales = wbq
@@ -203,8 +216,14 @@ def tile_list_kg_max_bias_kernel(
             )
 
         units = [(c, g, u) for c in range(2) for g in range(2) for u in range(4)]
-        ha = {unit: project_a(*unit) for unit in units[:LEAD]}
-        wbq = {0: quantise_wb(0, nc.vector.tensor_copy, held("wb_bf0", [P, 4 * PASS], BF16))}
+        ha = {}
+        ha_order = [(c, g, u) for g in range(2) for c in range(2) for u in range(4)]
+        project_a(ha_order[:4])
+        for unit in ha_order[4:8]:
+            project_a([unit])
+        wb1_rounded = round_wb(1, held("wb_bf1", [P, 4 * PASS], BF16, tag="slot_a"))
+        for unit in ha_order[8:LEAD]:
+            project_a([unit])
         h = {}
         for c in range(2):
             for g in range(2):
@@ -212,7 +231,8 @@ def tile_list_kg_max_bias_kernel(
         waiting = []
         for n, (c, g, u) in enumerate(units):
             if (c, g, u) == (0, 1, 0):
-                wbq[1] = quantise_wb(1, nc.scalar.copy, at("wb_bf1", [P, 4 * PASS], BF16, 16 * 1024))
+                tab2_g.append(gather_tab2(1, held("tab2_g1", [P, HALF], U32, tag="ha003")))
+                wbq[1] = quantise_wb(1, wb1_rounded, held("wb1", [P, PASS], U32))
             s = u % 2
             if s == 0:
                 rounded = held("h_bf%d" % n, [P, 8 * UNIT], BF16)
@@ -224,26 +244,34 @@ def tile_list_kg_max_bias_kernel(
                 cols = slice(UNIT * (u - 1), UNIT * (u + 1))
                 waiting.append(dict(out=words[:, cols].bitcast(FP8X4), scales=scales[:, cols], in_=rounded[:]))
             if LEAD + n < len(units):
-                ha[units[LEAD + n]] = project_a(*units[LEAD + n])
+                project_a([ha_order[LEAD + n]])
         nc.vector.quantize_mx(**waiting.pop())
 
+        def y_pass(bank, c, g, nt):
+            words, scales = h[c, g]
+            nc.tensor.matmul_mx(
+                out=bank[:],
+                lhsT=en[:, g, 2 * P * nt : 2 * P * (nt + 1)].bitcast(FP4X4),
+                lhsT_scale=en_sc[:, g, P * nt : P * (nt + 1)],
+                rhs=words[:].bitcast(FP8X4),
+                rhs_scale=scales[:],
+                start=(g == 0),
+                stop=(g == 1),
+            )
+
         for c in range(2):
+            banks = {}
+            for nt in range(ACC_BANKS):
+                banks[nt] = acc_pool.tile([P, HALF], F32, name="acc")
+                y_pass(banks[nt], c, 0, nt)
             for nt in range(N // P):
-                bank = acc_pool.tile([P, HALF], F32, name="acc")
-                for g in range(2):
-                    words, scales = h[c, g]
-                    nc.tensor.matmul_mx(
-                        out=bank[:],
-                        lhsT=en[:, g, 2 * P * nt : 2 * P * (nt + 1)].bitcast(FP4X4),
-                        lhsT_scale=en_sc[:, g, P * nt : P * (nt + 1)],
-                        rhs=words[:].bitcast(FP8X4),
-                        rhs_scale=scales[:],
-                        start=(g == 0),
-                        stop=(g == 1),
-                    )
+                if nt not in banks:
+                    banks[nt] = acc_pool.tile([P, HALF], F32, name="acc")
+                    y_pass(banks[nt], c, 0, nt)
+                y_pass(banks[nt], c, 1, nt)
                 scores = stage.tile([P, HALF], F32, name="scores")
                 if c == 1 and nt % 2 == 1:
-                    nc.vector.tensor_scalar_add(scores[:], bank[:], bias[:, nt : nt + 1])
+                    nc.vector.tensor_scalar_add(scores[:], banks[nt][:], bias[:, nt : nt + 1])
                 else:
-                    nc.scalar.activation(scores[:], bank[:], IDENTITY, bias=bias[:, nt : nt + 1])
+                    nc.scalar.activation(scores[:], banks[nt][:], IDENTITY, bias=bias[:, nt : nt + 1])
                 nc.sync.dma_start(out[P * nt : P * (nt + 1), HALF * c : HALF * (c + 1)], scores[:])

@@ -20,9 +20,9 @@ P = 128
 PASS = 512
 HALF = 512
 UNIT = 128
-PARKED = 12
-TAB2_ROW = 8
-LEAD = 10
+PARKED = 16
+SPAN = 100
+LEAD = 8
 KB = 1024
 ACC_BANKS = 5
 
@@ -49,65 +49,61 @@ def tile_list_kg_max_bias_kernel(
         idx2 = lists.tile([P, J // 16], U16, name="idx2")
         nc.sync.dma_start(idx[:], offs)
         nc.sync.dma_start(idx2[:], offs2)
-
-        zeros = at("zeros", [P, 544], F32, 16 * KB - 64)
-        ident = held("ident", [P, P], F32)
-        nc.gpsimd.memset(zeros[:, 0:P], 0.0)
-        nc.gpsimd.affine_select(
-            out=ident[:], in_=zeros[:, 0:P], compare_op=mybir.AluOpType.not_equal, fill=1.0, base=0, pattern=[[-1, P]], channel_multiplier=1
-        )
-
-        tab_sc_win = at("tab_sc_win", [P, T], U8, 28 * KB)
-        nc.gpsimd.memset(tab_sc_win[:, 0 : T // 2].bitcast(I32), 0)
-        nc.vector.memset(tab_sc_win[:, T // 2 : T].bitcast(I32), 0)
-        nc.sync.dma_start(tab_sc_win[PARKED : PARKED + 16, :].bitcast(I32), tab_scales[1].bitcast(I32))
-        for q in range(4):
-            nc.sync.dma_start(tab_sc_win[32 * q : 32 * q + 4, :].bitcast(I32), tab_scales[0, 4 * q : 4 * q + 4, :].bitcast(I32))
-
-        tab2_sc_win = at("tab2_sc_win", [P, T], U8, 60 * KB)
-        wa_sc_raw = at("wa_sc_raw", [P, 2, R], U8, 16 * KB)
-        bias_rows = held("bias_rows", [P, P], F32)
-        nc.vector.memset(bias_rows[:], 0.0)
-        nc.vector.memset(tab2_sc_win[:].bitcast(I32), 0)
-        nc.vector.memset(wa_sc_raw[:].bitcast(I32), 0)
-
         tab_win = at("tab_win", [P, T], U32, 0)
         nc.sync.dma_start(tab_win[:].bitcast(I32), tab_words[0].rearrange("p t i -> p (t i)").bitcast(I32))
         wa_hbm = wa_words.rearrange("a p r i -> p a (r i)")
-        wa_raw = [at("wa_raw0", [P, 2, PASS], I32, 18 * KB)]
+        wa_raw = [at("wa_raw0", [P, 2, PASS], I32, 48 * KB)]
         nc.sync.dma_start(wa_raw[0][:], wa_hbm[:, :, 0 : 4 * PASS].bitcast(I32))
 
-        for q in range(4):
-            nc.sync.dma_start(
-                wa_sc_raw[32 * q : 32 * q + 4, :, :].bitcast(I32),
-                wa_scales[:, 4 * q : 4 * q + 4, :].rearrange("a r n -> r a n").bitcast(I32),
-            )
+        tab_sc_win = at("tab_sc_win", [P, T], U8, 58 * KB)
+        nc.gpsimd.memset(tab_sc_win[:, 0 : T // 2].bitcast(I32), 0)
+        nc.vector.memset(tab_sc_win[:, T // 2 : T].bitcast(I32), 0)
+        tab_sc_hbm = tab_scales.rearrange("a (q r) t -> r q a t", r=4)
+        for r in range(4):
+            nc.scalar.dma_start(tab_sc_win[r:P:PARKED, :].bitcast(I32), tab_sc_hbm[r].bitcast(I32))
 
-        bias = held("bias", [P, N // P], F32)
-        nc.gpsimd.dma_start(bias_rows[0 : N // P, :], b.rearrange("(c p) -> c p", p=P))
-        bias_ps = acc_pool.tile([P, PASS], F32, name="acc")
-        nc.tensor.transpose(bias_ps[:, 0:P], bias_rows[:], ident[:])
-        nc.scalar.copy(bias[:], bias_ps[:, 0 : N // P])
-
-        for q in range(4):
-            row = 32 * q + TAB2_ROW
-            nc.gpsimd.dma_start(tab2_sc_win[row : row + 4, :].bitcast(I32), tab2_scales[0, 4 * q : 4 * q + 4, :].bitcast(I32))
-
-        tab_sc0 = held("tab_sc0", [P, J], U8)
+        wa_sc_raw = held("wa_sc_raw", [P, 2, R], U8)
+        tab2_sc_win = at("tab2_sc_win", [P, T], U8, 66 * KB)
+        zeros = at("zeros", [P, P], F32, 24 * KB - 256)
+        bias_rows = held("bias_rows", [P, P], F32)
         tab_sc1 = held("tab_sc1", [P, J], U8)
+        en_sc = held("en_sc", [P, 2, N], U8)
+        nc.vector.memset(wa_sc_raw[:].bitcast(I32), 0)
+        nc.vector.memset(tab2_sc_win[:].bitcast(I32), 0)
+        nc.vector.memset(zeros[:], 0.0)
+        nc.vector.memset(bias_rows[:], 0.0)
         nc.vector.memset(tab_sc1[:].bitcast(I32), 0)
-        nc.vector.tensor_copy(tab_sc0[:], tab_sc_win[:].indirect(idx[:]))
-        for q in range(4):
-            nc.scalar.dma_start(
-                tab_sc1[32 * q : 32 * q + 4, :].bitcast(I32), tab_sc0[PARKED + 4 * q : PARKED + 4 * q + 4, :].bitcast(I32)
+        nc.vector.memset(en_sc[:].bitcast(I32), 0)
+
+        ident = held("ident", [P, P], F32)
+        nc.gpsimd.affine_select(
+            out=ident[:], in_=zeros[:], compare_op=mybir.AluOpType.not_equal, fill=1.0, base=0, pattern=[[-1, P]], channel_multiplier=1
+        )
+
+        def load_plane_rows(queue, plane, scales, q):
+            queue.dma_start(
+                plane[32 * q : 32 * q + 4, :, :].bitcast(I32),
+                scales[:, 4 * q : 4 * q + 4, :].rearrange("a r n -> r a n").bitcast(I32),
             )
-        tab_sc = [tab_sc0, tab_sc1]
+
+        for q in range(4):
+            load_plane_rows(nc.scalar if q < 2 else nc.gpsimd, wa_sc_raw, wa_scales, q)
+        for q in range(4):
+            nc.gpsimd.dma_start(tab2_sc_win[32 * q : 32 * q + 4, :].bitcast(I32), tab2_scales[0, 4 * q : 4 * q + 4, :].bitcast(I32))
+        nc.gpsimd.dma_start(bias_rows[0 : N // P, :], b.rearrange("(c p) -> c p", p=P))
+        for q in range(4):
+            load_plane_rows(nc.gpsimd, en_sc, en_scales, q)
 
         wb_hbm = wb.rearrange("(p i) r -> p i r", i=4)
-        wb_raw = [at("wb_raw0", [P, 4, PASS], F32, 22 * KB)]
+        wb_raw = [at("wb_raw0", [P, 4, PASS], F32, 16 * KB)]
         nc.sync.dma_start(wb_raw[0][:], wb_hbm[:, :, 0:PASS])
-        wa_raw.append(at("wa_raw1", [P, 2, PASS], I32, 30 * KB))
-        nc.sync.dma_start(wa_raw[1][:], wa_hbm[:, :, 4 * PASS : 8 * PASS].bitcast(I32))
+        tab2_win = at("tab2_win", [P, T], U32, 24 * KB)
+        nc.sync.dma_start(tab2_win[:].bitcast(I32), tab2_words[0].rearrange("p t i -> p (t i)").bitcast(I32))
+
+        tab_sc0 = held("tab_sc0", [P, J], U8)
+        nc.vector.tensor_copy(tab_sc0[:], tab_sc_win[:].indirect(idx[:]))
+        nc.scalar.dma_start(tab_sc1[0:SPAN, :].bitcast(I32), tab_sc0[PARKED : PARKED + SPAN, :].bitcast(I32))
+        tab_sc = [tab_sc0, tab_sc1]
 
         def list_half(offsets, c):
             return offsets[:, c * HALF // 16 : (c + 1) * HALF // 16]
@@ -118,8 +114,7 @@ def tile_list_kg_max_bias_kernel(
             nc.vector.tensor_copy(words[:].bitcast(U16), pairs[:].bitcast(U16).rearrange("p (j d) -> p d j", d=2))
             return words
 
-        def order_wa_scales(g):
-            scales = held("wa_sc%d" % g, [P, 2, PASS], U8)
+        def order_wa_scales(g, scales):
             nc.vector.tensor_copy(
                 scales[:].rearrange("p a (t m) -> p a t m", t=4),
                 wa_sc_raw[:, :, PASS * g : PASS * (g + 1)].rearrange("p a (m t) -> p a t m", t=4),
@@ -133,36 +128,12 @@ def tile_list_kg_max_bias_kernel(
             )
             return words
 
-        tab_g = [gather_tab(0, at("tab_pairs0", [P, HALF], U32, 34 * KB))]
-        tab2_win = at("tab2_win", [P, T], U32, 34 * KB)
-        nc.sync.dma_start(tab2_win[:].bitcast(I32), tab2_words[0].rearrange("p t i -> p (t i)").bitcast(I32))
-        wa = [(order_wa_words(0, held("wa0", [P, 2, PASS], I32, tag="slot_a")), order_wa_scales(0))]
-        scales1 = order_wa_scales(1)
-        tab_g.append(gather_tab(1, at("tab_pairs1", [P, HALF], U32, 16 * KB)))
-        wa.append((order_wa_words(1, held("wa1", [P, 2, PASS], I32)), scales1))
-
-        wb_raw.append(at("wb_raw1", [P, 4, PASS], F32, 0))
-        nc.sync.dma_start(wb_raw[1][:], wb_hbm[:, :, PASS : 2 * PASS])
-        en = at("en", [P, 2, 2 * N], U8, 30 * KB)
-        nc.sync.dma_start(en[:].bitcast(I32), en_words.rearrange("a p c -> p a c").bitcast(I32))
-
-        tab2_sc = at("tab2_sc", [P, J], U8, 16 * KB)
-        nc.vector.tensor_copy(tab2_sc[:], tab2_sc_win[:].indirect(idx2[:]))
-
-        en_sc = at("en_sc", [P, 2, N], U8, 60 * KB)
-        nc.vector.memset(en_sc[:].bitcast(I32), 0)
-        for q in range(4):
-            nc.sync.dma_start(
-                en_sc[32 * q : 32 * q + 4, :, :].bitcast(I32),
-                en_scales[:, 4 * q : 4 * q + 4, :].rearrange("a r n -> r a n").bitcast(I32),
-            )
-
         def gather_tab2(c, words):
             nc.vector.tensor_copy(words[:], tab2_win[:].indirect(list_half(idx2, c)))
             return words
 
-        def round_wb(g, rounded):
-            nc.scalar.copy(rounded[:].rearrange("p (t m i) -> p m t i", t=4, i=4), wb_raw[g][:].rearrange("p i (m t) -> p m t i", t=4))
+        def round_wb(copy, g, rounded):
+            copy(rounded[:].rearrange("p (t m i) -> p m t i", t=4, i=4), wb_raw[g][:].rearrange("p i (m t) -> p m t i", t=4))
             return rounded
 
         def quantise_wb(g, rounded, words):
@@ -170,8 +141,25 @@ def tile_list_kg_max_bias_kernel(
             nc.vector.quantize_mx(out=words[:].bitcast(FP8X4), scales=scales[:], in_=rounded[:])
             return words, scales
 
-        wbq = {0: quantise_wb(0, round_wb(0, held("wb_bf0", [P, 4 * PASS], BF16)), at("wb0", [P, PASS], U32, 62 * KB))}
-        tab2_g = [gather_tab2(0, at("tab2_g0", [P, HALF], U32, 17 * KB))]
+        tab_g = [gather_tab(0, at("tab_pairs0", [P, HALF], U32, 59 * KB))]
+        wa0_words = order_wa_words(0, at("wa0", [P, 2, PASS], I32, 54 * KB + 64))
+        wa = [(wa0_words, order_wa_scales(0, at("wa_sc0", [P, 2, PASS], U8, 61 * KB)))]
+        wa_raw.append(at("wa_raw1", [P, 2, PASS], I32, 50 * KB))
+        nc.sync.dma_start(wa_raw[1][:], wa_hbm[:, :, 4 * PASS : 8 * PASS].bitcast(I32))
+        tab_g.append(gather_tab(1, at("tab_pairs1", [P, HALF], U32, 48 * KB)))
+        wb_raw.append(at("wb_raw1", [P, 4, PASS], F32, 40 * KB + 64))
+        nc.sync.dma_start(wb_raw[1][:], wb_hbm[:, :, PASS : 2 * PASS])
+
+        tab2_sc = at("tab2_sc", [P, J], U8, 49 * KB)
+        nc.vector.tensor_copy(tab2_sc[:], tab2_sc_win[:].indirect(idx2[:]))
+        en = at("en", [P, 2, 2 * N], U8, 62 * KB + 64)
+        nc.sync.dma_start(en[:].bitcast(I32), en_words.rearrange("a p c -> p a c").bitcast(I32))
+
+        wb0_rounded = round_wb(nc.scalar.copy, 0, held("wb_bf0", [P, 4 * PASS], BF16))
+        wbq = {0: quantise_wb(0, wb0_rounded, at("wb0", [P, PASS], U32, 66 * KB + 64))}
+        tab2_g = [gather_tab2(0, at("tab2_g0", [P, HALF], U32, 70 * KB - 64))]
+        wa1_scales = order_wa_scales(1, at("wa_sc1", [P, 2, PASS], U8, 68 * KB + 512))
+        wa.append((order_wa_words(1, held("wa1", [P, 2, PASS], I32, tag="wb_bf0")), wa1_scales))
 
         def ha_pass(bank, a, c, g, u):
             words, scales = wa[g]
@@ -192,7 +180,10 @@ def tile_list_kg_max_bias_kernel(
                 ha_pass(bank, 0, *unit)
             for bank, unit in zip(banks, group):
                 ha_pass(bank, 1, *unit)
-                ha[unit] = held("ha%d%d%d" % unit, [P, 4 * UNIT], F32)
+                if unit == (0, 0, 1):
+                    ha[unit] = at("ha001", [P, 4 * UNIT], F32, 72 * KB)
+                else:
+                    ha[unit] = held("ha%d%d%d" % unit, [P, 4 * UNIT], F32)
                 nc.scalar.copy(ha[unit][:].rearrange("p (j t) -> p j t", t=4), bank[:].rearrange("p t j -> p j t"))
 
         def join(c, g, u, ha, wbq, rounded):
@@ -204,7 +195,7 @@ def tile_list_kg_max_bias_kernel(
                     lhsT=words[:, P * t : P * (t + 1)].bitcast(FP8X4),
                     lhsT_scale=scales[:, P * t : P * (t + 1)],
                     rhs=tab2_g[c][:, UNIT * u : UNIT * (u + 1)].bitcast(FP8X4),
-                    rhs_scale=tab2_sc[TAB2_ROW:P, HALF * c + UNIT * u : HALF * c + UNIT * (u + 1)],
+                    rhs_scale=tab2_sc[:, HALF * c + UNIT * u : HALF * c + UNIT * (u + 1)],
                     start=True,
                     stop=True,
                 )
@@ -219,10 +210,7 @@ def tile_list_kg_max_bias_kernel(
         ha = {}
         ha_order = [(c, g, u) for g in range(2) for c in range(2) for u in range(4)]
         project_a(ha_order[:4])
-        for unit in ha_order[4:8]:
-            project_a([unit])
-        wb1_rounded = round_wb(1, held("wb_bf1", [P, 4 * PASS], BF16, tag="slot_a"))
-        for unit in ha_order[8:LEAD]:
+        for unit in ha_order[4:LEAD]:
             project_a([unit])
         h = {}
         for c in range(2):
@@ -231,8 +219,11 @@ def tile_list_kg_max_bias_kernel(
         waiting = []
         for n, (c, g, u) in enumerate(units):
             if (c, g, u) == (0, 1, 0):
-                tab2_g.append(gather_tab2(1, held("tab2_g1", [P, HALF], U32, tag="ha003")))
+                wb1_rounded = round_wb(nc.vector.tensor_copy, 1, at("wb_bf1", [P, 4 * PASS], BF16, 73 * KB))
                 wbq[1] = quantise_wb(1, wb1_rounded, held("wb1", [P, PASS], U32))
+            if (c, g, u) == (1, 0, 0):
+                nc.vector.quantize_mx(**waiting.pop())
+                tab2_g.append(gather_tab2(1, held("tab2_g1", [P, HALF], U32, tag="ha013")))
             s = u % 2
             if s == 0:
                 rounded = held("h_bf%d" % n, [P, 8 * UNIT], BF16)
@@ -246,6 +237,11 @@ def tile_list_kg_max_bias_kernel(
             if LEAD + n < len(units):
                 project_a([ha_order[LEAD + n]])
         nc.vector.quantize_mx(**waiting.pop())
+
+        bias = held("bias", [P, N // P], F32)
+        bias_ps = acc_pool.tile([P, PASS], F32, name="acc")
+        nc.tensor.transpose(bias_ps[:, 0:P], bias_rows[:], ident[:])
+        nc.scalar.copy(bias[:], bias_ps[:, 0 : N // P])
 
         def y_pass(bank, c, g, nt):
             words, scales = h[c, g]

@@ -22,7 +22,6 @@ HALF = 512
 UNIT = 128
 PARKED = 16
 SPAN = 100
-LEAD = 8
 KB = 1024
 ACC_BANKS = 5
 
@@ -49,61 +48,59 @@ def tile_list_kg_max_bias_kernel(
         idx2 = lists.tile([P, J // 16], U16, name="idx2")
         nc.sync.dma_start(idx[:], offs)
         nc.sync.dma_start(idx2[:], offs2)
+
+        tab_sc_win = at("tab_sc_win", [P, T], U8, 36 * KB)
+        tab_sc1 = held("tab_sc1", [P, J], U8)
+        zeros = at("zeros", [P, 1568], F32, 16 * KB - 64)
+        nc.vector.memset(tab_sc_win[:].bitcast(I32), 0)
+        nc.vector.memset(zeros[:, 0:P], 0.0)
+        tab_sc_hbm = tab_scales.rearrange("a (q r) t -> r q a t", r=4)
+        for r in range(4):
+            nc.sync.dma_start(tab_sc_win[r:P:PARKED, :].bitcast(I32), tab_sc_hbm[r].bitcast(I32))
+
+        ident = held("ident", [P, P], F32)
+        nc.vector.tensor_copy(ident[:], zeros[:, 0:P])
+        nc.gpsimd.affine_select(
+            out=ident[:], in_=ident[:], compare_op=mybir.AluOpType.not_equal, fill=1.0, base=0, pattern=[[-1, P]], channel_multiplier=1
+        )
+
         tab_win = at("tab_win", [P, T], U32, 0)
         nc.sync.dma_start(tab_win[:].bitcast(I32), tab_words[0].rearrange("p t i -> p (t i)").bitcast(I32))
         wa_hbm = wa_words.rearrange("a p r i -> p a (r i)")
-        wa_raw = [at("wa_raw0", [P, 2, PASS], I32, 48 * KB)]
+        wa_raw = [at("wa_raw0", [P, 2, PASS], I32, 22 * KB)]
         nc.sync.dma_start(wa_raw[0][:], wa_hbm[:, :, 0 : 4 * PASS].bitcast(I32))
 
-        tab_sc_win = at("tab_sc_win", [P, T], U8, 58 * KB)
-        nc.gpsimd.memset(tab_sc_win[:, 0 : T // 2].bitcast(I32), 0)
-        nc.vector.memset(tab_sc_win[:, T // 2 : T].bitcast(I32), 0)
-        tab_sc_hbm = tab_scales.rearrange("a (q r) t -> r q a t", r=4)
-        for r in range(4):
-            nc.scalar.dma_start(tab_sc_win[r:P:PARKED, :].bitcast(I32), tab_sc_hbm[r].bitcast(I32))
-
-        wa_sc_raw = held("wa_sc_raw", [P, 2, R], U8)
-        tab2_sc_win = at("tab2_sc_win", [P, T], U8, 66 * KB)
-        zeros = at("zeros", [P, P], F32, 24 * KB - 256)
-        bias_rows = held("bias_rows", [P, P], F32)
-        tab_sc1 = held("tab_sc1", [P, J], U8)
-        en_sc = held("en_sc", [P, 2, N], U8)
+        wa_sc_raw = at("wa_sc_raw", [P, 2, R], U8, 20 * KB)
+        tab2_sc_win = at("tab2_sc_win", [P, T], U8, 16 * KB)
         nc.vector.memset(wa_sc_raw[:].bitcast(I32), 0)
         nc.vector.memset(tab2_sc_win[:].bitcast(I32), 0)
-        nc.vector.memset(zeros[:], 0.0)
-        nc.vector.memset(bias_rows[:], 0.0)
         nc.vector.memset(tab_sc1[:].bitcast(I32), 0)
-        nc.vector.memset(en_sc[:].bitcast(I32), 0)
 
-        ident = held("ident", [P, P], F32)
-        nc.gpsimd.affine_select(
-            out=ident[:], in_=zeros[:], compare_op=mybir.AluOpType.not_equal, fill=1.0, base=0, pattern=[[-1, P]], channel_multiplier=1
-        )
+        def load_plane_rows(plane, scales):
+            for q in range(4):
+                nc.sync.dma_start(
+                    plane[32 * q : 32 * q + 4, :, :].bitcast(I32),
+                    scales[:, 4 * q : 4 * q + 4, :].rearrange("a r n -> r a n").bitcast(I32),
+                )
 
-        def load_plane_rows(queue, plane, scales, q):
-            queue.dma_start(
-                plane[32 * q : 32 * q + 4, :, :].bitcast(I32),
-                scales[:, 4 * q : 4 * q + 4, :].rearrange("a r n -> r a n").bitcast(I32),
-            )
-
+        load_plane_rows(wa_sc_raw, wa_scales)
         for q in range(4):
-            load_plane_rows(nc.scalar if q < 2 else nc.gpsimd, wa_sc_raw, wa_scales, q)
-        for q in range(4):
-            nc.gpsimd.dma_start(tab2_sc_win[32 * q : 32 * q + 4, :].bitcast(I32), tab2_scales[0, 4 * q : 4 * q + 4, :].bitcast(I32))
-        nc.gpsimd.dma_start(bias_rows[0 : N // P, :], b.rearrange("(c p) -> c p", p=P))
-        for q in range(4):
-            load_plane_rows(nc.gpsimd, en_sc, en_scales, q)
-
-        wb_hbm = wb.rearrange("(p i) r -> p i r", i=4)
-        wb_raw = [at("wb_raw0", [P, 4, PASS], F32, 16 * KB)]
-        nc.sync.dma_start(wb_raw[0][:], wb_hbm[:, :, 0:PASS])
-        tab2_win = at("tab2_win", [P, T], U32, 24 * KB)
-        nc.sync.dma_start(tab2_win[:].bitcast(I32), tab2_words[0].rearrange("p t i -> p (t i)").bitcast(I32))
+            queue = nc.sync if q == 0 else nc.gpsimd
+            queue.dma_start(tab2_sc_win[32 * q : 32 * q + 4, :].bitcast(I32), tab2_scales[0, 4 * q : 4 * q + 4, :].bitcast(I32))
 
         tab_sc0 = held("tab_sc0", [P, J], U8)
         nc.vector.tensor_copy(tab_sc0[:], tab_sc_win[:].indirect(idx[:]))
         nc.scalar.dma_start(tab_sc1[0:SPAN, :].bitcast(I32), tab_sc0[PARKED : PARKED + SPAN, :].bitcast(I32))
         tab_sc = [tab_sc0, tab_sc1]
+
+        wb_hbm = wb.rearrange("(p i) r -> p i r", i=4)
+        wb_raw = [at("wb_raw0", [P, 4, PASS], F32, 28 * KB + 64)]
+        nc.sync.dma_start(wb_raw[0][:], wb_hbm[:, :, 0:PASS])
+        tab2_win = at("tab2_win", [P, T], U32, 40 * KB - 64)
+        nc.sync.dma_start(tab2_win[:].bitcast(I32), tab2_words[0].rearrange("p t i -> p (t i)").bitcast(I32))
+        bias_rows = at("bias_rows", [P, P], F32, 39 * KB)
+        nc.vector.memset(bias_rows[:], 0.0)
+        nc.gpsimd.dma_start(bias_rows[0 : N // P, :], b.rearrange("(c p) -> c p", p=P))
 
         def list_half(offsets, c):
             return offsets[:, c * HALF // 16 : (c + 1) * HALF // 16]
@@ -113,13 +110,6 @@ def tile_list_kg_max_bias_kernel(
             nc.vector.tensor_copy(pairs[:], tab_win[:].indirect(list_half(idx, c)))
             nc.vector.tensor_copy(words[:].bitcast(U16), pairs[:].bitcast(U16).rearrange("p (j d) -> p d j", d=2))
             return words
-
-        def order_wa_scales(g, scales):
-            nc.vector.tensor_copy(
-                scales[:].rearrange("p a (t m) -> p a t m", t=4),
-                wa_sc_raw[:, :, PASS * g : PASS * (g + 1)].rearrange("p a (m t) -> p a t m", t=4),
-            )
-            return scales
 
         def order_wa_words(g, words):
             nc.vector.tensor_copy(
@@ -141,33 +131,39 @@ def tile_list_kg_max_bias_kernel(
             nc.vector.quantize_mx(out=words[:].bitcast(FP8X4), scales=scales[:], in_=rounded[:])
             return words, scales
 
-        tab_g = [gather_tab(0, at("tab_pairs0", [P, HALF], U32, 59 * KB))]
-        wa0_words = order_wa_words(0, at("wa0", [P, 2, PASS], I32, 54 * KB + 64))
-        wa = [(wa0_words, order_wa_scales(0, at("wa_sc0", [P, 2, PASS], U8, 61 * KB)))]
-        wa_raw.append(at("wa_raw1", [P, 2, PASS], I32, 50 * KB))
+        tab_g = [gather_tab(0, at("tab_pairs0", [P, HALF], U32, 62 * KB))]
+        wa = [order_wa_words(0, at("wa0", [P, 2, PASS], I32, 63 * KB))]
+        wa_sc = at("wa_sc", [P, 2, R], U8, 61 * KB)
+        nc.vector.tensor_copy(
+            wa_sc[:].rearrange("p a r -> p (a r)").rearrange("p (s t m) -> p s t m", t=4, m=P),
+            wa_sc_raw[:].rearrange("p a r -> p (a r)").rearrange("p (s m t) -> p s t m", t=4, m=P),
+        )
+        wa_raw.append(at("wa_raw1", [P, 2, PASS], I32, 24 * KB))
         nc.sync.dma_start(wa_raw[1][:], wa_hbm[:, :, 4 * PASS : 8 * PASS].bitcast(I32))
-        tab_g.append(gather_tab(1, at("tab_pairs1", [P, HALF], U32, 48 * KB)))
-        wb_raw.append(at("wb_raw1", [P, 4, PASS], F32, 40 * KB + 64))
+        tab_g.append(gather_tab(1, at("tab_pairs1", [P, HALF], U32, 21 * KB)))
+        wb_raw.append(at("wb_raw1", [P, 4, PASS], F32, 0))
         nc.sync.dma_start(wb_raw[1][:], wb_hbm[:, :, PASS : 2 * PASS])
-
-        tab2_sc = at("tab2_sc", [P, J], U8, 49 * KB)
-        nc.vector.tensor_copy(tab2_sc[:], tab2_sc_win[:].indirect(idx2[:]))
-        en = at("en", [P, 2, 2 * N], U8, 62 * KB + 64)
+        en = at("en", [P, 2, 2 * N], U8, 8 * KB)
         nc.sync.dma_start(en[:].bitcast(I32), en_words.rearrange("a p c -> p a c").bitcast(I32))
 
+        tab2_sc = at("tab2_sc", [P, J], U8, 22 * KB)
+        nc.vector.tensor_copy(tab2_sc[:], tab2_sc_win[:].indirect(idx2[:]))
+
         wb0_rounded = round_wb(nc.scalar.copy, 0, held("wb_bf0", [P, 4 * PASS], BF16))
-        wbq = {0: quantise_wb(0, wb0_rounded, at("wb0", [P, PASS], U32, 66 * KB + 64))}
-        tab2_g = [gather_tab2(0, at("tab2_g0", [P, HALF], U32, 70 * KB - 64))]
-        wa1_scales = order_wa_scales(1, at("wa_sc1", [P, 2, PASS], U8, 68 * KB + 512))
-        wa.append((order_wa_words(1, held("wa1", [P, 2, PASS], I32, tag="wb_bf0")), wa1_scales))
+        wbq = {0: quantise_wb(0, wb0_rounded, at("wb0", [P, PASS], U32, 16 * KB))}
+        tab2_g = [gather_tab2(0, at("tab2_g0", [P, HALF], U32, 18 * KB))]
+        wa.append(order_wa_words(1, held("wa1", [P, 2, PASS], I32, tag="wb_bf0")))
+
+        en_sc = at("en_sc", [P, 2, N], U8, 20 * KB)
+        nc.vector.memset(en_sc[:].bitcast(I32), 0)
+        load_plane_rows(en_sc, en_scales)
 
         def ha_pass(bank, a, c, g, u):
-            words, scales = wa[g]
             for t in range(4):
                 nc.tensor.matmul_mx(
                     out=bank[:, t, :],
-                    lhsT=words[:, a, P * t : P * (t + 1)].bitcast(FP8X4),
-                    lhsT_scale=scales[:, a, P * t : P * (t + 1)],
+                    lhsT=wa[g][:, a, P * t : P * (t + 1)].bitcast(FP8X4),
+                    lhsT_scale=wa_sc[:, a, PASS * g + P * t : PASS * g + P * (t + 1)],
                     rhs=tab_g[c][:, a, 2 * UNIT * u : 2 * UNIT * (u + 1)].bitcast(FP4X4),
                     rhs_scale=tab_sc[a][:, HALF * c + UNIT * u : HALF * c + UNIT * (u + 1)],
                     start=(a == 0 and t == 0),
@@ -180,8 +176,8 @@ def tile_list_kg_max_bias_kernel(
                 ha_pass(bank, 0, *unit)
             for bank, unit in zip(banks, group):
                 ha_pass(bank, 1, *unit)
-                if unit == (0, 0, 1):
-                    ha[unit] = at("ha001", [P, 4 * UNIT], F32, 72 * KB)
+                if unit[:2] == (0, 0):
+                    ha[unit] = at("ha%d%d%d" % unit, [P, 4 * UNIT], F32, (28 + 2 * unit[2]) * KB + 64)
                 else:
                     ha[unit] = held("ha%d%d%d" % unit, [P, 4 * UNIT], F32)
                 nc.scalar.copy(ha[unit][:].rearrange("p (j t) -> p j t", t=4), bank[:].rearrange("p t j -> p j t"))
@@ -208,10 +204,9 @@ def tile_list_kg_max_bias_kernel(
 
         units = [(c, g, u) for c in range(2) for g in range(2) for u in range(4)]
         ha = {}
-        ha_order = [(c, g, u) for g in range(2) for c in range(2) for u in range(4)]
-        project_a(ha_order[:4])
-        for unit in ha_order[4:LEAD]:
-            project_a([unit])
+        project_a([(0, 0, u) for u in range(4)])
+        for u in range(4):
+            project_a([(1, 0, u)])
         h = {}
         for c in range(2):
             for g in range(2):
@@ -219,7 +214,7 @@ def tile_list_kg_max_bias_kernel(
         waiting = []
         for n, (c, g, u) in enumerate(units):
             if (c, g, u) == (0, 1, 0):
-                wb1_rounded = round_wb(nc.vector.tensor_copy, 1, at("wb_bf1", [P, 4 * PASS], BF16, 73 * KB))
+                wb1_rounded = round_wb(nc.vector.tensor_copy, 1, at("wb_bf1", [P, 4 * PASS], BF16, 35 * KB))
                 wbq[1] = quantise_wb(1, wb1_rounded, held("wb1", [P, PASS], U32))
             if (c, g, u) == (1, 0, 0):
                 nc.vector.quantize_mx(**waiting.pop())
@@ -234,8 +229,9 @@ def tile_list_kg_max_bias_kernel(
                 words, scales = h[c, g]
                 cols = slice(UNIT * (u - 1), UNIT * (u + 1))
                 waiting.append(dict(out=words[:, cols].bitcast(FP8X4), scales=scales[:, cols], in_=rounded[:]))
-            if LEAD + n < len(units):
-                project_a([ha_order[LEAD + n]])
+            if c == 0 and u == 3:
+                for later in range(4):
+                    project_a([(g, 1, later)])
         nc.vector.quantize_mx(**waiting.pop())
 
         bias = held("bias", [P, N // P], F32)

@@ -1,6 +1,7 @@
 from contextlib import ExitStack
 
 import concourse.mybir as mybir
+from concourse.masks import make_identity
 
 K, L, R, N, T, J = 1024, 512, 1024, 1024, 4096, 1024
 FLOPS = 2 * J * (K * R + L * R + R * N)
@@ -20,8 +21,6 @@ P = 128
 PASS = 512
 HALF = 512
 UNIT = 128
-PARKED = 16
-SPAN = 100
 KB = 1024
 ACC_BANKS = 5
 
@@ -34,7 +33,7 @@ def tile_list_kg_max_bias_kernel(
         lists = ctx.enter_context(tc.tile_pool(name="lists", bufs=1))
         keep = ctx.enter_context(tc.tile_pool(name="keep", bufs=1))
         placed = ctx.enter_context(tc.tile_pool(name="placed", bufs=1))
-        stage = ctx.enter_context(tc.tile_pool(name="stage", bufs=6))
+        stage = ctx.enter_context(tc.tile_pool(name="stage", bufs=8))
         acc_pool = ctx.enter_context(tc.psum_pool(name="acc", bufs=ACC_BANKS))
         hb_pool = ctx.enter_context(tc.psum_pool(name="hb", bufs=3))
 
@@ -46,61 +45,69 @@ def tile_list_kg_max_bias_kernel(
 
         idx = lists.tile([P, J // 16], U16, name="idx")
         idx2 = lists.tile([P, J // 16], U16, name="idx2")
+        tab_sc_win = at("tab_sc_win", [P, T], U8, 0)
+        wa_sc_raw = at("wa_sc_raw", [P, R], U8, 32 * KB - 512)
+        tab2_sc_win = at("tab2_sc_win", [P, T], U8, 46 * KB)
         nc.sync.dma_start(idx[:], offs)
+        nc.sync.dma_start(tab_sc_win[96:P, :].bitcast(I32), tab_scales.rearrange("a q t -> q a t").bitcast(I32))
+        nc.sync.dma_start(wa_sc_raw[96:P, :].bitcast(I32), wa_scales.rearrange("a q r -> q a r").bitcast(I32))
         nc.sync.dma_start(idx2[:], offs2)
+        nc.sync.dma_start(tab2_sc_win[112:P, :].bitcast(I32), tab2_scales[0].bitcast(I32))
+        nc.vector.memset(tab_sc_win[0:96, :].bitcast(I32), 0)
+        nc.vector.memset(wa_sc_raw[0:96, :].bitcast(I32), 0)
+        nc.vector.memset(tab2_sc_win[0:112, :].bitcast(I32), 0)
+        tab_sc = held("tab_sc", [P, 2, J], U8)
+        wa_sc = held("wa_sc", [P, 2, R], U8)
+        tab2_sc = held("tab2_sc", [P, J], U8)
+        nc.vector.memset(tab_sc[:].bitcast(I32), 0)
+        nc.gpsimd.memset(wa_sc[:].bitcast(I32), 0)
+        nc.gpsimd.memset(tab2_sc[:].bitcast(I32), 0)
 
-        tab_sc_win = at("tab_sc_win", [P, T], U8, 36 * KB)
-        tab_sc1 = held("tab_sc1", [P, J], U8)
-        zeros = at("zeros", [P, 1568], F32, 16 * KB - 64)
-        nc.vector.memset(tab_sc_win[:].bitcast(I32), 0)
-        nc.vector.memset(zeros[:, 0:P], 0.0)
-        tab_sc_hbm = tab_scales.rearrange("a (q r) t -> r q a t", r=4)
-        for r in range(4):
-            nc.sync.dma_start(tab_sc_win[r:P:PARKED, :].bitcast(I32), tab_sc_hbm[r].bitcast(I32))
-
-        ident = held("ident", [P, P], F32)
-        nc.vector.tensor_copy(ident[:], zeros[:, 0:P])
-        nc.gpsimd.affine_select(
-            out=ident[:], in_=ident[:], compare_op=mybir.AluOpType.not_equal, fill=1.0, base=0, pattern=[[-1, P]], channel_multiplier=1
-        )
-
-        tab_win = at("tab_win", [P, T], U32, 0)
+        tab_win = at("tab_win", [P, T], U32, 4 * KB)
         nc.sync.dma_start(tab_win[:].bitcast(I32), tab_words[0].rearrange("p t i -> p (t i)").bitcast(I32))
         wa_hbm = wa_words.rearrange("a p r i -> p a (r i)")
-        wa_raw = [at("wa_raw0", [P, 2, PASS], I32, 22 * KB)]
+        wa_raw = [at("wa_raw0", [P, 2, PASS], I32, 20 * KB)]
         nc.sync.dma_start(wa_raw[0][:], wa_hbm[:, :, 0 : 4 * PASS].bitcast(I32))
 
-        wa_sc_raw = at("wa_sc_raw", [P, 2, R], U8, 20 * KB)
-        tab2_sc_win = at("tab2_sc_win", [P, T], U8, 16 * KB)
-        nc.vector.memset(wa_sc_raw[:].bitcast(I32), 0)
-        nc.vector.memset(tab2_sc_win[:].bitcast(I32), 0)
-        nc.vector.memset(tab_sc1[:].bitcast(I32), 0)
+        bias_rows = held("bias_rows", [P, P], F32)
+        nc.gpsimd.dma_start(bias_rows[P - N // P : P, :], b.rearrange("(c p) -> c p", p=P))
+        nc.gpsimd.memset(bias_rows[0 : P - N // P, :], 0.0)
+        ident = held("ident", [P, P], F32)
+        make_identity(nc, ident[:])
 
-        def load_plane_rows(plane, scales):
+        bias = held("bias", [P, N // P], F32)
+        bias_ps = acc_pool.tile([P, PASS], F32, name="acc")
+        nc.tensor.transpose(bias_ps[:, 0:P], bias_rows[:], ident[:])
+        nc.scalar.copy(bias[:], bias_ps[:, P - N // P : P])
+
+        def deal_rows(plane, rows, first, count):
             for q in range(4):
-                nc.sync.dma_start(
-                    plane[32 * q : 32 * q + 4, :, :].bitcast(I32),
-                    scales[:, 4 * q : 4 * q + 4, :].rearrange("a r n -> r a n").bitcast(I32),
+                nc.scalar.dma_start(
+                    plane[32 * q : 32 * q + 4].bitcast(I32), rows[first + count * q : first + count * (q + 1), :].bitcast(I32)
                 )
 
-        load_plane_rows(wa_sc_raw, wa_scales)
-        for q in range(4):
-            queue = nc.sync if q == 0 else nc.gpsimd
-            queue.dma_start(tab2_sc_win[32 * q : 32 * q + 4, :].bitcast(I32), tab2_scales[0, 4 * q : 4 * q + 4, :].bitcast(I32))
-
-        tab_sc0 = held("tab_sc0", [P, J], U8)
-        nc.vector.tensor_copy(tab_sc0[:], tab_sc_win[:].indirect(idx[:]))
-        nc.scalar.dma_start(tab_sc1[0:SPAN, :].bitcast(I32), tab_sc0[PARKED : PARKED + SPAN, :].bitcast(I32))
-        tab_sc = [tab_sc0, tab_sc1]
+        tab_sc_g = held("tab_sc_g", [P, J], U8)
+        nc.vector.tensor_copy(tab_sc_g[:], tab_sc_win[:].indirect(idx[:]))
+        deal_rows(tab_sc, tab_sc_g, 96, 8)
+        wa_sc_ord = held("wa_sc_ord", [P, R], U8)
+        nc.vector.tensor_copy(
+            wa_sc_ord[:].rearrange("p (g t m) -> p g t m", t=4, m=P), wa_sc_raw[:].rearrange("p (g m t) -> p g t m", t=4, m=P)
+        )
+        deal_rows(wa_sc, wa_sc_ord, 96, 8)
 
         wb_hbm = wb.rearrange("(p i) r -> p i r", i=4)
-        wb_raw = [at("wb_raw0", [P, 4, PASS], F32, 28 * KB + 64)]
+        wb_raw = [at("wb_raw0", [P, 4, PASS], F32, 24 * KB)]
         nc.sync.dma_start(wb_raw[0][:], wb_hbm[:, :, 0:PASS])
-        tab2_win = at("tab2_win", [P, T], U32, 40 * KB - 64)
+        wa_raw.append(at("wa_raw1", [P, 2, PASS], I32, 32 * KB))
+        nc.sync.dma_start(wa_raw[1][:], wa_hbm[:, :, 4 * PASS : 8 * PASS].bitcast(I32))
+
+        tab2_sc_g = held("tab2_sc_g", [P, J], U8)
+        nc.vector.tensor_copy(tab2_sc_g[:], tab2_sc_win[:].indirect(idx2[:]))
+        deal_rows(tab2_sc, tab2_sc_g, 112, 4)
+        wb_raw.append(at("wb_raw1", [P, 4, PASS], F32, 40 * KB))
+        nc.sync.dma_start(wb_raw[1][:], wb_hbm[:, :, PASS : 2 * PASS])
+        tab2_win = at("tab2_win", [P, T], U32, 48 * KB)
         nc.sync.dma_start(tab2_win[:].bitcast(I32), tab2_words[0].rearrange("p t i -> p (t i)").bitcast(I32))
-        bias_rows = at("bias_rows", [P, P], F32, 39 * KB)
-        nc.vector.memset(bias_rows[:], 0.0)
-        nc.gpsimd.dma_start(bias_rows[0 : N // P, :], b.rearrange("(c p) -> c p", p=P))
 
         def list_half(offsets, c):
             return offsets[:, c * HALF // 16 : (c + 1) * HALF // 16]
@@ -131,32 +138,26 @@ def tile_list_kg_max_bias_kernel(
             nc.vector.quantize_mx(out=words[:].bitcast(FP8X4), scales=scales[:], in_=rounded[:])
             return words, scales
 
-        tab_g = [gather_tab(0, at("tab_pairs0", [P, HALF], U32, 62 * KB))]
-        wa = [order_wa_words(0, at("wa0", [P, 2, PASS], I32, 63 * KB))]
-        wa_sc = at("wa_sc", [P, 2, R], U8, 61 * KB)
-        nc.vector.tensor_copy(
-            wa_sc[:].rearrange("p a r -> p (a r)").rearrange("p (s t m) -> p s t m", t=4, m=P),
-            wa_sc_raw[:].rearrange("p a r -> p (a r)").rearrange("p (s m t) -> p s t m", t=4, m=P),
-        )
-        wa_raw.append(at("wa_raw1", [P, 2, PASS], I32, 24 * KB))
-        nc.sync.dma_start(wa_raw[1][:], wa_hbm[:, :, 4 * PASS : 8 * PASS].bitcast(I32))
-        tab_g.append(gather_tab(1, at("tab_pairs1", [P, HALF], U32, 21 * KB)))
-        wb_raw.append(at("wb_raw1", [P, 4, PASS], F32, 0))
-        nc.sync.dma_start(wb_raw[1][:], wb_hbm[:, :, PASS : 2 * PASS])
-        en = at("en", [P, 2, 2 * N], U8, 8 * KB)
+        tab_g = [gather_tab(0, held("tab_pairs0", [P, HALF], U32))]
+        wa = [order_wa_words(0, held("wa0", [P, 2, PASS], I32))]
+        tab_g.append(gather_tab(1, at("tab_pairs1", [P, HALF], U32, 20 * KB)))
+
+        en = at("en", [P, 2, 2 * N], U8, 4 * KB)
         nc.sync.dma_start(en[:].bitcast(I32), en_words.rearrange("a p c -> p a c").bitcast(I32))
-
-        tab2_sc = at("tab2_sc", [P, J], U8, 22 * KB)
-        nc.vector.tensor_copy(tab2_sc[:], tab2_sc_win[:].indirect(idx2[:]))
-
-        wb0_rounded = round_wb(nc.scalar.copy, 0, held("wb_bf0", [P, 4 * PASS], BF16))
-        wbq = {0: quantise_wb(0, wb0_rounded, at("wb0", [P, PASS], U32, 16 * KB))}
-        tab2_g = [gather_tab2(0, at("tab2_g0", [P, HALF], U32, 18 * KB))]
-        wa.append(order_wa_words(1, held("wa1", [P, 2, PASS], I32, tag="wb_bf0")))
-
-        en_sc = at("en_sc", [P, 2, N], U8, 20 * KB)
+        en_sc = at("en_sc", [P, 2, N], U8, 8 * KB)
         nc.vector.memset(en_sc[:].bitcast(I32), 0)
-        load_plane_rows(en_sc, en_scales)
+        for q in range(4):
+            nc.sync.dma_start(
+                en_sc[32 * q : 32 * q + 4, :, :].bitcast(I32),
+                en_scales[:, 4 * q : 4 * q + 4, :].rearrange("a r n -> r a n").bitcast(I32),
+            )
+
+        wb0_rounded = round_wb(nc.vector.tensor_copy, 0, held("wb_bf0", [P, 4 * PASS], BF16))
+        wa.append(order_wa_words(1, held("wa1", [P, 2, PASS], I32)))
+        wbq = {0: quantise_wb(0, wb0_rounded, held("wb0", [P, PASS], U32))}
+        wb1_rounded = round_wb(nc.vector.tensor_copy, 1, held("wb_bf1", [P, 4 * PASS], BF16))
+        wbq[1] = quantise_wb(1, wb1_rounded, held("wb1", [P, PASS], U32))
+        tab2_g = [gather_tab2(c, held("tab2_g%d" % c, [P, HALF], U32)) for c in range(2)]
 
         def ha_pass(bank, a, c, g, u):
             for t in range(4):
@@ -165,7 +166,7 @@ def tile_list_kg_max_bias_kernel(
                     lhsT=wa[g][:, a, P * t : P * (t + 1)].bitcast(FP8X4),
                     lhsT_scale=wa_sc[:, a, PASS * g + P * t : PASS * g + P * (t + 1)],
                     rhs=tab_g[c][:, a, 2 * UNIT * u : 2 * UNIT * (u + 1)].bitcast(FP4X4),
-                    rhs_scale=tab_sc[a][:, HALF * c + UNIT * u : HALF * c + UNIT * (u + 1)],
+                    rhs_scale=tab_sc[:, a, HALF * c + UNIT * u : HALF * c + UNIT * (u + 1)],
                     start=(a == 0 and t == 0),
                     stop=(a == 1 and t == 3),
                 )
@@ -176,10 +177,7 @@ def tile_list_kg_max_bias_kernel(
                 ha_pass(bank, 0, *unit)
             for bank, unit in zip(banks, group):
                 ha_pass(bank, 1, *unit)
-                if unit[:2] == (0, 0):
-                    ha[unit] = at("ha%d%d%d" % unit, [P, 4 * UNIT], F32, (28 + 2 * unit[2]) * KB + 64)
-                else:
-                    ha[unit] = held("ha%d%d%d" % unit, [P, 4 * UNIT], F32)
+                ha[unit] = held("ha%d%d%d" % unit, [P, 4 * UNIT], F32)
                 nc.scalar.copy(ha[unit][:].rearrange("p (j t) -> p j t", t=4), bank[:].rearrange("p t j -> p j t"))
 
         def join(c, g, u, ha, wbq, rounded):
@@ -204,21 +202,15 @@ def tile_list_kg_max_bias_kernel(
 
         units = [(c, g, u) for c in range(2) for g in range(2) for u in range(4)]
         ha = {}
-        project_a([(0, 0, u) for u in range(4)])
-        for u in range(4):
-            project_a([(1, 0, u)])
+        for c, g in ((0, 0), (1, 0), (0, 1)):
+            for u in range(4):
+                project_a([(c, g, u)])
         h = {}
         for c in range(2):
             for g in range(2):
                 h[c, g] = (held("h%d%d" % (c, g), [P, HALF], U32), held("h_sc%d%d" % (c, g), [P, HALF], U8))
         waiting = []
         for n, (c, g, u) in enumerate(units):
-            if (c, g, u) == (0, 1, 0):
-                wb1_rounded = round_wb(nc.vector.tensor_copy, 1, at("wb_bf1", [P, 4 * PASS], BF16, 35 * KB))
-                wbq[1] = quantise_wb(1, wb1_rounded, held("wb1", [P, PASS], U32))
-            if (c, g, u) == (1, 0, 0):
-                nc.vector.quantize_mx(**waiting.pop())
-                tab2_g.append(gather_tab2(1, held("tab2_g1", [P, HALF], U32, tag="ha013")))
             s = u % 2
             if s == 0:
                 rounded = held("h_bf%d" % n, [P, 8 * UNIT], BF16)
@@ -229,15 +221,10 @@ def tile_list_kg_max_bias_kernel(
                 words, scales = h[c, g]
                 cols = slice(UNIT * (u - 1), UNIT * (u + 1))
                 waiting.append(dict(out=words[:, cols].bitcast(FP8X4), scales=scales[:, cols], in_=rounded[:]))
-            if c == 0 and u == 3:
+            if (c, g, u) == (0, 0, 3):
                 for later in range(4):
-                    project_a([(g, 1, later)])
+                    project_a([(1, 1, later)])
         nc.vector.quantize_mx(**waiting.pop())
-
-        bias = held("bias", [P, N // P], F32)
-        bias_ps = acc_pool.tile([P, PASS], F32, name="acc")
-        nc.tensor.transpose(bias_ps[:, 0:P], bias_rows[:], ident[:])
-        nc.scalar.copy(bias[:], bias_ps[:, 0 : N // P])
 
         def y_pass(bank, c, g, nt):
             words, scales = h[c, g]

@@ -159,26 +159,21 @@ def tile_list_kg_max_bias_kernel(
         wbq[1] = quantise_wb(1, wb1_rounded, held("wb1", [P, PASS], U32))
         tab2_g = [gather_tab2(c, held("tab2_g%d" % c, [P, HALF], U32)) for c in range(2)]
 
-        def ha_pass(bank, a, c, g, u):
+        def project_a(c, g):
+            ha[c, g] = held("ha%d%d" % (c, g), [P, 4, HALF], F32)
             for t in range(4):
-                nc.tensor.matmul_mx(
-                    out=bank[:, t, :],
-                    lhsT=wa[g][:, a, P * t : P * (t + 1)].bitcast(FP8X4),
-                    lhsT_scale=wa_sc[:, a, PASS * g + P * t : PASS * g + P * (t + 1)],
-                    rhs=tab_g[c][:, a, 2 * UNIT * u : 2 * UNIT * (u + 1)].bitcast(FP4X4),
-                    rhs_scale=tab_sc[:, a, HALF * c + UNIT * u : HALF * c + UNIT * (u + 1)],
-                    start=(a == 0 and t == 0),
-                    stop=(a == 1 and t == 3),
-                )
-
-        def project_a(group):
-            banks = [acc_pool.tile([P, 4, UNIT], F32, name="acc") for unit in group]
-            for bank, unit in zip(banks, group):
-                ha_pass(bank, 0, *unit)
-            for bank, unit in zip(banks, group):
-                ha_pass(bank, 1, *unit)
-                ha[unit] = held("ha%d%d%d" % unit, [P, 4 * UNIT], F32)
-                nc.scalar.copy(ha[unit][:].rearrange("p (j t) -> p j t", t=4), bank[:].rearrange("p t j -> p j t"))
+                bank = acc_pool.tile([P, HALF], F32, name="acc")
+                for a in range(2):
+                    nc.tensor.matmul_mx(
+                        out=bank[:],
+                        lhsT=wa[g][:, a, P * t : P * (t + 1)].bitcast(FP8X4),
+                        lhsT_scale=wa_sc[:, a, PASS * g + P * t : PASS * g + P * (t + 1)],
+                        rhs=tab_g[c][:, a, :].bitcast(FP4X4),
+                        rhs_scale=tab_sc[:, a, HALF * c : HALF * (c + 1)],
+                        start=(a == 0),
+                        stop=(a == 1),
+                    )
+                nc.scalar.copy(ha[c, g][:, t, :], bank[:])
 
         def join(c, g, u, ha, wbq, rounded):
             words, scales = wbq
@@ -194,17 +189,16 @@ def tile_list_kg_max_bias_kernel(
                     stop=True,
                 )
             nc.vector.tensor_tensor(
-                rounded.rearrange("p (j t) -> p j t", t=4),
-                bank[:].rearrange("p t j -> p j t"),
-                ha[:].rearrange("p (j t) -> p j t", t=4),
+                rounded.rearrange("p (j i t) -> p j t i", t=4, i=2),
+                bank[:].rearrange("p t (j i) -> p j t i", i=2),
+                ha[:, :, UNIT * u : UNIT * (u + 1)].rearrange("p t (j i) -> p j t i", i=2),
                 MAX,
             )
 
         units = [(c, g, u) for c in range(2) for g in range(2) for u in range(4)]
         ha = {}
         for c, g in ((0, 0), (1, 0), (0, 1)):
-            for u in range(4):
-                project_a([(c, g, u)])
+            project_a(c, g)
         h = {}
         for c in range(2):
             for g in range(2):
@@ -214,7 +208,7 @@ def tile_list_kg_max_bias_kernel(
             s = u % 2
             if s == 0:
                 rounded = held("h_bf%d" % n, [P, 8 * UNIT], BF16)
-            join(c, g, u, ha[c, g, u], wbq[g], rounded[:, 4 * UNIT * s : 4 * UNIT * (s + 1)])
+            join(c, g, u, ha[c, g], wbq[g], rounded[:, 4 * UNIT * s : 4 * UNIT * (s + 1)])
             if s == 0 and waiting:
                 nc.vector.quantize_mx(**waiting.pop())
             if s == 1:
@@ -222,8 +216,7 @@ def tile_list_kg_max_bias_kernel(
                 cols = slice(UNIT * (u - 1), UNIT * (u + 1))
                 waiting.append(dict(out=words[:, cols].bitcast(FP8X4), scales=scales[:, cols], in_=rounded[:]))
             if (c, g, u) == (0, 0, 3):
-                for later in range(4):
-                    project_a([(1, 1, later)])
+                project_a(1, 1)
         nc.vector.quantize_mx(**waiting.pop())
 
         def y_pass(bank, c, g, nt):

@@ -1,7 +1,6 @@
 from contextlib import ExitStack
 
 import concourse.mybir as mybir
-from concourse.masks import make_identity
 
 K, L, R, N, T, J = 1024, 512, 1024, 1024, 4096, 1024
 FLOPS = 2 * J * (K * R + L * R + R * N)
@@ -52,15 +51,16 @@ def tile_list_kg_max_bias_kernel(
         nc.sync.dma_start(tab_sc_win[96:P, :].bitcast(I32), tab_scales.rearrange("a q t -> q a t").bitcast(I32))
         nc.sync.dma_start(wa_sc_raw[96:P, :].bitcast(I32), wa_scales.rearrange("a q r -> q a r").bitcast(I32))
         nc.sync.dma_start(idx2[:], offs2)
-        nc.sync.dma_start(tab2_sc_win[112:P, :].bitcast(I32), tab2_scales[0].bitcast(I32))
+        nc.sync.dma_start(tab2_sc_win[48:64, :].bitcast(I32), tab2_scales[0].bitcast(I32))
         nc.vector.memset(tab_sc_win[0:96, :].bitcast(I32), 0)
         nc.vector.memset(wa_sc_raw[0:96, :].bitcast(I32), 0)
-        nc.vector.memset(tab2_sc_win[0:112, :].bitcast(I32), 0)
         tab_sc = held("tab_sc", [P, 2, J], U8)
         wa_sc = held("wa_sc", [P, 2, R], U8)
         tab2_sc = held("tab2_sc", [P, J], U8)
-        nc.vector.memset(tab_sc[:].bitcast(I32), 0)
+        nc.vector.memset(tab2_sc_win[0:48, :].bitcast(I32), 0)
+        nc.gpsimd.memset(tab_sc[:].bitcast(I32), 0)
         nc.gpsimd.memset(wa_sc[:].bitcast(I32), 0)
+        nc.gpsimd.memset(tab2_sc_win[64:P, :].bitcast(I32), 0)
         nc.gpsimd.memset(tab2_sc[:].bitcast(I32), 0)
 
         tab_win = at("tab_win", [P, T], U32, 4 * KB)
@@ -68,17 +68,6 @@ def tile_list_kg_max_bias_kernel(
         wa_hbm = wa_words.rearrange("a p r i -> p a (r i)")
         wa_raw = [at("wa_raw0", [P, 2, PASS], I32, 20 * KB)]
         nc.sync.dma_start(wa_raw[0][:], wa_hbm[:, :, 0 : 4 * PASS].bitcast(I32))
-
-        bias_rows = held("bias_rows", [P, P], F32)
-        nc.gpsimd.dma_start(bias_rows[P - N // P : P, :], b.rearrange("(c p) -> c p", p=P))
-        nc.gpsimd.memset(bias_rows[0 : P - N // P, :], 0.0)
-        ident = held("ident", [P, P], F32)
-        make_identity(nc, ident[:])
-
-        bias = held("bias", [P, N // P], F32)
-        bias_ps = acc_pool.tile([P, PASS], F32, name="acc")
-        nc.tensor.transpose(bias_ps[:, 0:P], bias_rows[:], ident[:])
-        nc.scalar.copy(bias[:], bias_ps[:, P - N // P : P])
 
         def deal_rows(plane, rows, first, count):
             for q in range(4):
@@ -103,7 +92,7 @@ def tile_list_kg_max_bias_kernel(
 
         tab2_sc_g = held("tab2_sc_g", [P, J], U8)
         nc.vector.tensor_copy(tab2_sc_g[:], tab2_sc_win[:].indirect(idx2[:]))
-        deal_rows(tab2_sc, tab2_sc_g, 112, 4)
+        deal_rows(tab2_sc, tab2_sc_g, 48, 4)
         wb_raw.append(at("wb_raw1", [P, 4, PASS], F32, 40 * KB))
         nc.sync.dma_start(wb_raw[1][:], wb_hbm[:, :, PASS : 2 * PASS])
         tab2_win = at("tab2_win", [P, T], U32, 48 * KB)
@@ -151,6 +140,10 @@ def tile_list_kg_max_bias_kernel(
                 en_sc[32 * q : 32 * q + 4, :, :].bitcast(I32),
                 en_scales[:, 4 * q : 4 * q + 4, :].rearrange("a r n -> r a n").bitcast(I32),
             )
+
+        bias = at("bias", [P, N // P], F32, 12 * KB)
+        with nc.allow_non_contiguous_dma(reason="one bias value for each partition and tile of candidates"):
+            nc.sync.dma_start(bias[:], b.rearrange("(c p) -> p c", p=P))
 
         wb0_rounded = round_wb(nc.vector.tensor_copy, 0, held("wb_bf0", [P, 4 * PASS], BF16))
         wa.append(order_wa_words(1, held("wa1", [P, 2, PASS], I32)))
@@ -219,6 +212,8 @@ def tile_list_kg_max_bias_kernel(
                 project_a(1, 1)
         nc.vector.quantize_mx(**waiting.pop())
 
+        out_tiles = out.rearrange("(nt p) j -> p nt j", p=P)
+
         def y_pass(bank, c, g, nt):
             words, scales = h[c, g]
             nc.tensor.matmul_mx(
@@ -241,9 +236,11 @@ def tile_list_kg_max_bias_kernel(
                     banks[nt] = acc_pool.tile([P, HALF], F32, name="acc")
                     y_pass(banks[nt], c, 0, nt)
                 y_pass(banks[nt], c, 1, nt)
-                scores = stage.tile([P, HALF], F32, name="scores")
+                if nt % 2 == 0:
+                    scores = stage.tile([P, 2, HALF], F32, name="scores")
                 if c == 1 and nt % 2 == 1:
-                    nc.vector.tensor_scalar_add(scores[:], banks[nt][:], bias[:, nt : nt + 1])
+                    nc.vector.tensor_scalar_add(scores[:, 1, :], banks[nt][:], bias[:, nt : nt + 1])
                 else:
-                    nc.scalar.activation(scores[:], banks[nt][:], IDENTITY, bias=bias[:, nt : nt + 1])
-                nc.sync.dma_start(out[P * nt : P * (nt + 1), HALF * c : HALF * (c + 1)], scores[:])
+                    nc.scalar.activation(scores[:, nt % 2, :], banks[nt][:], IDENTITY, bias=bias[:, nt : nt + 1])
+                if nt % 2 == 1:
+                    nc.sync.dma_start(out_tiles[:, nt - 1 : nt + 1, HALF * c : HALF * (c + 1)], scores[:])

@@ -127,6 +127,17 @@ def tile_list_kg_max_bias_kernel(
             nc.vector.quantize_mx(out=words[:].bitcast(FP8X4), scales=scales[:], in_=rounded[:])
             return words, scales
 
+        warm = acc_pool.tile([P, HALF], F32, name="acc")
+        for t in range(2):
+            nc.tensor.matmul_mx(
+                out=warm[:],
+                lhsT=wa_raw[0][:, 0, P * t : P * (t + 1)].bitcast(FP8X4),
+                lhsT_scale=wa_sc_ord[:, P * t : P * (t + 1)],
+                rhs=wa_raw[0][:, 1, :].bitcast(FP8X4),
+                rhs_scale=wa_sc_ord[:, 0:PASS],
+                start=True,
+                stop=True,
+            )
         tab_g = [gather_tab(0, held("tab_pairs0", [P, HALF], U32))]
         wa = [order_wa_words(0, held("wa0", [P, 2, PASS], I32))]
         tab_g.append(gather_tab(1, at("tab_pairs1", [P, HALF], U32, 20 * KB)))

@@ -21,7 +21,23 @@ PASS = 512
 HALF = 512
 UNIT = 128
 KB = 1024
-ACC_BANKS = 5
+HB_BANKS = 3
+ACC_BANKS = 8 - HB_BANKS
+STORES = 8
+WARM_UP = 2
+
+ROWS_AT = 96
+TAB2_ROWS_AT = 48
+
+TAB_SC_WIN_AT = 0
+TAB_WIN_AT = 4 * KB
+EN_AT, EN_SC_AT, BIAS_AT = 4 * KB, 8 * KB, 12 * KB
+WA_RAW0_AT = 20 * KB
+TAB_PAIRS1_AT = 20 * KB
+WA_SC_RAW_AT = 32 * KB - 512
+WA_RAW1_AT, WB_RAW_AT = 28 * KB, 32 * KB
+TAB2_SC_WIN_AT = 62 * KB
+TAB2_WIN_AT = 48 * KB
 
 
 def tile_list_kg_max_bias_kernel(
@@ -32,70 +48,68 @@ def tile_list_kg_max_bias_kernel(
         lists = ctx.enter_context(tc.tile_pool(name="lists", bufs=1))
         keep = ctx.enter_context(tc.tile_pool(name="keep", bufs=1))
         placed = ctx.enter_context(tc.tile_pool(name="placed", bufs=1))
-        stage = ctx.enter_context(tc.tile_pool(name="stage", bufs=8))
+        stage = ctx.enter_context(tc.tile_pool(name="stage", bufs=STORES))
         acc_pool = ctx.enter_context(tc.psum_pool(name="acc", bufs=ACC_BANKS))
-        hb_pool = ctx.enter_context(tc.psum_pool(name="hb", bufs=3))
+        hb_pool = ctx.enter_context(tc.psum_pool(name="hb", bufs=HB_BANKS))
 
-        def held(name, shape, dtype, tag=None):
-            return keep.tile(shape, dtype, name=name, tag=tag or name, align_bytes=64)
+        def held(name, shape, dtype):
+            return keep.tile(shape, dtype, name=name, tag=name, align_bytes=64)
 
         def at(name, shape, dtype, offset):
             return placed.tile(shape, dtype, name=name, tag=name, align_bytes=64, offset=offset)
 
         idx = lists.tile([P, J // 16], U16, name="idx")
         idx2 = lists.tile([P, J // 16], U16, name="idx2")
-        tab_sc_win = at("tab_sc_win", [P, T], U8, 0)
-        wa_sc_raw = at("wa_sc_raw", [P, R], U8, 32 * KB - 512)
-        tab2_sc_win = at("tab2_sc_win", [P, T], U8, 46 * KB)
+        tab_sc_win = at("tab_sc_win", [P, T], U8, TAB_SC_WIN_AT)
+        wa_sc_raw = at("wa_sc_raw", [P, R], U8, WA_SC_RAW_AT)
+        tab2_sc_win = at("tab2_sc_win", [P, T], U8, TAB2_SC_WIN_AT)
         nc.sync.dma_start(idx[:], offs)
-        nc.sync.dma_start(tab_sc_win[96:P, :].bitcast(I32), tab_scales.rearrange("a q t -> q a t").bitcast(I32))
-        nc.sync.dma_start(wa_sc_raw[96:P, :].bitcast(I32), wa_scales.rearrange("a q r -> q a r").bitcast(I32))
+        nc.sync.dma_start(tab_sc_win[ROWS_AT:P, :].bitcast(I32), tab_scales.rearrange("a q t -> q a t").bitcast(I32))
+        nc.sync.dma_start(wa_sc_raw[ROWS_AT:P, :].bitcast(I32), wa_scales.rearrange("a q r -> q a r").bitcast(I32))
         nc.sync.dma_start(idx2[:], offs2)
-        nc.sync.dma_start(tab2_sc_win[48:64, :].bitcast(I32), tab2_scales[0].bitcast(I32))
-        nc.vector.memset(tab_sc_win[0:96, :].bitcast(I32), 0)
-        nc.vector.memset(wa_sc_raw[0:96, :].bitcast(I32), 0)
+        nc.sync.dma_start(tab2_sc_win[TAB2_ROWS_AT : TAB2_ROWS_AT + 16, :].bitcast(I32), tab2_scales[0].bitcast(I32))
+        nc.vector.memset(tab_sc_win[0:ROWS_AT, :].bitcast(I32), 0)
+        nc.vector.memset(wa_sc_raw[0:ROWS_AT, :].bitcast(I32), 0)
         tab_sc = held("tab_sc", [P, 2, J], U8)
         wa_sc = held("wa_sc", [P, 2, R], U8)
         tab2_sc = held("tab2_sc", [P, J], U8)
-        nc.vector.memset(tab2_sc_win[0:48, :].bitcast(I32), 0)
+        nc.vector.memset(tab2_sc_win[0:TAB2_ROWS_AT, :].bitcast(I32), 0)
         nc.gpsimd.memset(tab_sc[:].bitcast(I32), 0)
         nc.gpsimd.memset(wa_sc[:].bitcast(I32), 0)
-        nc.gpsimd.memset(tab2_sc_win[64:P, :].bitcast(I32), 0)
+        nc.gpsimd.memset(tab2_sc_win[TAB2_ROWS_AT + 16 : P, :].bitcast(I32), 0)
         nc.gpsimd.memset(tab2_sc[:].bitcast(I32), 0)
 
-        tab_win = at("tab_win", [P, T], U32, 4 * KB)
+        tab_win = at("tab_win", [P, T], U32, TAB_WIN_AT)
         nc.sync.dma_start(tab_win[:].bitcast(I32), tab_words[0].rearrange("p t i -> p (t i)").bitcast(I32))
         wa_hbm = wa_words.rearrange("a p r i -> p a (r i)")
-        wa_raw = [at("wa_raw0", [P, 2, PASS], I32, 20 * KB)]
+        wa_raw = [at("wa_raw0", [P, 2, PASS], I32, WA_RAW0_AT)]
         nc.sync.dma_start(wa_raw[0][:], wa_hbm[:, :, 0 : 4 * PASS].bitcast(I32))
 
         def deal_rows(plane, rows, first, count):
-            for q in range(4):
+            for quadrant in range(4):
                 nc.scalar.dma_start(
-                    plane[32 * q : 32 * q + 4].bitcast(I32), rows[first + count * q : first + count * (q + 1), :].bitcast(I32)
+                    plane[32 * quadrant : 32 * quadrant + 4].bitcast(I32),
+                    rows[first + count * quadrant : first + count * (quadrant + 1), :].bitcast(I32),
                 )
 
         tab_sc_g = held("tab_sc_g", [P, J], U8)
         nc.vector.tensor_copy(tab_sc_g[:], tab_sc_win[:].indirect(idx[:]))
-        deal_rows(tab_sc, tab_sc_g, 96, 8)
+        deal_rows(tab_sc, tab_sc_g, ROWS_AT, 8)
         wa_sc_ord = held("wa_sc_ord", [P, R], U8)
         nc.vector.tensor_copy(
             wa_sc_ord[:].rearrange("p (g t m) -> p g t m", t=4, m=P), wa_sc_raw[:].rearrange("p (g m t) -> p g t m", t=4, m=P)
         )
-        deal_rows(wa_sc, wa_sc_ord, 96, 8)
+        deal_rows(wa_sc, wa_sc_ord, ROWS_AT, 8)
 
-        wb_hbm = wb.rearrange("(p i) r -> p i r", i=4)
-        wb_raw = [at("wb_raw0", [P, 4, PASS], F32, 24 * KB)]
-        nc.sync.dma_start(wb_raw[0][:], wb_hbm[:, :, 0:PASS])
-        wa_raw.append(at("wa_raw1", [P, 2, PASS], I32, 32 * KB))
+        wa_raw.append(at("wa_raw1", [P, 2, PASS], I32, WA_RAW1_AT))
         nc.sync.dma_start(wa_raw[1][:], wa_hbm[:, :, 4 * PASS : 8 * PASS].bitcast(I32))
+        wb_raw = at("wb_raw", [P, 4, R], F32, WB_RAW_AT)
+        nc.sync.dma_start(wb_raw[:], wb.rearrange("(p i) r -> p i r", i=4))
 
         tab2_sc_g = held("tab2_sc_g", [P, J], U8)
         nc.vector.tensor_copy(tab2_sc_g[:], tab2_sc_win[:].indirect(idx2[:]))
-        deal_rows(tab2_sc, tab2_sc_g, 48, 4)
-        wb_raw.append(at("wb_raw1", [P, 4, PASS], F32, 40 * KB))
-        nc.sync.dma_start(wb_raw[1][:], wb_hbm[:, :, PASS : 2 * PASS])
-        tab2_win = at("tab2_win", [P, T], U32, 48 * KB)
+        deal_rows(tab2_sc, tab2_sc_g, TAB2_ROWS_AT, 4)
+        tab2_win = at("tab2_win", [P, T], U32, TAB2_WIN_AT)
         nc.sync.dma_start(tab2_win[:].bitcast(I32), tab2_words[0].rearrange("p t i -> p (t i)").bitcast(I32))
 
         def list_half(offsets, c):
@@ -107,28 +121,35 @@ def tile_list_kg_max_bias_kernel(
             nc.vector.tensor_copy(words[:].bitcast(U16), pairs[:].bitcast(U16).rearrange("p (j d) -> p d j", d=2))
             return words
 
-        def order_wa_words(g, words):
+        def order_wa_words(g):
+            words = held("wa%d" % g, [P, 2, PASS], I32)
             nc.vector.tensor_copy(
                 words[:].rearrange("p a (t m i) -> p a m t i", t=4, i=4),
                 wa_raw[g][:].rearrange("p a (m i t) -> p a m t i", t=4, i=4),
             )
             return words
 
-        def gather_tab2(c, words):
+        def gather_tab2(c):
+            words = held("tab2_g%d" % c, [P, HALF], U32)
             nc.vector.tensor_copy(words[:], tab2_win[:].indirect(list_half(idx2, c)))
             return words
 
-        def round_wb(copy, g, rounded):
-            copy(rounded[:].rearrange("p (t m i) -> p m t i", t=4, i=4), wb_raw[g][:].rearrange("p i (m t) -> p m t i", t=4))
+        def round_wb(g):
+            rounded = held("wb_bf%d" % g, [P, 4 * PASS], BF16)
+            nc.vector.tensor_copy(
+                rounded[:].rearrange("p (t m i) -> p m t i", t=4, i=4),
+                wb_raw[:, :, PASS * g : PASS * (g + 1)].rearrange("p i (m t) -> p m t i", t=4),
+            )
             return rounded
 
-        def quantise_wb(g, rounded, words):
+        def quantise_wb(g, rounded):
+            words = held("wb%d" % g, [P, PASS], U32)
             scales = held("wb_sc%d" % g, [P, PASS], U8)
             nc.vector.quantize_mx(out=words[:].bitcast(FP8X4), scales=scales[:], in_=rounded[:])
             return words, scales
 
         warm = acc_pool.tile([P, HALF], F32, name="acc")
-        for t in range(2):
+        for t in range(WARM_UP):
             nc.tensor.matmul_mx(
                 out=warm[:],
                 lhsT=wa_raw[0][:, 0, P * t : P * (t + 1)].bitcast(FP8X4),
@@ -138,30 +159,31 @@ def tile_list_kg_max_bias_kernel(
                 start=True,
                 stop=True,
             )
-        tab_g = [gather_tab(0, held("tab_pairs0", [P, HALF], U32))]
-        wa = [order_wa_words(0, held("wa0", [P, 2, PASS], I32))]
-        tab_g.append(gather_tab(1, at("tab_pairs1", [P, HALF], U32, 20 * KB)))
 
-        en = at("en", [P, 2, 2 * N], U8, 4 * KB)
-        nc.sync.dma_start(en[:].bitcast(I32), en_words.rearrange("a p c -> p a c").bitcast(I32))
-        en_sc = at("en_sc", [P, 2, N], U8, 8 * KB)
+        tab_g = [gather_tab(0, held("tab_pairs0", [P, HALF], U32))]
+        wa = [order_wa_words(0)]
+        tab_g.append(gather_tab(1, at("tab_pairs1", [P, HALF], U32, TAB_PAIRS1_AT)))
+
+        en = at("en", [P, 2, 2 * N], U8, EN_AT)
+        nc.sync.dma_start(en[:].bitcast(I32), en_words.rearrange("g p x -> p g x").bitcast(I32))
+        en_sc = at("en_sc", [P, 2, N], U8, EN_SC_AT)
         nc.vector.memset(en_sc[:].bitcast(I32), 0)
-        for q in range(4):
+        for quadrant in range(4):
             nc.sync.dma_start(
-                en_sc[32 * q : 32 * q + 4, :, :].bitcast(I32),
-                en_scales[:, 4 * q : 4 * q + 4, :].rearrange("a r n -> r a n").bitcast(I32),
+                en_sc[32 * quadrant : 32 * quadrant + 4, :, :].bitcast(I32),
+                en_scales[:, 4 * quadrant : 4 * quadrant + 4, :].rearrange("g s n -> s g n").bitcast(I32),
             )
 
-        bias = at("bias", [P, N // P], F32, 12 * KB)
+        bias = at("bias", [P, N // P], F32, BIAS_AT)
         with nc.allow_non_contiguous_dma(reason="one bias value for each partition and tile of candidates"):
-            nc.sync.dma_start(bias[:], b.rearrange("(c p) -> p c", p=P))
+            nc.sync.dma_start(bias[:], b.rearrange("(nt p) -> p nt", p=P))
 
-        wb0_rounded = round_wb(nc.vector.tensor_copy, 0, held("wb_bf0", [P, 4 * PASS], BF16))
-        wa.append(order_wa_words(1, held("wa1", [P, 2, PASS], I32)))
-        wbq = {0: quantise_wb(0, wb0_rounded, held("wb0", [P, PASS], U32))}
-        wb1_rounded = round_wb(nc.vector.tensor_copy, 1, held("wb_bf1", [P, 4 * PASS], BF16))
-        wbq[1] = quantise_wb(1, wb1_rounded, held("wb1", [P, PASS], U32))
-        tab2_g = [gather_tab2(c, held("tab2_g%d" % c, [P, HALF], U32)) for c in range(2)]
+        wa.append(order_wa_words(1))
+        wb_rounded = [round_wb(g) for g in range(2)]
+        wbq = [quantise_wb(g, wb_rounded[g]) for g in range(2)]
+        tab2_g = [gather_tab2(c) for c in range(2)]
+
+        ha = {}
 
         def project_a(c, g):
             ha[c, g] = held("ha%d%d" % (c, g), [P, 4, HALF], F32)
@@ -179,8 +201,8 @@ def tile_list_kg_max_bias_kernel(
                     )
                 nc.scalar.copy(ha[c, g][:, t, :], bank[:])
 
-        def join(c, g, u, ha, wbq, rounded):
-            words, scales = wbq
+        def join(c, g, u, rounded):
+            words, scales = wbq[g]
             bank = hb_pool.tile([P, 4, UNIT], F32, name="hb")
             for t in range(4):
                 nc.tensor.matmul_mx(
@@ -195,31 +217,30 @@ def tile_list_kg_max_bias_kernel(
             nc.vector.tensor_tensor(
                 rounded.rearrange("p (j i t) -> p j t i", t=4, i=2),
                 bank[:].rearrange("p t (j i) -> p j t i", i=2),
-                ha[:, :, UNIT * u : UNIT * (u + 1)].rearrange("p t (j i) -> p j t i", i=2),
+                ha[c, g][:, :, UNIT * u : UNIT * (u + 1)].rearrange("p t (j i) -> p j t i", i=2),
                 MAX,
             )
 
-        units = [(c, g, u) for c in range(2) for g in range(2) for u in range(4)]
-        ha = {}
         for c, g in ((0, 0), (1, 0), (0, 1)):
             project_a(c, g)
         h = {}
         for c in range(2):
             for g in range(2):
                 h[c, g] = (held("h%d%d" % (c, g), [P, HALF], U32), held("h_sc%d%d" % (c, g), [P, HALF], U8))
+        units_per_half = HALF // UNIT
         waiting = []
-        for n, (c, g, u) in enumerate(units):
-            s = u % 2
-            if s == 0:
-                rounded = held("h_bf%d" % n, [P, 8 * UNIT], BF16)
-            join(c, g, u, ha[c, g], wbq[g], rounded[:, 4 * UNIT * s : 4 * UNIT * (s + 1)])
-            if s == 0 and waiting:
+        for c, g, u in [(c, g, u) for c in range(2) for g in range(2) for u in range(units_per_half)]:
+            second = u % 2
+            if second == 0:
+                rounded = held("h_bf%d%d%d" % (c, g, u), [P, 8 * UNIT], BF16)
+            join(c, g, u, rounded[:, 4 * UNIT * second : 4 * UNIT * (second + 1)])
+            if second == 0 and waiting:
                 nc.vector.quantize_mx(**waiting.pop())
-            if s == 1:
+            if second == 1:
                 words, scales = h[c, g]
                 cols = slice(UNIT * (u - 1), UNIT * (u + 1))
                 waiting.append(dict(out=words[:, cols].bitcast(FP8X4), scales=scales[:, cols], in_=rounded[:]))
-            if (c, g, u) == (0, 0, 3):
+            if (c, g, u) == (0, 0, units_per_half - 1):
                 project_a(1, 1)
         nc.vector.quantize_mx(**waiting.pop())
 
@@ -238,20 +259,16 @@ def tile_list_kg_max_bias_kernel(
             )
 
         for c in range(2):
-            banks = {}
-            for nt in range(ACC_BANKS):
-                banks[nt] = acc_pool.tile([P, HALF], F32, name="acc")
-                y_pass(banks[nt], c, 0, nt)
             for nt in range(N // P):
-                if nt not in banks:
-                    banks[nt] = acc_pool.tile([P, HALF], F32, name="acc")
-                    y_pass(banks[nt], c, 0, nt)
-                y_pass(banks[nt], c, 1, nt)
-                if nt % 2 == 0:
+                bank = acc_pool.tile([P, HALF], F32, name="acc")
+                y_pass(bank, c, 0, nt)
+                y_pass(bank, c, 1, nt)
+                second = nt % 2
+                if second == 0:
                     scores = stage.tile([P, 2, HALF], F32, name="scores")
-                if c == 1 and nt % 2 == 1:
-                    nc.vector.tensor_scalar_add(scores[:, 1, :], banks[nt][:], bias[:, nt : nt + 1])
+                if c == 1 and second == 1:
+                    nc.vector.tensor_scalar_add(scores[:, second, :], bank[:], bias[:, nt : nt + 1])
                 else:
-                    nc.scalar.activation(scores[:, nt % 2, :], banks[nt][:], IDENTITY, bias=bias[:, nt : nt + 1])
-                if nt % 2 == 1:
+                    nc.scalar.activation(scores[:, second, :], bank[:], IDENTITY, bias=bias[:, nt : nt + 1])
+                if second == 1:
                     nc.sync.dma_start(out_tiles[:, nt - 1 : nt + 1, HALF * c : HALF * (c + 1)], scores[:])

@@ -21,23 +21,27 @@ PASS = 512
 HALF = 512
 UNIT = 128
 KB = 1024
-HB_BANKS = 3
-ACC_BANKS = 8 - HB_BANKS
-STORES = 8
+BANK = 2 * KB
 WARM_UP = 2
+STORES = 8
 
 ROWS_AT = 96
-TAB2_ROWS_AT = 48
+TAB2_ROWS_AT = 112
 
-TAB_SC_WIN_AT = 0
-TAB_WIN_AT = 4 * KB
-EN_AT, EN_SC_AT, BIAS_AT = 4 * KB, 8 * KB, 12 * KB
-WA_RAW0_AT = 20 * KB
-TAB_PAIRS1_AT = 20 * KB
-WA_SC_RAW_AT = 32 * KB - 512
-WA_RAW1_AT, WB_RAW_AT = 28 * KB, 32 * KB
-TAB2_SC_WIN_AT = 62 * KB
-TAB2_WIN_AT = 48 * KB
+TAB2_WIN_AT, WB_RAW0_AT = 0, 16 * KB
+TAB_SC_WIN_AT = 14 * KB
+WA_RAW0_AT, WA_RAW1_AT = 24 * KB, 28 * KB
+WA_SC_RAW_AT = 28 * KB - 512
+TAB_PAIRS1_AT = 24 * KB
+WB_RAW1_AT, BIAS_AT, EN_AT = 32 * KB, 40 * KB, 41 * KB
+TAB2_SC_WIN_AT = 38 * KB
+WB_BF0_AT = 56 * KB
+EN_SC_AT = 56 * KB
+WB_BF1_AT = 60 * KB
+H00_AT = 60 * KB
+HA01_AT = 48 * KB
+HA11_AT = 32 * KB
+H_BF10_AT = 48 * KB
 
 
 def tile_list_kg_max_bias_kernel(
@@ -49,8 +53,7 @@ def tile_list_kg_max_bias_kernel(
         keep = ctx.enter_context(tc.tile_pool(name="keep", bufs=1))
         placed = ctx.enter_context(tc.tile_pool(name="placed", bufs=1))
         stage = ctx.enter_context(tc.tile_pool(name="stage", bufs=STORES))
-        acc_pool = ctx.enter_context(tc.psum_pool(name="acc", bufs=ACC_BANKS))
-        hb_pool = ctx.enter_context(tc.psum_pool(name="hb", bufs=HB_BANKS))
+        psum = ctx.enter_context(tc.psum_pool(name="psum", bufs=1))
 
         def held(name, shape, dtype):
             return keep.tile(shape, dtype, name=name, tag=name, align_bytes=64)
@@ -58,59 +61,69 @@ def tile_list_kg_max_bias_kernel(
         def at(name, shape, dtype, offset):
             return placed.tile(shape, dtype, name=name, tag=name, align_bytes=64, offset=offset)
 
+        def bank_at(name, shape, index):
+            return psum.tile(shape, F32, name=name, tag=name, offset=index * BANK)
+
         idx = lists.tile([P, J // 16], U16, name="idx")
         idx2 = lists.tile([P, J // 16], U16, name="idx2")
         tab_sc_win = at("tab_sc_win", [P, T], U8, TAB_SC_WIN_AT)
         wa_sc_raw = at("wa_sc_raw", [P, R], U8, WA_SC_RAW_AT)
         tab2_sc_win = at("tab2_sc_win", [P, T], U8, TAB2_SC_WIN_AT)
+        nc.sync.dma_start(wa_sc_raw[ROWS_AT:P, :].bitcast(I32), wa_scales.rearrange("a q r -> q a r").bitcast(I32))
         nc.sync.dma_start(idx[:], offs)
         nc.sync.dma_start(tab_sc_win[ROWS_AT:P, :].bitcast(I32), tab_scales.rearrange("a q t -> q a t").bitcast(I32))
-        nc.sync.dma_start(wa_sc_raw[ROWS_AT:P, :].bitcast(I32), wa_scales.rearrange("a q r -> q a r").bitcast(I32))
         nc.sync.dma_start(idx2[:], offs2)
         nc.sync.dma_start(tab2_sc_win[TAB2_ROWS_AT : TAB2_ROWS_AT + 16, :].bitcast(I32), tab2_scales[0].bitcast(I32))
-        nc.vector.memset(tab_sc_win[0:ROWS_AT, :].bitcast(I32), 0)
         nc.vector.memset(wa_sc_raw[0:ROWS_AT, :].bitcast(I32), 0)
+        nc.vector.memset(tab_sc_win[0:ROWS_AT, :].bitcast(I32), 0)
         tab_sc = held("tab_sc", [P, 2, J], U8)
         wa_sc = held("wa_sc", [P, 2, R], U8)
         tab2_sc = held("tab2_sc", [P, J], U8)
-        nc.vector.memset(tab2_sc_win[0:TAB2_ROWS_AT, :].bitcast(I32), 0)
-        nc.gpsimd.memset(tab_sc[:].bitcast(I32), 0)
         nc.gpsimd.memset(wa_sc[:].bitcast(I32), 0)
-        nc.gpsimd.memset(tab2_sc_win[TAB2_ROWS_AT + 16 : P, :].bitcast(I32), 0)
+        nc.gpsimd.memset(tab_sc[:].bitcast(I32), 0)
+        nc.gpsimd.memset(tab2_sc_win[0:TAB2_ROWS_AT, :].bitcast(I32), 0)
         nc.gpsimd.memset(tab2_sc[:].bitcast(I32), 0)
 
-        tab_win = at("tab_win", [P, T], U32, TAB_WIN_AT)
+        tab_win = held("tab_win", [P, T], U32)
         nc.sync.dma_start(tab_win[:].bitcast(I32), tab_words[0].rearrange("p t i -> p (t i)").bitcast(I32))
-        wa_hbm = wa_words.rearrange("a p r i -> p a (r i)")
-        wa_raw = [at("wa_raw0", [P, 2, PASS], I32, WA_RAW0_AT)]
-        nc.sync.dma_start(wa_raw[0][:], wa_hbm[:, :, 0 : 4 * PASS].bitcast(I32))
 
         def deal_rows(plane, rows, first, count):
             for quadrant in range(4):
-                nc.scalar.dma_start(
+                nc.sync.dma_start(
                     plane[32 * quadrant : 32 * quadrant + 4].bitcast(I32),
                     rows[first + count * quadrant : first + count * (quadrant + 1), :].bitcast(I32),
                 )
 
-        tab_sc_g = held("tab_sc_g", [P, J], U8)
-        nc.vector.tensor_copy(tab_sc_g[:], tab_sc_win[:].indirect(idx[:]))
-        deal_rows(tab_sc, tab_sc_g, ROWS_AT, 8)
         wa_sc_ord = held("wa_sc_ord", [P, R], U8)
         nc.vector.tensor_copy(
             wa_sc_ord[:].rearrange("p (g t m) -> p g t m", t=4, m=P), wa_sc_raw[:].rearrange("p (g m t) -> p g t m", t=4, m=P)
         )
         deal_rows(wa_sc, wa_sc_ord, ROWS_AT, 8)
+        wa_hbm = wa_words.rearrange("a p r i -> p a (r i)")
+        wa_raw = [at("wa_raw%d" % g, [P, 2, PASS], I32, offset) for g, offset in enumerate((WA_RAW0_AT, WA_RAW1_AT))]
+        for g in range(2):
+            nc.sync.dma_start(wa_raw[g][:], wa_hbm[:, :, 4 * PASS * g : 4 * PASS * (g + 1)].bitcast(I32))
 
-        wa_raw.append(at("wa_raw1", [P, 2, PASS], I32, WA_RAW1_AT))
-        nc.sync.dma_start(wa_raw[1][:], wa_hbm[:, :, 4 * PASS : 8 * PASS].bitcast(I32))
-        wb_raw = at("wb_raw", [P, 4, R], F32, WB_RAW_AT)
-        nc.sync.dma_start(wb_raw[:], wb.rearrange("(p i) r -> p i r", i=4))
+        tab_sc_g = held("tab_sc_g", [P, J], U8)
+        nc.vector.tensor_copy(tab_sc_g[:], tab_sc_win[:].indirect(idx[:]))
+        deal_rows(tab_sc, tab_sc_g, ROWS_AT, 8)
+        wb_hbm = wb.rearrange("(p i) r -> p i r", i=4)
+        wb_raw = [at("wb_raw0", [P, 4, PASS], F32, WB_RAW0_AT)]
+        nc.sync.dma_start(wb_raw[0][:], wb_hbm[:, :, 0:PASS])
+        tab2_win = at("tab2_win", [P, T], U32, TAB2_WIN_AT)
+        nc.sync.dma_start(tab2_win[:].bitcast(I32), tab2_words[0].rearrange("p t i -> p (t i)").bitcast(I32))
 
         tab2_sc_g = held("tab2_sc_g", [P, J], U8)
         nc.vector.tensor_copy(tab2_sc_g[:], tab2_sc_win[:].indirect(idx2[:]))
         deal_rows(tab2_sc, tab2_sc_g, TAB2_ROWS_AT, 4)
-        tab2_win = at("tab2_win", [P, T], U32, TAB2_WIN_AT)
-        nc.sync.dma_start(tab2_win[:].bitcast(I32), tab2_words[0].rearrange("p t i -> p (t i)").bitcast(I32))
+        wb_raw.append(at("wb_raw1", [P, 4, PASS], F32, WB_RAW1_AT))
+        nc.sync.dma_start(wb_raw[1][:], wb_hbm[:, :, PASS : 2 * PASS])
+
+        en = at("en", [P, 2, 2 * N], U8, EN_AT)
+        nc.sync.dma_start(en[:].bitcast(I32), en_words.rearrange("g p x -> p g x").bitcast(I32))
+        bias = at("bias", [P, N // P], F32, BIAS_AT)
+        with nc.allow_non_contiguous_dma(reason="one bias value for each partition and tile of candidates"):
+            nc.sync.dma_start(bias[:], b.rearrange("(nt p) -> p nt", p=P))
 
         def list_half(offsets, c):
             return offsets[:, c * HALF // 16 : (c + 1) * HALF // 16]
@@ -129,16 +142,14 @@ def tile_list_kg_max_bias_kernel(
             )
             return words
 
-        def gather_tab2(c):
-            words = held("tab2_g%d" % c, [P, HALF], U32)
+        def gather_tab2(c, words):
             nc.vector.tensor_copy(words[:], tab2_win[:].indirect(list_half(idx2, c)))
             return words
 
-        def round_wb(g):
-            rounded = held("wb_bf%d" % g, [P, 4 * PASS], BF16)
-            nc.vector.tensor_copy(
+        def round_wb(g, copy, rounded):
+            copy(
                 rounded[:].rearrange("p (t m i) -> p m t i", t=4, i=4),
-                wb_raw[:, :, PASS * g : PASS * (g + 1)].rearrange("p i (m t) -> p m t i", t=4),
+                wb_raw[g][:].rearrange("p i (m t) -> p m t i", t=4),
             )
             return rounded
 
@@ -148,7 +159,7 @@ def tile_list_kg_max_bias_kernel(
             nc.vector.quantize_mx(out=words[:].bitcast(FP8X4), scales=scales[:], in_=rounded[:])
             return words, scales
 
-        warm = acc_pool.tile([P, HALF], F32, name="acc")
+        warm = bank_at("warm", [P, HALF], 7)
         for t in range(WARM_UP):
             nc.tensor.matmul_mx(
                 out=warm[:],
@@ -163,32 +174,29 @@ def tile_list_kg_max_bias_kernel(
         tab_g = [gather_tab(0, held("tab_pairs0", [P, HALF], U32))]
         wa = [order_wa_words(0)]
         tab_g.append(gather_tab(1, at("tab_pairs1", [P, HALF], U32, TAB_PAIRS1_AT)))
+        wa.append(order_wa_words(1))
 
-        en = at("en", [P, 2, 2 * N], U8, EN_AT)
-        nc.sync.dma_start(en[:].bitcast(I32), en_words.rearrange("g p x -> p g x").bitcast(I32))
+        wbq = [quantise_wb(0, round_wb(0, nc.vector.tensor_copy, at("wb_bf0", [P, 4 * PASS], BF16, WB_BF0_AT)))]
+        tab2_g = [gather_tab2(c, held("tab2_g%d" % c, [P, HALF], U32)) for c in range(2)]
+        wbq.append(quantise_wb(1, round_wb(1, nc.scalar.copy, at("wb_bf1", [P, 4 * PASS], BF16, WB_BF1_AT))))
+
         en_sc = at("en_sc", [P, 2, N], U8, EN_SC_AT)
-        nc.vector.memset(en_sc[:].bitcast(I32), 0)
+        nc.gpsimd.memset(en_sc[:].bitcast(I32), 0)
         for quadrant in range(4):
             nc.sync.dma_start(
                 en_sc[32 * quadrant : 32 * quadrant + 4, :, :].bitcast(I32),
                 en_scales[:, 4 * quadrant : 4 * quadrant + 4, :].rearrange("g s n -> s g n").bitcast(I32),
             )
 
-        bias = at("bias", [P, N // P], F32, BIAS_AT)
-        with nc.allow_non_contiguous_dma(reason="one bias value for each partition and tile of candidates"):
-            nc.sync.dma_start(bias[:], b.rearrange("(nt p) -> p nt", p=P))
-
-        wa.append(order_wa_words(1))
-        wb_rounded = [round_wb(g) for g in range(2)]
-        wbq = [quantise_wb(g, wb_rounded[g]) for g in range(2)]
-        tab2_g = [gather_tab2(c) for c in range(2)]
-
         ha = {}
 
         def project_a(c, g):
-            ha[c, g] = held("ha%d%d" % (c, g), [P, 4, HALF], F32)
+            if g == 1:
+                ha[c, g] = at("ha%d1" % c, [P, 4, HALF], F32, (HA01_AT, HA11_AT)[c])
+            else:
+                ha[c, g] = held("ha%d%d" % (c, g), [P, 4, HALF], F32)
             for t in range(4):
-                bank = acc_pool.tile([P, HALF], F32, name="acc")
+                bank = bank_at("ha_ps%d%d%d" % (c, g, t), [P, HALF], 4 * c + t)
                 for a in range(2):
                     nc.tensor.matmul_mx(
                         out=bank[:],
@@ -203,7 +211,7 @@ def tile_list_kg_max_bias_kernel(
 
         def join(c, g, u, rounded):
             words, scales = wbq[g]
-            bank = hb_pool.tile([P, 4, UNIT], F32, name="hb")
+            bank = bank_at("hb_ps%d%d%d" % (c, g, u), [P, 4, UNIT], u if (c, g) == (0, 1) else 4 + u)
             for t in range(4):
                 nc.tensor.matmul_mx(
                     out=bank[:, t, :],
@@ -226,12 +234,15 @@ def tile_list_kg_max_bias_kernel(
         h = {}
         for c in range(2):
             for g in range(2):
-                h[c, g] = (held("h%d%d" % (c, g), [P, HALF], U32), held("h_sc%d%d" % (c, g), [P, HALF], U8))
+                words = at("h00", [P, HALF], U32, H00_AT) if (c, g) == (0, 0) else held("h%d%d" % (c, g), [P, HALF], U32)
+                h[c, g] = (words, held("h_sc%d%d" % (c, g), [P, HALF], U8))
         units_per_half = HALF // UNIT
         waiting = []
         for c, g, u in [(c, g, u) for c in range(2) for g in range(2) for u in range(units_per_half)]:
             second = u % 2
-            if second == 0:
+            if (c, g) == (1, 0) and second == 0:
+                rounded = at("h_bf10%d" % u, [P, 8 * UNIT], BF16, H_BF10_AT + u * KB)
+            elif second == 0:
                 rounded = held("h_bf%d%d%d" % (c, g, u), [P, 8 * UNIT], BF16)
             join(c, g, u, rounded[:, 4 * UNIT * second : 4 * UNIT * (second + 1)])
             if second == 0 and waiting:
@@ -240,9 +251,10 @@ def tile_list_kg_max_bias_kernel(
                 words, scales = h[c, g]
                 cols = slice(UNIT * (u - 1), UNIT * (u + 1))
                 waiting.append(dict(out=words[:, cols].bitcast(FP8X4), scales=scales[:, cols], in_=rounded[:]))
+            if g == 1 and u == units_per_half - 1:
+                nc.vector.quantize_mx(**waiting.pop())
             if (c, g, u) == (0, 0, units_per_half - 1):
                 project_a(1, 1)
-        nc.vector.quantize_mx(**waiting.pop())
 
         out_tiles = out.rearrange("(nt p) j -> p nt j", p=P)
 
@@ -260,7 +272,7 @@ def tile_list_kg_max_bias_kernel(
 
         for c in range(2):
             for nt in range(N // P):
-                bank = acc_pool.tile([P, HALF], F32, name="acc")
+                bank = bank_at("y_ps%d%d" % (c, nt), [P, HALF], nt % (4 * (c + 1)))
                 y_pass(bank, c, 0, nt)
                 y_pass(bank, c, 1, nt)
                 second = nt % 2

@@ -37,6 +37,7 @@ WB_RAW1_AT, BIAS_AT, EN_AT = 32 * KB, 40 * KB, 41 * KB
 TAB2_SC_WIN_AT = 38 * KB
 WB_BF0_AT = 56 * KB
 EN_SC_AT = 56 * KB
+HA00_AT = 60 * KB
 WB_BF1_AT = 60 * KB
 H00_AT = 60 * KB
 HA01_AT = 48 * KB
@@ -146,17 +147,20 @@ def tile_list_kg_max_bias_kernel(
             nc.vector.tensor_copy(words[:], tab2_win[:].indirect(list_half(idx2, c)))
             return words
 
-        def round_wb(g, copy, rounded):
+        def round_wb(g, first, count, copy, rounded):
             copy(
-                rounded[:].rearrange("p (t m i) -> p m t i", t=4, i=4),
-                wb_raw[g][:].rearrange("p i (m t) -> p m t i", t=4),
+                rounded[:].rearrange("p (t m i) -> p m t i", t=count, i=4),
+                wb_raw[g][:].rearrange("p i (m t) -> p m t i", t=4)[:, :, first : first + count, :],
             )
             return rounded
 
-        def quantise_wb(g, rounded):
+        def quantise_wb(g, parts):
             words = held("wb%d" % g, [P, PASS], U32)
             scales = held("wb_sc%d" % g, [P, PASS], U8)
-            nc.vector.quantize_mx(out=words[:].bitcast(FP8X4), scales=scales[:], in_=rounded[:])
+            width = PASS // len(parts)
+            for n, rounded in enumerate(parts):
+                cols = slice(width * n, width * (n + 1))
+                nc.vector.quantize_mx(out=words[:, cols].bitcast(FP8X4), scales=scales[:, cols], in_=rounded[:])
             return words, scales
 
         warm = bank_at("warm", [P, HALF], 7)
@@ -176,9 +180,9 @@ def tile_list_kg_max_bias_kernel(
         tab_g.append(gather_tab(1, at("tab_pairs1", [P, HALF], U32, TAB_PAIRS1_AT)))
         wa.append(order_wa_words(1))
 
-        wbq = [quantise_wb(0, round_wb(0, nc.vector.tensor_copy, at("wb_bf0", [P, 4 * PASS], BF16, WB_BF0_AT)))]
+        wbq = [quantise_wb(0, [round_wb(0, 0, 4, nc.vector.tensor_copy, at("wb_bf0", [P, 4 * PASS], BF16, WB_BF0_AT))])]
         tab2_g = [gather_tab2(c, held("tab2_g%d" % c, [P, HALF], U32)) for c in range(2)]
-        wbq.append(quantise_wb(1, round_wb(1, nc.scalar.copy, at("wb_bf1", [P, 4 * PASS], BF16, WB_BF1_AT))))
+        wb1_low = round_wb(1, 0, 2, nc.scalar.copy, held("wb_bf1_low", [P, 2 * PASS], BF16))
 
         en_sc = at("en_sc", [P, 2, N], U8, EN_SC_AT)
         nc.gpsimd.memset(en_sc[:].bitcast(I32), 0)
@@ -191,8 +195,8 @@ def tile_list_kg_max_bias_kernel(
         ha = {}
 
         def project_a(c, g):
-            if g == 1:
-                ha[c, g] = at("ha%d1" % c, [P, 4, HALF], F32, (HA01_AT, HA11_AT)[c])
+            if (c, g) != (1, 0):
+                ha[c, g] = at("ha%d%d" % (c, g), [P, 4, HALF], F32, {(0, 0): HA00_AT, (0, 1): HA01_AT, (1, 1): HA11_AT}[c, g])
             else:
                 ha[c, g] = held("ha%d%d" % (c, g), [P, 4, HALF], F32)
             for t in range(4):
@@ -232,29 +236,38 @@ def tile_list_kg_max_bias_kernel(
         for c, g in ((0, 0), (1, 0), (0, 1)):
             project_a(c, g)
         h = {}
+
+        def quantise_h(c, g, rounded, first, count):
+            words, scales = h[c, g]
+            cols = slice(UNIT * first, UNIT * (first + count))
+            nc.vector.quantize_mx(
+                out=words[:, cols].bitcast(FP8X4),
+                scales=scales[:, cols],
+                in_=rounded[:, 4 * UNIT * first : 4 * UNIT * (first + count)],
+            )
+
+        units = HALF // UNIT
         for c in range(2):
+            low = at("h_bf10", [P, 4 * HALF], BF16, H_BF10_AT) if c == 1 else held("h_bf00", [P, 4 * HALF], BF16)
+            for u in range(units):
+                join(c, 0, u, low[:, 4 * UNIT * u : 4 * UNIT * (u + 1)])
+            if c == 0:
+                wb1_high = round_wb(1, 2, 2, nc.vector.tensor_copy, at("wb_bf1_high", [P, 2 * PASS], BF16, WB_BF1_AT))
+                wbq.append(quantise_wb(1, [wb1_low, wb1_high]))
+                project_a(1, 1)
             for g in range(2):
                 words = at("h00", [P, HALF], U32, H00_AT) if (c, g) == (0, 0) else held("h%d%d" % (c, g), [P, HALF], U32)
                 h[c, g] = (words, held("h_sc%d%d" % (c, g), [P, HALF], U8))
-        units_per_half = HALF // UNIT
-        waiting = []
-        for c, g, u in [(c, g, u) for c in range(2) for g in range(2) for u in range(units_per_half)]:
-            second = u % 2
-            if (c, g) == (1, 0) and second == 0:
-                rounded = at("h_bf10%d" % u, [P, 8 * UNIT], BF16, H_BF10_AT + u * KB)
-            elif second == 0:
-                rounded = held("h_bf%d%d%d" % (c, g, u), [P, 8 * UNIT], BF16)
-            join(c, g, u, rounded[:, 4 * UNIT * second : 4 * UNIT * (second + 1)])
-            if second == 0 and waiting:
-                nc.vector.quantize_mx(**waiting.pop())
-            if second == 1:
-                words, scales = h[c, g]
-                cols = slice(UNIT * (u - 1), UNIT * (u + 1))
-                waiting.append(dict(out=words[:, cols].bitcast(FP8X4), scales=scales[:, cols], in_=rounded[:]))
-            if g == 1 and u == units_per_half - 1:
-                nc.vector.quantize_mx(**waiting.pop())
-            if (c, g, u) == (0, 0, units_per_half - 1):
-                project_a(1, 1)
+            high = held("h_bf%d1" % c, [P, 4 * HALF], BF16)
+            if c == 0:
+                quantise_h(c, 0, low, 0, units)
+            for u in range(units):
+                join(c, 1, u, high[:, 4 * UNIT * u : 4 * UNIT * (u + 1)])
+                if c == 1 and u == 0:
+                    quantise_h(c, 0, low, 0, units)
+                if u == 2:
+                    quantise_h(c, 1, high, 0, 2)
+            quantise_h(c, 1, high, 2, 2)
 
         out_tiles = out.rearrange("(nt p) j -> p nt j", p=P)
 

@@ -22,11 +22,12 @@ HALF = 512
 UNIT = 128
 KB = 1024
 BANK = 2 * KB
+SCALAR_SHARE = 96
 WARM_UP = 2
-STORES = 8
 
 ROWS_AT = 96
-TAB2_ROWS_AT = 112
+TAB2_ROWS_AT = 48
+TAB2_PLANE_AT = 4
 
 TAB2_WIN_AT, WB_RAW0_AT = 0, 16 * KB
 TAB_SC_WIN_AT = 14 * KB
@@ -37,9 +38,6 @@ WB_RAW1_AT, BIAS_AT, EN_AT = 32 * KB, 40 * KB, 41 * KB
 TAB2_SC_WIN_AT = 38 * KB
 WB_BF0_AT = 56 * KB
 EN_SC_AT = 56 * KB
-HA00_AT = 60 * KB
-WB_BF1_AT = 60 * KB
-H00_AT = 60 * KB
 HA01_AT = 48 * KB
 HA11_AT = 32 * KB
 H_BF10_AT = 48 * KB
@@ -53,7 +51,6 @@ def tile_list_kg_max_bias_kernel(
         lists = ctx.enter_context(tc.tile_pool(name="lists", bufs=1))
         keep = ctx.enter_context(tc.tile_pool(name="keep", bufs=1))
         placed = ctx.enter_context(tc.tile_pool(name="placed", bufs=1))
-        stage = ctx.enter_context(tc.tile_pool(name="stage", bufs=STORES))
         psum = ctx.enter_context(tc.psum_pool(name="psum", bufs=1))
 
         def held(name, shape, dtype):
@@ -82,16 +79,17 @@ def tile_list_kg_max_bias_kernel(
         tab2_sc = held("tab2_sc", [P, J], U8)
         nc.gpsimd.memset(wa_sc[:].bitcast(I32), 0)
         nc.gpsimd.memset(tab_sc[:].bitcast(I32), 0)
-        nc.gpsimd.memset(tab2_sc_win[0:TAB2_ROWS_AT, :].bitcast(I32), 0)
+        nc.vector.memset(tab2_sc_win[0:TAB2_ROWS_AT, :].bitcast(I32), 0)
+        nc.gpsimd.memset(tab2_sc_win[TAB2_ROWS_AT + 16 : P, :].bitcast(I32), 0)
         nc.gpsimd.memset(tab2_sc[:].bitcast(I32), 0)
 
         tab_win = held("tab_win", [P, T], U32)
         nc.sync.dma_start(tab_win[:].bitcast(I32), tab_words[0].rearrange("p t i -> p (t i)").bitcast(I32))
 
-        def deal_rows(plane, rows, first, count):
+        def deal_rows(plane, rows, first, count, up=0):
             for quadrant in range(4):
                 nc.sync.dma_start(
-                    plane[32 * quadrant : 32 * quadrant + 4].bitcast(I32),
+                    plane[32 * quadrant + up : 32 * quadrant + up + 4].bitcast(I32),
                     rows[first + count * quadrant : first + count * (quadrant + 1), :].bitcast(I32),
                 )
 
@@ -116,7 +114,7 @@ def tile_list_kg_max_bias_kernel(
 
         tab2_sc_g = held("tab2_sc_g", [P, J], U8)
         nc.vector.tensor_copy(tab2_sc_g[:], tab2_sc_win[:].indirect(idx2[:]))
-        deal_rows(tab2_sc, tab2_sc_g, TAB2_ROWS_AT, 4)
+        deal_rows(tab2_sc, tab2_sc_g, TAB2_ROWS_AT, 4, TAB2_PLANE_AT)
         wb_raw.append(at("wb_raw1", [P, 4, PASS], F32, WB_RAW1_AT))
         nc.sync.dma_start(wb_raw[1][:], wb_hbm[:, :, PASS : 2 * PASS])
 
@@ -147,20 +145,16 @@ def tile_list_kg_max_bias_kernel(
             nc.vector.tensor_copy(words[:], tab2_win[:].indirect(list_half(idx2, c)))
             return words
 
-        def round_wb(g, first, count, copy, rounded):
+        def round_wb(g, first, last, copy, rounded):
             copy(
-                rounded[:].rearrange("p (t m i) -> p m t i", t=count, i=4),
-                wb_raw[g][:].rearrange("p i (m t) -> p m t i", t=4)[:, :, first : first + count, :],
+                rounded[:].rearrange("p (t m i) -> p m t i", t=4, i=4)[:, first:last],
+                wb_raw[g][:].rearrange("p i (m t) -> p m t i", t=4)[:, first:last],
             )
-            return rounded
 
-        def quantise_wb(g, parts):
+        def quantise_wb(g, rounded):
             words = held("wb%d" % g, [P, PASS], U32)
             scales = held("wb_sc%d" % g, [P, PASS], U8)
-            width = PASS // len(parts)
-            for n, rounded in enumerate(parts):
-                cols = slice(width * n, width * (n + 1))
-                nc.vector.quantize_mx(out=words[:, cols].bitcast(FP8X4), scales=scales[:, cols], in_=rounded[:])
+            nc.vector.quantize_mx(out=words[:].bitcast(FP8X4), scales=scales[:], in_=rounded[:])
             return words, scales
 
         warm = bank_at("warm", [P, HALF], 7)
@@ -180,9 +174,11 @@ def tile_list_kg_max_bias_kernel(
         tab_g.append(gather_tab(1, at("tab_pairs1", [P, HALF], U32, TAB_PAIRS1_AT)))
         wa.append(order_wa_words(1))
 
-        wbq = [quantise_wb(0, [round_wb(0, 0, 4, nc.vector.tensor_copy, at("wb_bf0", [P, 4 * PASS], BF16, WB_BF0_AT))])]
+        wb_bf = [at("wb_bf0", [P, 4 * PASS], BF16, WB_BF0_AT), held("wb_bf1", [P, 4 * PASS], BF16)]
+        round_wb(0, 0, P, nc.vector.tensor_copy, wb_bf[0])
+        wbq = [quantise_wb(0, wb_bf[0])]
         tab2_g = [gather_tab2(c, held("tab2_g%d" % c, [P, HALF], U32)) for c in range(2)]
-        wb1_low = round_wb(1, 0, 2, nc.scalar.copy, held("wb_bf1_low", [P, 2 * PASS], BF16))
+        round_wb(1, 0, SCALAR_SHARE, nc.scalar.copy, wb_bf[1])
 
         en_sc = at("en_sc", [P, 2, N], U8, EN_SC_AT)
         nc.gpsimd.memset(en_sc[:].bitcast(I32), 0)
@@ -195,8 +191,8 @@ def tile_list_kg_max_bias_kernel(
         ha = {}
 
         def project_a(c, g):
-            if (c, g) != (1, 0):
-                ha[c, g] = at("ha%d%d" % (c, g), [P, 4, HALF], F32, {(0, 0): HA00_AT, (0, 1): HA01_AT, (1, 1): HA11_AT}[c, g])
+            if g == 1:
+                ha[c, g] = at("ha%d1" % c, [P, 4, HALF], F32, (HA01_AT, HA11_AT)[c])
             else:
                 ha[c, g] = held("ha%d%d" % (c, g), [P, 4, HALF], F32)
             for t in range(4):
@@ -222,7 +218,7 @@ def tile_list_kg_max_bias_kernel(
                     lhsT=words[:, P * t : P * (t + 1)].bitcast(FP8X4),
                     lhsT_scale=scales[:, P * t : P * (t + 1)],
                     rhs=tab2_g[c][:, UNIT * u : UNIT * (u + 1)].bitcast(FP8X4),
-                    rhs_scale=tab2_sc[:, HALF * c + UNIT * u : HALF * c + UNIT * (u + 1)],
+                    rhs_scale=tab2_sc[TAB2_PLANE_AT:P, HALF * c + UNIT * u : HALF * c + UNIT * (u + 1)],
                     start=True,
                     stop=True,
                 )
@@ -251,22 +247,20 @@ def tile_list_kg_max_bias_kernel(
             low = at("h_bf10", [P, 4 * HALF], BF16, H_BF10_AT) if c == 1 else held("h_bf00", [P, 4 * HALF], BF16)
             for u in range(units):
                 join(c, 0, u, low[:, 4 * UNIT * u : 4 * UNIT * (u + 1)])
-            if c == 0:
-                wb1_high = round_wb(1, 2, 2, nc.vector.tensor_copy, at("wb_bf1_high", [P, 2 * PASS], BF16, WB_BF1_AT))
-                wbq.append(quantise_wb(1, [wb1_low, wb1_high]))
-                project_a(1, 1)
             for g in range(2):
-                words = at("h00", [P, HALF], U32, H00_AT) if (c, g) == (0, 0) else held("h%d%d" % (c, g), [P, HALF], U32)
-                h[c, g] = (words, held("h_sc%d%d" % (c, g), [P, HALF], U8))
+                h[c, g] = (held("h%d%d" % (c, g), [P, HALF], U32), held("h_sc%d%d" % (c, g), [P, HALF], U8))
             high = held("h_bf%d1" % c, [P, 4 * HALF], BF16)
             if c == 0:
-                quantise_h(c, 0, low, 0, units)
+                round_wb(1, SCALAR_SHARE, P, nc.vector.tensor_copy, wb_bf[1])
+                quantise_h(c, 0, low, 0, 2)
+                wbq.append(quantise_wb(1, wb_bf[1]))
+                quantise_h(c, 0, low, 2, 2)
+                project_a(1, 1)
             for u in range(units):
                 join(c, 1, u, high[:, 4 * UNIT * u : 4 * UNIT * (u + 1)])
                 if c == 1 and u == 0:
                     quantise_h(c, 0, low, 0, units)
-                if u == 2:
-                    quantise_h(c, 1, high, 0, 2)
+            quantise_h(c, 1, high, 0, 2)
             quantise_h(c, 1, high, 2, 2)
 
         out_tiles = out.rearrange("(nt p) j -> p nt j", p=P)
@@ -284,16 +278,15 @@ def tile_list_kg_max_bias_kernel(
             )
 
         for c in range(2):
-            for nt in range(N // P):
-                bank = bank_at("y_ps%d%d" % (c, nt), [P, HALF], nt % (4 * (c + 1)))
-                y_pass(bank, c, 0, nt)
-                y_pass(bank, c, 1, nt)
-                second = nt % 2
-                if second == 0:
-                    scores = stage.tile([P, 2, HALF], F32, name="scores")
-                if c == 1 and second == 1:
-                    nc.vector.tensor_scalar_add(scores[:, second, :], bank[:], bias[:, nt : nt + 1])
-                else:
-                    nc.scalar.activation(scores[:, second, :], bank[:], IDENTITY, bias=bias[:, nt : nt + 1])
-                if second == 1:
-                    nc.sync.dma_start(out_tiles[:, nt - 1 : nt + 1, HALF * c : HALF * (c + 1)], scores[:])
+            groups = ((0, 1), (2, 3), (4, 5), (6, 7)) if c == 0 else ((0,), (1,), (2, 3), (4, 5), (6,), (7,))
+            for group in groups:
+                scores = held("scores%d%d" % (c, group[0]), [P, len(group), HALF], F32)
+                for n, nt in enumerate(group):
+                    bank = bank_at("y_ps%d%d" % (c, nt), [P, HALF], nt % (4 * (c + 1)))
+                    y_pass(bank, c, 0, nt)
+                    y_pass(bank, c, 1, nt)
+                    if c == 1 and nt % 2 == 1:
+                        nc.vector.tensor_scalar_add(scores[:, n, :], bank[:], bias[:, nt : nt + 1])
+                    else:
+                        nc.scalar.activation(scores[:, n, :], bank[:], IDENTITY, bias=bias[:, nt : nt + 1])
+                nc.sync.dma_start(out_tiles[:, group[0] : group[-1] + 1, HALF * c : HALF * (c + 1)], scores[:])

@@ -14,6 +14,8 @@ U8 = mybir.dt.uint8
 FP8X4 = mybir.dt.float8_e4m3fn_x4
 FP4X4 = mybir.dt.float4_e2m1fn_x4
 MAX = mybir.AluOpType.max
+MULT = mybir.AluOpType.mult
+ADD = mybir.AluOpType.add
 IDENTITY = mybir.ActivationFunctionType.Identity
 
 P = 128
@@ -22,22 +24,23 @@ HALF = 512
 UNIT = 128
 KB = 1024
 BANK = 2 * KB
-SCALAR_SHARE = 96
+SCALAR_SHARE = 80
 WARM_UP = 2
 
 ROWS_AT = 96
 TAB2_ROWS_AT = 48
 TAB2_PLANE_AT = 4
 
-TAB2_WIN_AT, WB_RAW0_AT = 0, 16 * KB
-TAB_SC_WIN_AT = 14 * KB
-WA_RAW0_AT, WA_RAW1_AT = 24 * KB, 28 * KB
-WA_SC_RAW_AT = 28 * KB - 512
-TAB_PAIRS1_AT = 24 * KB
-WB_RAW1_AT, BIAS_AT, EN_AT = 32 * KB, 40 * KB, 41 * KB
-TAB2_SC_WIN_AT = 38 * KB
-WB_BF0_AT = 56 * KB
-EN_SC_AT = 56 * KB
+TAB_SC_WIN_AT = 15 * KB
+TAB2_WIN_AT, TAB_SC_AT, WB_RAW0_AT = 0, 16 * KB, 18 * KB
+WA_RAW0_AT, WA_RAW1_AT = 64 * KB, 68 * KB
+WA_SC_RAW_AT = 68 * KB - 512
+TAB_PAIRS1_AT = 64 * KB
+TAB2_SC_WIN_AT = 39 * KB
+WB_RAW1_AT, TAB2_SC_AT, BIAS_AT, EN_AT = 32 * KB, 40 * KB, 41 * KB, 42 * KB
+EN_SC_AT = 68 * KB
+WB_BF1_AT = 56 * KB
+H00_AT = 56 * KB
 HA01_AT = 48 * KB
 HA11_AT = 32 * KB
 H_BF10_AT = 48 * KB
@@ -74,14 +77,12 @@ def tile_list_kg_max_bias_kernel(
         nc.sync.dma_start(tab2_sc_win[TAB2_ROWS_AT : TAB2_ROWS_AT + 16, :].bitcast(I32), tab2_scales[0].bitcast(I32))
         nc.vector.memset(wa_sc_raw[0:ROWS_AT, :].bitcast(I32), 0)
         nc.vector.memset(tab_sc_win[0:ROWS_AT, :].bitcast(I32), 0)
-        tab_sc = held("tab_sc", [P, 2, J], U8)
+        tab_sc = at("tab_sc", [P, 2, J], U8, TAB_SC_AT)
         wa_sc = held("wa_sc", [P, 2, R], U8)
-        tab2_sc = held("tab2_sc", [P, J], U8)
+        tab2_sc = at("tab2_sc", [P, J], U8, TAB2_SC_AT)
         nc.gpsimd.memset(wa_sc[:].bitcast(I32), 0)
-        nc.gpsimd.memset(tab_sc[:].bitcast(I32), 0)
-        nc.vector.memset(tab2_sc_win[0:TAB2_ROWS_AT, :].bitcast(I32), 0)
+        nc.gpsimd.memset(tab2_sc_win[0:TAB2_ROWS_AT, :].bitcast(I32), 0)
         nc.gpsimd.memset(tab2_sc_win[TAB2_ROWS_AT + 16 : P, :].bitcast(I32), 0)
-        nc.gpsimd.memset(tab2_sc[:].bitcast(I32), 0)
 
         tab_win = held("tab_win", [P, T], U32)
         nc.sync.dma_start(tab_win[:].bitcast(I32), tab_words[0].rearrange("p t i -> p (t i)").bitcast(I32))
@@ -135,10 +136,11 @@ def tile_list_kg_max_bias_kernel(
 
         def order_wa_words(g):
             words = held("wa%d" % g, [P, 2, PASS], I32)
-            nc.vector.tensor_copy(
-                words[:].rearrange("p a (t m i) -> p a m t i", t=4, i=4),
-                wa_raw[g][:].rearrange("p a (m i t) -> p a m t i", t=4, i=4),
-            )
+            for passes in (slice(0, 1), slice(1, 2)) if g == 0 else (slice(0, 2),):
+                nc.vector.tensor_copy(
+                    words[:, passes, :].rearrange("p a (t m i) -> p a m t i", t=4, i=4),
+                    wa_raw[g][:, passes, :].rearrange("p a (m i t) -> p a m t i", t=4, i=4),
+                )
             return words
 
         def gather_tab2(c, words):
@@ -174,14 +176,14 @@ def tile_list_kg_max_bias_kernel(
         tab_g.append(gather_tab(1, at("tab_pairs1", [P, HALF], U32, TAB_PAIRS1_AT)))
         wa.append(order_wa_words(1))
 
-        wb_bf = [at("wb_bf0", [P, 4 * PASS], BF16, WB_BF0_AT), held("wb_bf1", [P, 4 * PASS], BF16)]
+        wb_bf = [held("wb_bf0", [P, 4 * PASS], BF16), at("wb_bf1", [P, 4 * PASS], BF16, WB_BF1_AT)]
         round_wb(0, 0, P, nc.vector.tensor_copy, wb_bf[0])
         wbq = [quantise_wb(0, wb_bf[0])]
         tab2_g = [gather_tab2(c, held("tab2_g%d" % c, [P, HALF], U32)) for c in range(2)]
         round_wb(1, 0, SCALAR_SHARE, nc.scalar.copy, wb_bf[1])
+        round_wb(1, SCALAR_SHARE, P, lambda dst, src: nc.gpsimd.tensor_scalar(dst, src, 1.0, 0.0, MULT, ADD), wb_bf[1])
 
         en_sc = at("en_sc", [P, 2, N], U8, EN_SC_AT)
-        nc.gpsimd.memset(en_sc[:].bitcast(I32), 0)
         for quadrant in range(4):
             nc.sync.dma_start(
                 en_sc[32 * quadrant : 32 * quadrant + 4, :, :].bitcast(I32),
@@ -248,13 +250,12 @@ def tile_list_kg_max_bias_kernel(
             for u in range(units):
                 join(c, 0, u, low[:, 4 * UNIT * u : 4 * UNIT * (u + 1)])
             for g in range(2):
-                h[c, g] = (held("h%d%d" % (c, g), [P, HALF], U32), held("h_sc%d%d" % (c, g), [P, HALF], U8))
+                words = at("h00", [P, HALF], U32, H00_AT) if (c, g) == (0, 0) else held("h%d%d" % (c, g), [P, HALF], U32)
+                h[c, g] = (words, held("h_sc%d%d" % (c, g), [P, HALF], U8))
             high = held("h_bf%d1" % c, [P, 4 * HALF], BF16)
             if c == 0:
-                round_wb(1, SCALAR_SHARE, P, nc.vector.tensor_copy, wb_bf[1])
-                quantise_h(c, 0, low, 0, 2)
                 wbq.append(quantise_wb(1, wb_bf[1]))
-                quantise_h(c, 0, low, 2, 2)
+                quantise_h(c, 0, low, 0, units)
                 project_a(1, 1)
             for u in range(units):
                 join(c, 1, u, high[:, 4 * UNIT * u : 4 * UNIT * (u + 1)])
@@ -278,14 +279,14 @@ def tile_list_kg_max_bias_kernel(
             )
 
         for c in range(2):
-            groups = ((0, 1), (2, 3), (4, 5), (6, 7)) if c == 0 else ((0,), (1,), (2, 3), (4, 5), (6,), (7,))
+            groups = [(nt,) for nt in range(N // P)]
             for group in groups:
                 scores = held("scores%d%d" % (c, group[0]), [P, len(group), HALF], F32)
                 for n, nt in enumerate(group):
                     bank = bank_at("y_ps%d%d" % (c, nt), [P, HALF], nt % (4 * (c + 1)))
                     y_pass(bank, c, 0, nt)
                     y_pass(bank, c, 1, nt)
-                    if c == 1 and nt % 2 == 1:
+                    if c == 1 and nt % 2 == 0:
                         nc.vector.tensor_scalar_add(scores[:, n, :], bank[:], bias[:, nt : nt + 1])
                     else:
                         nc.scalar.activation(scores[:, n, :], bank[:], IDENTITY, bias=bias[:, nt : nt + 1])

@@ -35,12 +35,16 @@ TAB_SC_WIN_AT = 15 * KB
 TAB2_WIN_AT, TAB_SC_AT, WB_RAW0_AT = 0, 16 * KB, 18 * KB
 WA_RAW0_AT, WA_RAW1_AT = 64 * KB, 68 * KB
 WA_SC_RAW_AT = 68 * KB - 512
-TAB_PAIRS1_AT = 64 * KB
+TAB_PAIRS0_AT = 64 * KB
 TAB2_SC_WIN_AT = 39 * KB
 WB_RAW1_AT, TAB2_SC_AT, BIAS_AT, EN_AT = 32 * KB, 40 * KB, 41 * KB, 42 * KB
 EN_SC_AT = 68 * KB
 WB_BF1_AT = 56 * KB
 H00_AT = 56 * KB
+WB_BF0_AT = 72 * KB
+HA10_WOVEN_AT = 72 * KB
+HA10_AT = 60 * KB
+TAB2_G0_AT = 60 * KB
 HA01_AT = 48 * KB
 HA11_AT = 32 * KB
 H_BF10_AT = 48 * KB
@@ -171,17 +175,14 @@ def tile_list_kg_max_bias_kernel(
                 stop=True,
             )
 
-        tab_g = [gather_tab(0, held("tab_pairs0", [P, HALF], U32))]
+        tab_g = {1: gather_tab(1, held("tab_pairs1", [P, HALF], U32))}
         wa = [order_wa_words(0)]
-        tab_g.append(gather_tab(1, at("tab_pairs1", [P, HALF], U32, TAB_PAIRS1_AT)))
+        tab_g[0] = gather_tab(0, at("tab_pairs0", [P, HALF], U32, TAB_PAIRS0_AT))
         wa.append(order_wa_words(1))
 
-        wb_bf = [held("wb_bf0", [P, 4 * PASS], BF16), at("wb_bf1", [P, 4 * PASS], BF16, WB_BF1_AT)]
+        wb_bf = [at("wb_bf0", [P, 4 * PASS], BF16, WB_BF0_AT), at("wb_bf1", [P, 4 * PASS], BF16, WB_BF1_AT)]
         round_wb(0, 0, P, nc.vector.tensor_copy, wb_bf[0])
         wbq = [quantise_wb(0, wb_bf[0])]
-        tab2_g = [gather_tab2(c, held("tab2_g%d" % c, [P, HALF], U32)) for c in range(2)]
-        round_wb(1, 0, SCALAR_SHARE, nc.scalar.copy, wb_bf[1])
-        round_wb(1, SCALAR_SHARE, P, lambda dst, src: nc.gpsimd.tensor_scalar(dst, src, 1.0, 0.0, MULT, ADD), wb_bf[1])
 
         en_sc = at("en_sc", [P, 2, N], U8, EN_SC_AT)
         for quadrant in range(4):
@@ -196,9 +197,9 @@ def tile_list_kg_max_bias_kernel(
             if g == 1:
                 ha[c, g] = at("ha%d1" % c, [P, 4, HALF], F32, (HA01_AT, HA11_AT)[c])
             else:
-                ha[c, g] = held("ha%d%d" % (c, g), [P, 4, HALF], F32)
+                ha[c, g] = at("ha10", [P, 4, HALF], BF16, HA10_AT) if c == 1 else held("ha00", [P, 4, HALF], F32)
             for t in range(4):
-                bank = bank_at("ha_ps%d%d%d" % (c, g, t), [P, HALF], 4 * c + t)
+                bank = bank_at("ha_ps%d%d%d" % (c, g, t), [P, HALF], 4 * (c == g) + t)
                 for a in range(2):
                     nc.tensor.matmul_mx(
                         out=bank[:],
@@ -211,7 +212,7 @@ def tile_list_kg_max_bias_kernel(
                     )
                 nc.scalar.copy(ha[c, g][:, t, :], bank[:])
 
-        def join(c, g, u, rounded):
+        def project_b(c, g, u):
             words, scales = wbq[g]
             bank = bank_at("hb_ps%d%d%d" % (c, g, u), [P, 4, UNIT], u if (c, g) == (0, 1) else 4 + u)
             for t in range(4):
@@ -224,15 +225,29 @@ def tile_list_kg_max_bias_kernel(
                     start=True,
                     stop=True,
                 )
+            return bank[:].rearrange("p t (j i) -> p j t i", i=2)
+
+        def join(c, g, u, rounded):
             nc.vector.tensor_tensor(
                 rounded.rearrange("p (j i t) -> p j t i", t=4, i=2),
-                bank[:].rearrange("p t (j i) -> p j t i", i=2),
+                project_b(c, g, u),
                 ha[c, g][:, :, UNIT * u : UNIT * (u + 1)].rearrange("p t (j i) -> p j t i", i=2),
                 MAX,
             )
 
-        for c, g in ((0, 0), (1, 0), (0, 1)):
+        for c, g in ((1, 0), (0, 0), (0, 1)):
             project_a(c, g)
+        ha10_woven = at("ha10_woven", [P, 4 * HALF], BF16, HA10_WOVEN_AT)
+        nc.vector.tensor_copy(
+            ha10_woven[:].rearrange("p (j i t) -> p j t i", t=4, i=4), ha[1, 0][:].rearrange("p t (j i) -> p j t i", i=4)
+        )
+        tab2_g = [
+            gather_tab2(0, at("tab2_g0", [P, HALF], U32, TAB2_G0_AT)),
+            gather_tab2(1, held("tab2_g1", [P, HALF], U32)),
+        ]
+        round_wb(1, 0, SCALAR_SHARE, nc.scalar.copy, wb_bf[1])
+        round_wb(1, SCALAR_SHARE, P, lambda dst, src: nc.gpsimd.tensor_scalar(dst, src, 1.0, 0.0, MULT, ADD), wb_bf[1])
+
         h = {}
 
         def quantise_h(c, g, rounded, first, count):
@@ -247,8 +262,11 @@ def tile_list_kg_max_bias_kernel(
         units = HALF // UNIT
         for c in range(2):
             low = at("h_bf10", [P, 4 * HALF], BF16, H_BF10_AT) if c == 1 else held("h_bf00", [P, 4 * HALF], BF16)
-            for u in range(units):
-                join(c, 0, u, low[:, 4 * UNIT * u : 4 * UNIT * (u + 1)])
+            if c == 0:
+                for u in range(units):
+                    join(c, 0, u, low[:, 4 * UNIT * u : 4 * UNIT * (u + 1)])
+            else:
+                nc.vector.tensor_tensor(low[:], hb10_woven[:], ha10_woven[:], MAX)
             for g in range(2):
                 words = at("h00", [P, HALF], U32, H00_AT) if (c, g) == (0, 0) else held("h%d%d" % (c, g), [P, HALF], U32)
                 h[c, g] = (words, held("h_sc%d%d" % (c, g), [P, HALF], U8))
@@ -257,12 +275,17 @@ def tile_list_kg_max_bias_kernel(
                 wbq.append(quantise_wb(1, wb_bf[1]))
                 quantise_h(c, 0, low, 0, units)
                 project_a(1, 1)
+                hb10_woven = held("hb10_woven", [P, 4 * HALF], BF16)
             for u in range(units):
                 join(c, 1, u, high[:, 4 * UNIT * u : 4 * UNIT * (u + 1)])
                 if c == 1 and u == 0:
                     quantise_h(c, 0, low, 0, units)
             quantise_h(c, 1, high, 0, 2)
             quantise_h(c, 1, high, 2, 2)
+            if c == 0:
+                for u in range(units):
+                    part = hb10_woven[:, 4 * UNIT * u : 4 * UNIT * (u + 1)]
+                    nc.scalar.copy(part.rearrange("p (j i t) -> p j t i", t=4, i=2), project_b(1, 0, u))
 
         out_tiles = out.rearrange("(nt p) j -> p nt j", p=P)
 
@@ -283,7 +306,7 @@ def tile_list_kg_max_bias_kernel(
             for group in groups:
                 scores = held("scores%d%d" % (c, group[0]), [P, len(group), HALF], F32)
                 for n, nt in enumerate(group):
-                    bank = bank_at("y_ps%d%d" % (c, nt), [P, HALF], nt % (4 * (c + 1)))
+                    bank = bank_at("y_ps%d%d" % (c, nt), [P, HALF], (nt + 4 * c) % (4 * (c + 1)))
                     y_pass(bank, c, 0, nt)
                     y_pass(bank, c, 1, nt)
                     if c == 1 and nt % 2 == 0:

@@ -24,7 +24,7 @@ HALF = 512
 UNIT = 128
 KB = 1024
 BANK = 2 * KB
-SCALAR_SHARE = 80
+SCALAR_SHARE = 104
 WARM_UP = 2
 
 ROWS_AT = 96
@@ -120,8 +120,9 @@ def tile_list_kg_max_bias_kernel(
         tab2_sc_g = held("tab2_sc_g", [P, J], U8)
         nc.vector.tensor_copy(tab2_sc_g[:], tab2_sc_win[:].indirect(idx2[:]))
         deal_rows(tab2_sc, tab2_sc_g, TAB2_ROWS_AT, 4, TAB2_PLANE_AT)
-        wb_raw.append(at("wb_raw1", [P, 4, PASS], F32, WB_RAW1_AT))
-        nc.sync.dma_start(wb_raw[1][:], wb_hbm[:, :, PASS : 2 * PASS])
+        wb_raw1 = at("wb_raw1", [P, 2, 4, PASS // 2], F32, WB_RAW1_AT)
+        for part in range(2):
+            nc.sync.dma_start(wb_raw1[:, part], wb_hbm[:, :, PASS + part * PASS // 2 : PASS + (part + 1) * PASS // 2])
 
         en = at("en", [P, 2, 2 * N], U8, EN_AT)
         nc.sync.dma_start(en[:].bitcast(I32), en_words.rearrange("g p x -> p g x").bitcast(I32))
@@ -151,10 +152,10 @@ def tile_list_kg_max_bias_kernel(
             nc.vector.tensor_copy(words[:], tab2_win[:].indirect(list_half(idx2, c)))
             return words
 
-        def round_wb(g, first, last, copy, rounded):
+        def round_wb(raw, raw_first, first, last, copy, rounded):
             copy(
                 rounded[:].rearrange("p (t m i) -> p m t i", t=4, i=4)[:, first:last],
-                wb_raw[g][:].rearrange("p i (m t) -> p m t i", t=4)[:, first:last],
+                raw.rearrange("p i (m t) -> p m t i", t=4)[:, first - raw_first : last - raw_first],
             )
 
         def quantise_wb(g, rounded):
@@ -181,7 +182,7 @@ def tile_list_kg_max_bias_kernel(
         wa.append(order_wa_words(1))
 
         wb_bf = [at("wb_bf0", [P, 4 * PASS], BF16, WB_BF0_AT), at("wb_bf1", [P, 4 * PASS], BF16, WB_BF1_AT)]
-        round_wb(0, 0, P, nc.vector.tensor_copy, wb_bf[0])
+        round_wb(wb_raw[0][:], 0, 0, P, nc.vector.tensor_copy, wb_bf[0])
         wbq = [quantise_wb(0, wb_bf[0])]
 
         en_sc = at("en_sc", [P, 2, N], U8, EN_SC_AT)
@@ -245,8 +246,9 @@ def tile_list_kg_max_bias_kernel(
             gather_tab2(0, at("tab2_g0", [P, HALF], U32, TAB2_G0_AT)),
             gather_tab2(1, held("tab2_g1", [P, HALF], U32)),
         ]
-        round_wb(1, 0, SCALAR_SHARE, nc.scalar.copy, wb_bf[1])
-        round_wb(1, SCALAR_SHARE, P, lambda dst, src: nc.gpsimd.tensor_scalar(dst, src, 1.0, 0.0, MULT, ADD), wb_bf[1])
+        round_wb(wb_raw1[:, 0], 0, 0, P // 2, nc.scalar.copy, wb_bf[1])
+        round_wb(wb_raw1[:, 1], P // 2, P // 2, SCALAR_SHARE, nc.scalar.copy, wb_bf[1])
+        round_wb(wb_raw1[:, 1], P // 2, SCALAR_SHARE, P, lambda dst, src: nc.gpsimd.tensor_scalar(dst, src, 1.0, 0.0, MULT, ADD), wb_bf[1])
 
         h = {}
 

@@ -24,7 +24,6 @@ HALF = 512
 UNIT = 128
 KB = 1024
 BANK = 2 * KB
-SCALAR_SHARE = 104
 WARM_UP = 2
 
 ROWS_AT = 96
@@ -35,9 +34,10 @@ TAB_SC_WIN_AT = 15 * KB
 TAB2_WIN_AT, TAB_SC_AT, WB_RAW0_AT = 0, 16 * KB, 18 * KB
 WA_RAW0_AT, WA_RAW1_AT = 64 * KB, 68 * KB
 WA_SC_RAW_AT = 68 * KB - 512
-TAB_PAIRS0_AT = 64 * KB
+TAB_PAIRS0_AT = 84 * KB
 TAB2_SC_WIN_AT = 39 * KB
-WB_RAW1_AT, TAB2_SC_AT, BIAS_AT, EN_AT = 32 * KB, 40 * KB, 41 * KB, 42 * KB
+WB_RAW1_AT, TAB2_SC_AT, BIAS_AT, EN_AT = (35 * KB + 256, 80 * KB + 512), 40 * KB, 84 * KB + 512, 85 * KB
+HB00_WOVEN_AT = 37 * KB + 256
 EN_SC_AT = 68 * KB
 WB_BF1_AT = 56 * KB
 H00_AT = 56 * KB
@@ -46,7 +46,7 @@ HA10_WOVEN_AT = 72 * KB
 HA10_AT = 60 * KB
 TAB2_G0_AT = 60 * KB
 HA01_AT = 48 * KB
-HA11_AT = 32 * KB
+HA11_AT = 29 * KB + 256
 H_BF10_AT = 48 * KB
 
 
@@ -120,15 +120,8 @@ def tile_list_kg_max_bias_kernel(
         tab2_sc_g = held("tab2_sc_g", [P, J], U8)
         nc.vector.tensor_copy(tab2_sc_g[:], tab2_sc_win[:].indirect(idx2[:]))
         deal_rows(tab2_sc, tab2_sc_g, TAB2_ROWS_AT, 4, TAB2_PLANE_AT)
-        wb_raw1 = at("wb_raw1", [P, 2, 4, PASS // 2], F32, WB_RAW1_AT)
-        for part in range(2):
-            nc.sync.dma_start(wb_raw1[:, part], wb_hbm[:, :, PASS + part * PASS // 2 : PASS + (part + 1) * PASS // 2])
-
-        en = at("en", [P, 2, 2 * N], U8, EN_AT)
-        nc.sync.dma_start(en[:].bitcast(I32), en_words.rearrange("g p x -> p g x").bitcast(I32))
-        bias = at("bias", [P, N // P], F32, BIAS_AT)
-        with nc.allow_non_contiguous_dma(reason="one bias value for each partition and tile of candidates"):
-            nc.sync.dma_start(bias[:], b.rearrange("(nt p) -> p nt", p=P))
+        wb_raw1 = [at("wb_raw10", [P, 4, PASS // 2], F32, WB_RAW1_AT[0])]
+        nc.sync.dma_start(wb_raw1[0][:], wb_hbm[:, :, PASS : PASS + PASS // 2])
 
         def list_half(offsets, c):
             return offsets[:, c * HALF // 16 : (c + 1) * HALF // 16]
@@ -141,10 +134,16 @@ def tile_list_kg_max_bias_kernel(
 
         def order_wa_words(g):
             words = held("wa%d" % g, [P, 2, PASS], I32)
-            for passes in (slice(0, 1), slice(1, 2)) if g == 0 else (slice(0, 2),):
+            if g == 0:
+                for a in range(2):
+                    nc.scalar.copy(
+                        words[:, a, :].bitcast(U32).rearrange("p (t m i) -> p m t i", t=4, i=4),
+                        wa_raw[g][:, a, :].bitcast(U32).rearrange("p (m i t) -> p m t i", t=4, i=4),
+                    )
+            else:
                 nc.vector.tensor_copy(
-                    words[:, passes, :].rearrange("p a (t m i) -> p a m t i", t=4, i=4),
-                    wa_raw[g][:, passes, :].rearrange("p a (m i t) -> p a m t i", t=4, i=4),
+                    words[:].rearrange("p a (t m i) -> p a m t i", t=4, i=4),
+                    wa_raw[g][:].rearrange("p a (m i t) -> p a m t i", t=4, i=4),
                 )
             return words
 
@@ -176,10 +175,18 @@ def tile_list_kg_max_bias_kernel(
                 stop=True,
             )
 
-        tab_g = {1: gather_tab(1, held("tab_pairs1", [P, HALF], U32))}
+        tab_g = {1: gather_tab(1, at("tab_pairs1", [P, HALF], U32, TAB_PAIRS0_AT))}
         wa = [order_wa_words(0)]
         tab_g[0] = gather_tab(0, at("tab_pairs0", [P, HALF], U32, TAB_PAIRS0_AT))
         wa.append(order_wa_words(1))
+        wb_raw1.append(at("wb_raw11", [P, 4, PASS // 2], F32, WB_RAW1_AT[1]))
+        nc.sync.dma_start(wb_raw1[1][:], wb_hbm[:, :, PASS + PASS // 2 : R])
+
+        en = at("en", [P, 2, 2 * N], U8, EN_AT)
+        nc.sync.dma_start(en[:].bitcast(I32), en_words.rearrange("g p x -> p g x").bitcast(I32))
+        bias = at("bias", [P, N // P], F32, BIAS_AT)
+        with nc.allow_non_contiguous_dma(reason="one bias value for each partition and tile of candidates"):
+            nc.sync.dma_start(bias[:], b.rearrange("(nt p) -> p nt", p=P))
 
         wb_bf = [at("wb_bf0", [P, 4 * PASS], BF16, WB_BF0_AT), at("wb_bf1", [P, 4 * PASS], BF16, WB_BF1_AT)]
         round_wb(wb_raw[0][:], 0, 0, P, nc.vector.tensor_copy, wb_bf[0])
@@ -194,12 +201,14 @@ def tile_list_kg_max_bias_kernel(
 
         ha = {}
 
-        def project_a(c, g):
-            if g == 1:
+        def project_a(c, g, slices=range(4)):
+            if (c, g) in ha:
+                pass
+            elif g == 1:
                 ha[c, g] = at("ha%d1" % c, [P, 4, HALF], F32, (HA01_AT, HA11_AT)[c])
             else:
                 ha[c, g] = at("ha10", [P, 4, HALF], BF16, HA10_AT) if c == 1 else held("ha00", [P, 4, HALF], F32)
-            for t in range(4):
+            for t in slices:
                 bank = bank_at("ha_ps%d%d%d" % (c, g, t), [P, HALF], 4 * (c == g) + t)
                 for a in range(2):
                     nc.tensor.matmul_mx(
@@ -215,7 +224,7 @@ def tile_list_kg_max_bias_kernel(
 
         def project_b(c, g, u):
             words, scales = wbq[g]
-            bank = bank_at("hb_ps%d%d%d" % (c, g, u), [P, 4, UNIT], u if (c, g) == (0, 1) else 4 + u)
+            bank = bank_at("hb_ps%d%d%d" % (c, g, u), [P, 4, UNIT], (u + {(0, 0): 6, (0, 1): 2}[c, g]) % (8 if g == 0 else 4) if c == 0 else 4 + u)
             for t in range(4):
                 nc.tensor.matmul_mx(
                     out=bank[:, t, :],
@@ -238,6 +247,11 @@ def tile_list_kg_max_bias_kernel(
 
         for c, g in ((1, 0), (0, 0), (0, 1)):
             project_a(c, g)
+        ha00_woven = held("ha00_woven", [P, 2 * HALF], BF16)
+        nc.vector.tensor_copy(
+            ha00_woven[:].rearrange("p (j i t) -> p j t i", t=4, i=4),
+            ha[0, 0][:, :, HALF // 2 : HALF].rearrange("p t (j i) -> p j t i", i=4),
+        )
         ha10_woven = at("ha10_woven", [P, 4 * HALF], BF16, HA10_WOVEN_AT)
         nc.vector.tensor_copy(
             ha10_woven[:].rearrange("p (j i t) -> p j t i", t=4, i=4), ha[1, 0][:].rearrange("p t (j i) -> p j t i", i=4)
@@ -246,10 +260,11 @@ def tile_list_kg_max_bias_kernel(
             gather_tab2(0, at("tab2_g0", [P, HALF], U32, TAB2_G0_AT)),
             gather_tab2(1, held("tab2_g1", [P, HALF], U32)),
         ]
-        round_wb(wb_raw1[:, 0], 0, 0, P // 2, nc.scalar.copy, wb_bf[1])
-        round_wb(wb_raw1[:, 1], P // 2, P // 2, SCALAR_SHARE, nc.scalar.copy, wb_bf[1])
-        round_wb(wb_raw1[:, 1], P // 2, SCALAR_SHARE, P, lambda dst, src: nc.gpsimd.tensor_scalar(dst, src, 1.0, 0.0, MULT, ADD), wb_bf[1])
+        round_wb(wb_raw1[0][:], 0, 0, P // 4, nc.scalar.copy, wb_bf[1])
+        round_wb(wb_raw1[0][:], 0, P // 4, P // 2, lambda dst, src: nc.gpsimd.tensor_scalar(dst, src, 1.0, 0.0, MULT, ADD), wb_bf[1])
+        round_wb(wb_raw1[1][:], P // 2, P // 2, P, lambda dst, src: nc.gpsimd.tensor_scalar(dst, src, 1.0, 0.0, MULT, ADD), wb_bf[1])
 
+        project_a(1, 1, range(2))
         h = {}
 
         def quantise_h(c, g, rounded, first, count):
@@ -260,34 +275,6 @@ def tile_list_kg_max_bias_kernel(
                 scales=scales[:, cols],
                 in_=rounded[:, 4 * UNIT * first : 4 * UNIT * (first + count)],
             )
-
-        units = HALF // UNIT
-        for c in range(2):
-            low = at("h_bf10", [P, 4 * HALF], BF16, H_BF10_AT) if c == 1 else held("h_bf00", [P, 4 * HALF], BF16)
-            if c == 0:
-                for u in range(units):
-                    join(c, 0, u, low[:, 4 * UNIT * u : 4 * UNIT * (u + 1)])
-            else:
-                nc.vector.tensor_tensor(low[:], hb10_woven[:], ha10_woven[:], MAX)
-            for g in range(2):
-                words = at("h00", [P, HALF], U32, H00_AT) if (c, g) == (0, 0) else held("h%d%d" % (c, g), [P, HALF], U32)
-                h[c, g] = (words, held("h_sc%d%d" % (c, g), [P, HALF], U8))
-            high = held("h_bf%d1" % c, [P, 4 * HALF], BF16)
-            if c == 0:
-                wbq.append(quantise_wb(1, wb_bf[1]))
-                quantise_h(c, 0, low, 0, units)
-                project_a(1, 1)
-                hb10_woven = held("hb10_woven", [P, 4 * HALF], BF16)
-            for u in range(units):
-                join(c, 1, u, high[:, 4 * UNIT * u : 4 * UNIT * (u + 1)])
-                if c == 1 and u == 0:
-                    quantise_h(c, 0, low, 0, units)
-            quantise_h(c, 1, high, 0, 2)
-            quantise_h(c, 1, high, 2, 2)
-            if c == 0:
-                for u in range(units):
-                    part = hb10_woven[:, 4 * UNIT * u : 4 * UNIT * (u + 1)]
-                    nc.scalar.copy(part.rearrange("p (j i t) -> p j t i", t=4, i=2), project_b(1, 0, u))
 
         out_tiles = out.rearrange("(nt p) j -> p nt j", p=P)
 
@@ -303,16 +290,50 @@ def tile_list_kg_max_bias_kernel(
                 stop=(g == 1),
             )
 
+        def score(c, nt):
+            scores = held("scores%d%d" % (c, nt), [P, HALF], F32)
+            bank = bank_at("y_ps%d%d" % (c, nt), [P, HALF], (nt + 2) % 4 if c == 0 else (nt + 4) % 8)
+            y_pass(bank, c, 0, nt)
+            y_pass(bank, c, 1, nt)
+            if c == 1 and nt % 2 == 0:
+                nc.vector.tensor_scalar_add(scores[:], bank[:], bias[:, nt : nt + 1])
+            else:
+                nc.scalar.activation(scores[:], bank[:], IDENTITY, bias=bias[:, nt : nt + 1])
+            nc.sync.dma_start(out_tiles[:, nt, HALF * c : HALF * (c + 1)], scores[:])
+
+        units = HALF // UNIT
         for c in range(2):
-            groups = [(nt,) for nt in range(N // P)]
-            for group in groups:
-                scores = held("scores%d%d" % (c, group[0]), [P, len(group), HALF], F32)
-                for n, nt in enumerate(group):
-                    bank = bank_at("y_ps%d%d" % (c, nt), [P, HALF], (nt + 4 * c) % (4 * (c + 1)))
-                    y_pass(bank, c, 0, nt)
-                    y_pass(bank, c, 1, nt)
-                    if c == 1 and nt % 2 == 0:
-                        nc.vector.tensor_scalar_add(scores[:, n, :], bank[:], bias[:, nt : nt + 1])
-                    else:
-                        nc.scalar.activation(scores[:, n, :], bank[:], IDENTITY, bias=bias[:, nt : nt + 1])
-                nc.sync.dma_start(out_tiles[:, group[0] : group[-1] + 1, HALF * c : HALF * (c + 1)], scores[:])
+            low = at("h_bf10", [P, 4 * HALF], BF16, H_BF10_AT) if c == 1 else held("h_bf00", [P, 4 * HALF], BF16)
+            if c == 0:
+                for u in range(2):
+                    join(c, 0, u, low[:, 4 * UNIT * u : 4 * UNIT * (u + 1)])
+                hb00_woven = at("hb00_woven", [P, 2 * HALF], BF16, HB00_WOVEN_AT)
+                for u in range(2):
+                    part = hb00_woven[:, 4 * UNIT * u : 4 * UNIT * (u + 1)]
+                    nc.scalar.copy(part.rearrange("p (j i t) -> p j t i", t=4, i=2), project_b(0, 0, 2 + u))
+            else:
+                nc.vector.tensor_tensor(low[:], hb10_woven[:], ha10_woven[:], MAX)
+            for g in range(2):
+                words = at("h00", [P, HALF], U32, H00_AT) if (c, g) == (0, 0) else held("h%d%d" % (c, g), [P, HALF], U32)
+                h[c, g] = (words, held("h_sc%d%d" % (c, g), [P, HALF], U8))
+            high = held("h_bf%d1" % c, [P, 4 * HALF], BF16)
+            if c == 0:
+                wbq.append(quantise_wb(1, wb_bf[1]))
+                nc.vector.tensor_tensor(low[:, 2 * HALF : 4 * HALF], hb00_woven[:], ha00_woven[:], MAX)
+                quantise_h(c, 0, low, 0, units)
+                project_a(1, 1, range(2, 4))
+                hb10_woven = held("hb10_woven", [P, 4 * HALF], BF16)
+            for u in range(units):
+                join(c, 1, u, high[:, 4 * UNIT * u : 4 * UNIT * (u + 1)])
+                if c == 1 and u == 0:
+                    quantise_h(c, 0, low, 0, units)
+            quantise_h(c, 1, high, 0, 2)
+            quantise_h(c, 1, high, 2, 2)
+            if c == 0:
+                for u in range(units):
+                    part = hb10_woven[:, 4 * UNIT * u : 4 * UNIT * (u + 1)]
+                    nc.scalar.copy(part.rearrange("p (j i t) -> p j t i", t=4, i=2), project_b(1, 0, u))
+                score(0, 0)
+
+        for c, nt in [(c, nt) for c in range(2) for nt in range(N // P)][1:]:
+            score(c, nt)

@@ -24,7 +24,7 @@ HALF = 512
 UNIT = 128
 KB = 1024
 BANK = 2 * KB
-WARM_UP = 2
+WARM_UP = 4
 
 ROWS_AT = 96
 TAB2_ROWS_AT = 48
@@ -32,7 +32,7 @@ TAB2_PLANE_AT = 4
 
 TAB_SC_WIN_AT = 15 * KB
 TAB2_WIN_AT, TAB_SC_AT, WB_RAW0_AT = 0, 16 * KB, 18 * KB
-WA_RAW0_AT, WA_RAW1_AT = 64 * KB, 68 * KB
+WA_RAW01_AT, WA_RAW1_AT = 66 * KB, 68 * KB
 WA_SC_RAW_AT = 68 * KB - 512
 TAB_PAIRS0_AT = 84 * KB
 TAB2_SC_WIN_AT = 39 * KB
@@ -90,6 +90,9 @@ def tile_list_kg_max_bias_kernel(
 
         tab_win = held("tab_win", [P, T], U32)
         nc.sync.dma_start(tab_win[:].bitcast(I32), tab_words[0].rearrange("p t i -> p (t i)").bitcast(I32))
+        wa_hbm = wa_words.rearrange("a p r i -> p a (r i)")
+        wa_raw0 = [held("wa_raw00", [P, PASS], I32), at("wa_raw01", [P, PASS], I32, WA_RAW01_AT)]
+        nc.sync.dma_start(wa_raw0[0][:], wa_hbm[:, 0, 0 : 4 * PASS].bitcast(I32))
 
         def deal_rows(plane, rows, first, count, up=0):
             for quadrant in range(4):
@@ -103,10 +106,9 @@ def tile_list_kg_max_bias_kernel(
             wa_sc_ord[:].rearrange("p (g t m) -> p g t m", t=4, m=P), wa_sc_raw[:].rearrange("p (g m t) -> p g t m", t=4, m=P)
         )
         deal_rows(wa_sc, wa_sc_ord, ROWS_AT, 8)
-        wa_hbm = wa_words.rearrange("a p r i -> p a (r i)")
-        wa_raw = [at("wa_raw%d" % g, [P, 2, PASS], I32, offset) for g, offset in enumerate((WA_RAW0_AT, WA_RAW1_AT))]
-        for g in range(2):
-            nc.sync.dma_start(wa_raw[g][:], wa_hbm[:, :, 4 * PASS * g : 4 * PASS * (g + 1)].bitcast(I32))
+        nc.sync.dma_start(wa_raw0[1][:], wa_hbm[:, 1, 0 : 4 * PASS].bitcast(I32))
+        wa_raw1 = at("wa_raw1", [P, 2, PASS], I32, WA_RAW1_AT)
+        nc.sync.dma_start(wa_raw1[:], wa_hbm[:, :, 4 * PASS : 8 * PASS].bitcast(I32))
 
         tab_sc_g = held("tab_sc_g", [P, J], U8)
         nc.vector.tensor_copy(tab_sc_g[:], tab_sc_win[:].indirect(idx[:]))
@@ -138,12 +140,12 @@ def tile_list_kg_max_bias_kernel(
                 for a in range(2):
                     nc.scalar.copy(
                         words[:, a, :].bitcast(U32).rearrange("p (t m i) -> p m t i", t=4, i=4),
-                        wa_raw[g][:, a, :].bitcast(U32).rearrange("p (m i t) -> p m t i", t=4, i=4),
+                        wa_raw0[a][:].bitcast(U32).rearrange("p (m i t) -> p m t i", t=4, i=4),
                     )
             else:
                 nc.vector.tensor_copy(
                     words[:].rearrange("p a (t m i) -> p a m t i", t=4, i=4),
-                    wa_raw[g][:].rearrange("p a (m i t) -> p a m t i", t=4, i=4),
+                    wa_raw1[:].rearrange("p a (m i t) -> p a m t i", t=4, i=4),
                 )
             return words
 
@@ -167,9 +169,9 @@ def tile_list_kg_max_bias_kernel(
         for t in range(WARM_UP):
             nc.tensor.matmul_mx(
                 out=warm[:],
-                lhsT=wa_raw[0][:, 0, P * t : P * (t + 1)].bitcast(FP8X4),
+                lhsT=wa_raw0[0][:, P * t : P * (t + 1)].bitcast(FP8X4),
                 lhsT_scale=wa_sc_ord[:, P * t : P * (t + 1)],
-                rhs=wa_raw[0][:, 1, :].bitcast(FP8X4),
+                rhs=wa_raw0[0][:].bitcast(FP8X4),
                 rhs_scale=wa_sc_ord[:, 0:PASS],
                 start=True,
                 stop=True,
@@ -319,14 +321,14 @@ def tile_list_kg_max_bias_kernel(
             high = held("h_bf%d1" % c, [P, 4 * HALF], BF16)
             if c == 0:
                 wbq.append(quantise_wb(1, wb_bf[1]))
+                quantise_h(c, 0, low, 0, 2)
                 nc.vector.tensor_tensor(low[:, 2 * HALF : 4 * HALF], hb00_woven[:], ha00_woven[:], MAX)
-                quantise_h(c, 0, low, 0, units)
                 project_a(1, 1, range(2, 4))
                 hb10_woven = held("hb10_woven", [P, 4 * HALF], BF16)
             for u in range(units):
                 join(c, 1, u, high[:, 4 * UNIT * u : 4 * UNIT * (u + 1)])
-                if c == 1 and u == 0:
-                    quantise_h(c, 0, low, 0, units)
+                if u == 0:
+                    quantise_h(c, 0, low, 2 - 2 * c, 2 + 2 * c)
             quantise_h(c, 1, high, 0, 2)
             quantise_h(c, 1, high, 2, 2)
             if c == 0:

@@ -31,14 +31,14 @@ TAB2_ROWS_AT = 48
 TAB2_PLANE_AT = 4
 
 TAB_SC_WIN_AT = 15 * KB
-TAB2_WIN_AT, TAB_SC_AT, WB_RAW0_AT = 0, 16 * KB, 18 * KB
+TAB2_WIN_AT, TAB_SC_AT, WB_RAW0_AT = 0, 16 * KB + 64, 18 * KB + 512
 WA_RAW01_AT, WA_RAW1_AT = 66 * KB, 68 * KB
 WA_SC_RAW_AT = 68 * KB - 512
 TAB_PAIRS0_AT = 84 * KB
 TAB2_SC_WIN_AT = 39 * KB
-WB_RAW1_AT, TAB2_SC_AT, BIAS_AT, EN_AT = (35 * KB + 256, 80 * KB + 512), 40 * KB, 84 * KB + 512, 85 * KB
+WB_RAW1_AT, TAB2_SC_AT, BIAS_AT, EN_AT = (35 * KB + 256, 80 * KB + 512), 40 * KB + 64, 84 * KB + 512, 85 * KB + 128
 HB00_WOVEN_AT = 37 * KB + 256
-EN_SC_AT = 68 * KB
+EN_SC_AT = 68 * KB + 192
 WB_BF1_AT = 56 * KB
 H00_AT = 56 * KB
 WB_BF0_AT = 72 * KB
@@ -61,10 +61,16 @@ def tile_list_kg_max_bias_kernel(
         psum = ctx.enter_context(tc.psum_pool(name="psum", bufs=1))
 
         def held(name, shape, dtype):
-            return keep.tile(shape, dtype, name=name, tag=name, align_bytes=64)
+            return keep.tile(shape, dtype, name=name, tag=name, align_bytes=256)
+
+        def shifted(name, shape, dtype, shift):
+            size = {U8: 1, U32: 4, I32: 4}[dtype]
+            count = shape[1] * (shape[2] if len(shape) == 3 else 1)
+            flat = held(name, [P, count + 256 // size], dtype)[:, shift // size : shift // size + count]
+            return flat.rearrange("p (a n) -> p a n", a=shape[1]) if len(shape) == 3 else flat
 
         def at(name, shape, dtype, offset):
-            return placed.tile(shape, dtype, name=name, tag=name, align_bytes=64, offset=offset)
+            return placed.tile(shape, dtype, name=name, tag=name, align_bytes=64 if offset % 256 else 256, offset=offset)
 
         def bank_at(name, shape, index):
             return psum.tile(shape, F32, name=name, tag=name, offset=index * BANK)
@@ -82,7 +88,7 @@ def tile_list_kg_max_bias_kernel(
         nc.vector.memset(wa_sc_raw[0:ROWS_AT, :].bitcast(I32), 0)
         nc.vector.memset(tab_sc_win[0:ROWS_AT, :].bitcast(I32), 0)
         tab_sc = at("tab_sc", [P, 2, J], U8, TAB_SC_AT)
-        wa_sc = held("wa_sc", [P, 2, R], U8)
+        wa_sc = shifted("wa_sc", [P, 2, R], U8, 192)
         tab2_sc = at("tab2_sc", [P, J], U8, TAB2_SC_AT)
         nc.gpsimd.memset(wa_sc[:].bitcast(I32), 0)
         nc.gpsimd.memset(tab2_sc_win[0:TAB2_ROWS_AT, :].bitcast(I32), 0)
@@ -135,7 +141,7 @@ def tile_list_kg_max_bias_kernel(
             return words
 
         def order_wa_words(g):
-            words = held("wa%d" % g, [P, 2, PASS], I32)
+            words = shifted("wa%d" % g, [P, 2, PASS], I32, 128)
             if g == 0:
                 for a in range(2):
                     nc.scalar.copy(
@@ -160,8 +166,8 @@ def tile_list_kg_max_bias_kernel(
             )
 
         def quantise_wb(g, rounded):
-            words = held("wb%d" % g, [P, PASS], U32)
-            scales = held("wb_sc%d" % g, [P, PASS], U8)
+            words = shifted("wb%d" % g, [P, PASS], U32, 128)
+            scales = shifted("wb_sc%d" % g, [P, PASS], U8, 192)
             nc.vector.quantize_mx(out=words[:].bitcast(FP8X4), scales=scales[:], in_=rounded[:])
             return words, scales
 
@@ -317,7 +323,7 @@ def tile_list_kg_max_bias_kernel(
                 nc.vector.tensor_tensor(low[:], hb10_woven[:], ha10_woven[:], MAX)
             for g in range(2):
                 words = at("h00", [P, HALF], U32, H00_AT) if (c, g) == (0, 0) else held("h%d%d" % (c, g), [P, HALF], U32)
-                h[c, g] = (words, held("h_sc%d%d" % (c, g), [P, HALF], U8))
+                h[c, g] = (words, shifted("h_sc%d%d" % (c, g), [P, HALF], U8, 64))
             high = held("h_bf%d1" % c, [P, 4 * HALF], BF16)
             if c == 0:
                 wbq.append(quantise_wb(1, wb_bf[1]))

@@ -31,12 +31,12 @@ TAB2_ROWS_AT = 48
 TAB2_PLANE_AT = 4
 
 TAB_SC_WIN_AT = 15 * KB
-TAB2_WIN_AT, TAB_SC_AT, WB_RAW0_AT = 0, 16 * KB + 64, 18 * KB + 512
+TAB2_WIN_AT, TAB_SC_AT, WB_RAW0_AT = 0, 16 * KB + 128, 18 * KB + 512
 WA_RAW01_AT, WA_RAW1_AT = 66 * KB, 68 * KB
 WA_SC_RAW_AT = 68 * KB - 512
 TAB_PAIRS0_AT = 84 * KB
 TAB2_SC_WIN_AT = 39 * KB
-WB_RAW1_AT, TAB2_SC_AT, BIAS_AT, EN_AT = (35 * KB + 256, 80 * KB + 512), 40 * KB + 64, 84 * KB + 512, 85 * KB + 128
+WB_RAW1_AT, TAB2_SC_AT, BIAS_AT, EN_AT = (35 * KB + 256, 80 * KB + 512), 40 * KB + 128, 84 * KB + 512, 85 * KB + 64
 HB00_WOVEN_AT = 37 * KB + 256
 EN_SC_AT = 68 * KB + 192
 WB_BF1_AT = 56 * KB
@@ -141,7 +141,7 @@ def tile_list_kg_max_bias_kernel(
             return words
 
         def order_wa_words(g):
-            words = shifted("wa%d" % g, [P, 2, PASS], I32, 128)
+            words = shifted("wa%d" % g, [P, 2, PASS], I32, 64)
             if g == 0:
                 for a in range(2):
                     nc.scalar.copy(
@@ -166,7 +166,7 @@ def tile_list_kg_max_bias_kernel(
             )
 
         def quantise_wb(g, rounded):
-            words = shifted("wb%d" % g, [P, PASS], U32, 128)
+            words = shifted("wb%d" % g, [P, PASS], U32, 64)
             scales = shifted("wb_sc%d" % g, [P, PASS], U8, 192)
             nc.vector.quantize_mx(out=words[:].bitcast(FP8X4), scales=scales[:], in_=rounded[:])
             return words, scales
@@ -323,7 +323,7 @@ def tile_list_kg_max_bias_kernel(
                 nc.vector.tensor_tensor(low[:], hb10_woven[:], ha10_woven[:], MAX)
             for g in range(2):
                 words = at("h00", [P, HALF], U32, H00_AT) if (c, g) == (0, 0) else held("h%d%d" % (c, g), [P, HALF], U32)
-                h[c, g] = (words, shifted("h_sc%d%d" % (c, g), [P, HALF], U8, 64))
+                h[c, g] = (words, shifted("h_sc%d%d" % (c, g), [P, HALF], U8, 128))
             high = held("h_bf%d1" % c, [P, 4 * HALF], BF16)
             if c == 0:
                 wbq.append(quantise_wb(1, wb_bf[1]))

@@ -30,6 +30,8 @@ ROWS_AT = 96
 TAB2_ROWS_AT = 48
 TAB2_PLANE_AT = 4
 
+PORTS_IN_TURN = (0, 2, 1, 3)
+
 TAB_SC_WIN_AT = 15 * KB
 TAB2_WIN_AT, TAB_SC_AT, WB_RAW0_AT = 0, 16 * KB + 128, 18 * KB + 512
 WA_RAW01_AT, WA_RAW1_AT = 66 * KB, 68 * KB
@@ -101,7 +103,7 @@ def tile_list_kg_max_bias_kernel(
         nc.sync.dma_start(wa_raw0[0][:], wa_hbm[:, 0, 0 : 4 * PASS].bitcast(I32))
 
         def deal_rows(plane, rows, first, count, up=0):
-            for quadrant in range(4):
+            for quadrant in PORTS_IN_TURN:
                 nc.sync.dma_start(
                     plane[32 * quadrant + up : 32 * quadrant + up + 4].bitcast(I32),
                     rows[first + count * quadrant : first + count * (quadrant + 1), :].bitcast(I32),
@@ -201,7 +203,7 @@ def tile_list_kg_max_bias_kernel(
         wbq = [quantise_wb(0, wb_bf[0])]
 
         en_sc = at("en_sc", [P, 2, N], U8, EN_SC_AT)
-        for quadrant in range(4):
+        for quadrant in PORTS_IN_TURN:
             nc.sync.dma_start(
                 en_sc[32 * quadrant : 32 * quadrant + 4, :, :].bitcast(I32),
                 en_scales[:, 4 * quadrant : 4 * quadrant + 4, :].rearrange("g s n -> s g n").bitcast(I32),

from contextlib import ExitStack

import concourse.mybir as mybir

K, L, R, N, T, J = 1024, 512, 1024, 1024, 4096, 1024
FLOPS = 2 * J * (K * R + L * R + R * N)

F32 = mybir.dt.float32
BF16 = mybir.dt.bfloat16
I32 = mybir.dt.int32
U32 = mybir.dt.uint32
U16 = mybir.dt.uint16
U8 = mybir.dt.uint8
FP8X4 = mybir.dt.float8_e4m3fn_x4
FP4X4 = mybir.dt.float4_e2m1fn_x4
MAX = mybir.AluOpType.max
MULT = mybir.AluOpType.mult
ADD = mybir.AluOpType.add
IDENTITY = mybir.ActivationFunctionType.Identity

P = 128
PASS = 512
HALF = 512
UNIT = 128
KB = 1024
BANK = 2 * KB
WARM_UP = 4

ROWS_AT = 96
TAB2_ROWS_AT = 48
TAB2_PLANE_AT = 4

PORTS_IN_TURN = (0, 2, 1, 3)

TAB_SC_WIN_AT = 15 * KB
TAB2_WIN_AT, TAB_SC_AT, WB_RAW0_AT = 0, 16 * KB + 128, 18 * KB + 512
WA_RAW01_AT, WA_RAW1_AT = 66 * KB, 68 * KB
WA_SC_RAW_AT = 68 * KB - 512
TAB_PAIRS0_AT = 84 * KB
TAB2_SC_WIN_AT = 39 * KB
WB_RAW1_AT, TAB2_SC_AT, BIAS_AT, EN_AT = (35 * KB + 256, 80 * KB + 512), 40 * KB + 128, 84 * KB + 512, 85 * KB + 64
HB00_WOVEN_AT = 37 * KB + 256
EN_SC_AT = 68 * KB + 192
WB_BF1_AT = 56 * KB
H00_AT = 56 * KB
WB_BF0_AT = 72 * KB
HA10_WOVEN_AT = 72 * KB
HA10_AT = 60 * KB
TAB2_G0_AT = 60 * KB
HA01_AT = 48 * KB
HA11_AT = 29 * KB + 256
H_BF10_AT = 48 * KB


def tile_list_kg_max_bias_kernel(
    tc, tab_words, tab_scales, tab2_words, tab2_scales, wa_words, wa_scales, wb, en_words, en_scales, b, offs, offs2, out
):
    nc = tc.nc
    with ExitStack() as ctx:
        lists = ctx.enter_context(tc.tile_pool(name="lists", bufs=1))
        keep = ctx.enter_context(tc.tile_pool(name="keep", bufs=1))
        placed = ctx.enter_context(tc.tile_pool(name="placed", bufs=1))
        psum = ctx.enter_context(tc.psum_pool(name="psum", bufs=1))

        def held(name, shape, dtype):
            return keep.tile(shape, dtype, name=name, tag=name, align_bytes=256)

        def shifted(name, shape, dtype, shift):
            size = {U8: 1, U32: 4, I32: 4}[dtype]
            count = shape[1] * (shape[2] if len(shape) == 3 else 1)
            flat = held(name, [P, count + 256 // size], dtype)[:, shift // size : shift // size + count]
            return flat.rearrange("p (a n) -> p a n", a=shape[1]) if len(shape) == 3 else flat

        def at(name, shape, dtype, offset):
            return placed.tile(shape, dtype, name=name, tag=name, align_bytes=64 if offset % 256 else 256, offset=offset)

        def bank_at(name, shape, index):
            return psum.tile(shape, F32, name=name, tag=name, offset=index * BANK)

        idx = lists.tile([P, J // 16], U16, name="idx")
        idx2 = lists.tile([P, J // 16], U16, name="idx2")
        tab_sc_win = at("tab_sc_win", [P, T], U8, TAB_SC_WIN_AT)
        wa_sc_raw = at("wa_sc_raw", [P, R], U8, WA_SC_RAW_AT)
        tab2_sc_win = at("tab2_sc_win", [P, T], U8, TAB2_SC_WIN_AT)
        nc.sync.dma_start(wa_sc_raw[ROWS_AT:P, :].bitcast(I32), wa_scales.rearrange("a q r -> q a r").bitcast(I32))
        nc.sync.dma_start(idx[:], offs)
        nc.sync.dma_start(tab_sc_win[ROWS_AT:P, :].bitcast(I32), tab_scales.rearrange("a q t -> q a t").bitcast(I32))
        nc.sync.dma_start(idx2[:], offs2)
        nc.sync.dma_start(tab2_sc_win[TAB2_ROWS_AT : TAB2_ROWS_AT + 16, :].bitcast(I32), tab2_scales[0].bitcast(I32))
        nc.vector.memset(wa_sc_raw[0:ROWS_AT, :].bitcast(I32), 0)
        nc.vector.memset(tab_sc_win[0:ROWS_AT, :].bitcast(I32), 0)
        tab_sc = at("tab_sc", [P, 2, J], U8, TAB_SC_AT)
        wa_sc = shifted("wa_sc", [P, 2, R], U8, 192)
        tab2_sc = at("tab2_sc", [P, J], U8, TAB2_SC_AT)
        nc.gpsimd.memset(wa_sc[:].bitcast(I32), 0)
        nc.gpsimd.memset(tab2_sc_win[0:TAB2_ROWS_AT, :].bitcast(I32), 0)
        nc.gpsimd.memset(tab2_sc_win[TAB2_ROWS_AT + 16 : P, :].bitcast(I32), 0)

        tab_win = held("tab_win", [P, T], U32)
        nc.sync.dma_start(tab_win[:].bitcast(I32), tab_words[0].rearrange("p t i -> p (t i)").bitcast(I32))
        wa_hbm = wa_words.rearrange("a p r i -> p a (r i)")
        wa_raw0 = [held("wa_raw00", [P, PASS], I32), at("wa_raw01", [P, PASS], I32, WA_RAW01_AT)]
        nc.sync.dma_start(wa_raw0[0][:], wa_hbm[:, 0, 0 : 4 * PASS].bitcast(I32))

        def deal_rows(plane, rows, first, count, up=0):
            for quadrant in PORTS_IN_TURN:
                nc.sync.dma_start(
                    plane[32 * quadrant + up : 32 * quadrant + up + 4].bitcast(I32),
                    rows[first + count * quadrant : first + count * (quadrant + 1), :].bitcast(I32),
                )

        wa_sc_ord = held("wa_sc_ord", [P, R], U8)
        nc.vector.tensor_copy(
            wa_sc_ord[:].rearrange("p (g t m) -> p g t m", t=4, m=P), wa_sc_raw[:].rearrange("p (g m t) -> p g t m", t=4, m=P)
        )
        deal_rows(wa_sc, wa_sc_ord, ROWS_AT, 8)
        nc.sync.dma_start(wa_raw0[1][:], wa_hbm[:, 1, 0 : 4 * PASS].bitcast(I32))
        wa_raw1 = at("wa_raw1", [P, 2, PASS], I32, WA_RAW1_AT)
        nc.sync.dma_start(wa_raw1[:], wa_hbm[:, :, 4 * PASS : 8 * PASS].bitcast(I32))

        tab_sc_g = held("tab_sc_g", [P, J], U8)
        nc.vector.tensor_copy(tab_sc_g[:], tab_sc_win[:].indirect(idx[:]))
        deal_rows(tab_sc, tab_sc_g, ROWS_AT, 8)
        wb_hbm = wb.rearrange("(p i) r -> p i r", i=4)
        wb_raw = [at("wb_raw0", [P, 4, PASS], F32, WB_RAW0_AT)]
        nc.sync.dma_start(wb_raw[0][:], wb_hbm[:, :, 0:PASS])
        tab2_win = at("tab2_win", [P, T], U32, TAB2_WIN_AT)
        nc.sync.dma_start(tab2_win[:].bitcast(I32), tab2_words[0].rearrange("p t i -> p (t i)").bitcast(I32))

        tab2_sc_g = held("tab2_sc_g", [P, J], U8)
        nc.vector.tensor_copy(tab2_sc_g[:], tab2_sc_win[:].indirect(idx2[:]))
        deal_rows(tab2_sc, tab2_sc_g, TAB2_ROWS_AT, 4, TAB2_PLANE_AT)
        wb_raw1 = [at("wb_raw10", [P, 4, PASS // 2], F32, WB_RAW1_AT[0])]
        nc.sync.dma_start(wb_raw1[0][:], wb_hbm[:, :, PASS : PASS + PASS // 2])

        def list_half(offsets, c):
            return offsets[:, c * HALF // 16 : (c + 1) * HALF // 16]

        def gather_tab(c, pairs):
            words = held("tab_g%d" % c, [P, 2, 2 * HALF], U8)
            nc.vector.tensor_copy(pairs[:], tab_win[:].indirect(list_half(idx, c)))
            nc.vector.tensor_copy(words[:].bitcast(U16), pairs[:].bitcast(U16).rearrange("p (j d) -> p d j", d=2))
            return words

        def order_wa_words(g):
            words = shifted("wa%d" % g, [P, 2, PASS], I32, 64)
            if g == 0:
                for a in range(2):
                    nc.scalar.copy(
                        words[:, a, :].bitcast(U32).rearrange("p (t m i) -> p m t i", t=4, i=4),
                        wa_raw0[a][:].bitcast(U32).rearrange("p (m i t) -> p m t i", t=4, i=4),
                    )
            else:
                nc.vector.tensor_copy(
                    words[:].rearrange("p a (t m i) -> p a m t i", t=4, i=4),
                    wa_raw1[:].rearrange("p a (m i t) -> p a m t i", t=4, i=4),
                )
            return words

        def gather_tab2(c, words):
            nc.vector.tensor_copy(words[:], tab2_win[:].indirect(list_half(idx2, c)))
            return words

        def round_wb(raw, raw_first, first, last, copy, rounded):
            copy(
                rounded[:].rearrange("p (t m i) -> p m t i", t=4, i=4)[:, first:last],
                raw.rearrange("p i (m t) -> p m t i", t=4)[:, first - raw_first : last - raw_first],
            )

        def quantise_wb(g, rounded):
            words = shifted("wb%d" % g, [P, PASS], U32, 64)
            scales = shifted("wb_sc%d" % g, [P, PASS], U8, 192)
            nc.vector.quantize_mx(out=words[:].bitcast(FP8X4), scales=scales[:], in_=rounded[:])
            return words, scales

        warm = bank_at("warm", [P, HALF], 7)
        for t in range(WARM_UP):
            nc.tensor.matmul_mx(
                out=warm[:],
                lhsT=wa_raw0[0][:, P * t : P * (t + 1)].bitcast(FP8X4),
                lhsT_scale=wa_sc_ord[:, P * t : P * (t + 1)],
                rhs=wa_raw0[0][:].bitcast(FP8X4),
                rhs_scale=wa_sc_ord[:, 0:PASS],
                start=True,
                stop=True,
            )

        tab_g = {1: gather_tab(1, at("tab_pairs1", [P, HALF], U32, TAB_PAIRS0_AT))}
        wa = [order_wa_words(0)]
        tab_g[0] = gather_tab(0, at("tab_pairs0", [P, HALF], U32, TAB_PAIRS0_AT))
        wa.append(order_wa_words(1))
        wb_raw1.append(at("wb_raw11", [P, 4, PASS // 2], F32, WB_RAW1_AT[1]))
        nc.sync.dma_start(wb_raw1[1][:], wb_hbm[:, :, PASS + PASS // 2 : R])

        en = at("en", [P, 2, 2 * N], U8, EN_AT)
        nc.sync.dma_start(en[:].bitcast(I32), en_words.rearrange("g p x -> p g x").bitcast(I32))
        bias = at("bias", [P, N // P], F32, BIAS_AT)
        with nc.allow_non_contiguous_dma(reason="one bias value for each partition and tile of candidates"):
            nc.sync.dma_start(bias[:], b.rearrange("(nt p) -> p nt", p=P))

        wb_bf = [at("wb_bf0", [P, 4 * PASS], BF16, WB_BF0_AT), at("wb_bf1", [P, 4 * PASS], BF16, WB_BF1_AT)]
        round_wb(wb_raw[0][:], 0, 0, P, nc.vector.tensor_copy, wb_bf[0])
        wbq = [quantise_wb(0, wb_bf[0])]

        en_sc = at("en_sc", [P, 2, N], U8, EN_SC_AT)
        for quadrant in PORTS_IN_TURN:
            nc.sync.dma_start(
                en_sc[32 * quadrant : 32 * quadrant + 4, :, :].bitcast(I32),
                en_scales[:, 4 * quadrant : 4 * quadrant + 4, :].rearrange("g s n -> s g n").bitcast(I32),
            )

        ha = {}

        def project_a(c, g, slices=range(4)):
            if (c, g) in ha:
                pass
            elif g == 1:
                ha[c, g] = at("ha%d1" % c, [P, 4, HALF], F32, (HA01_AT, HA11_AT)[c])
            else:
                ha[c, g] = at("ha10", [P, 4, HALF], BF16, HA10_AT) if c == 1 else held("ha00", [P, 4, HALF], F32)
            for t in slices:
                bank = bank_at("ha_ps%d%d%d" % (c, g, t), [P, HALF], 4 * (c == g) + t)
                for a in range(2):
                    nc.tensor.matmul_mx(
                        out=bank[:],
                        lhsT=wa[g][:, a, P * t : P * (t + 1)].bitcast(FP8X4),
                        lhsT_scale=wa_sc[:, a, PASS * g + P * t : PASS * g + P * (t + 1)],
                        rhs=tab_g[c][:, a, :].bitcast(FP4X4),
                        rhs_scale=tab_sc[:, a, HALF * c : HALF * (c + 1)],
                        start=(a == 0),
                        stop=(a == 1),
                    )
                nc.scalar.copy(ha[c, g][:, t, :], bank[:])

        def project_b(c, g, u):
            words, scales = wbq[g]
            bank = bank_at("hb_ps%d%d%d" % (c, g, u), [P, 4, UNIT], (u + {(0, 0): 6, (0, 1): 2}[c, g]) % (8 if g == 0 else 4) if c == 0 else 4 + u)
            for t in range(4):
                nc.tensor.matmul_mx(
                    out=bank[:, t, :],
                    lhsT=words[:, P * t : P * (t + 1)].bitcast(FP8X4),
                    lhsT_scale=scales[:, P * t : P * (t + 1)],
                    rhs=tab2_g[c][:, UNIT * u : UNIT * (u + 1)].bitcast(FP8X4),
                    rhs_scale=tab2_sc[TAB2_PLANE_AT:P, HALF * c + UNIT * u : HALF * c + UNIT * (u + 1)],
                    start=True,
                    stop=True,
                )
            return bank[:].rearrange("p t (j i) -> p j t i", i=2)

        def join(c, g, u, rounded):
            nc.vector.tensor_tensor(
                rounded.rearrange("p (j i t) -> p j t i", t=4, i=2),
                project_b(c, g, u),
                ha[c, g][:, :, UNIT * u : UNIT * (u + 1)].rearrange("p t (j i) -> p j t i", i=2),
                MAX,
            )

        for c, g in ((1, 0), (0, 0), (0, 1)):
            project_a(c, g)
        ha00_woven = held("ha00_woven", [P, 2 * HALF], BF16)
        nc.vector.tensor_copy(
            ha00_woven[:].rearrange("p (j i t) -> p j t i", t=4, i=4),
            ha[0, 0][:, :, HALF // 2 : HALF].rearrange("p t (j i) -> p j t i", i=4),
        )
        ha10_woven = at("ha10_woven", [P, 4 * HALF], BF16, HA10_WOVEN_AT)
        nc.vector.tensor_copy(
            ha10_woven[:].rearrange("p (j i t) -> p j t i", t=4, i=4), ha[1, 0][:].rearrange("p t (j i) -> p j t i", i=4)
        )
        tab2_g = [
            gather_tab2(0, at("tab2_g0", [P, HALF], U32, TAB2_G0_AT)),
            gather_tab2(1, held("tab2_g1", [P, HALF], U32)),
        ]
        round_wb(wb_raw1[0][:], 0, 0, P // 4, nc.scalar.copy, wb_bf[1])
        round_wb(wb_raw1[0][:], 0, P // 4, P // 2, lambda dst, src: nc.gpsimd.tensor_scalar(dst, src, 1.0, 0.0, MULT, ADD), wb_bf[1])
        round_wb(wb_raw1[1][:], P // 2, P // 2, P, lambda dst, src: nc.gpsimd.tensor_scalar(dst, src, 1.0, 0.0, MULT, ADD), wb_bf[1])

        project_a(1, 1, range(2))
        h = {}

        def quantise_h(c, g, rounded, first, count):
            words, scales = h[c, g]
            cols = slice(UNIT * first, UNIT * (first + count))
            nc.vector.quantize_mx(
                out=words[:, cols].bitcast(FP8X4),
                scales=scales[:, cols],
                in_=rounded[:, 4 * UNIT * first : 4 * UNIT * (first + count)],
            )

        out_tiles = out.rearrange("(nt p) j -> p nt j", p=P)

        def y_pass(bank, c, g, nt):
            words, scales = h[c, g]
            nc.tensor.matmul_mx(
                out=bank[:],
                lhsT=en[:, g, 2 * P * nt : 2 * P * (nt + 1)].bitcast(FP4X4),
                lhsT_scale=en_sc[:, g, P * nt : P * (nt + 1)],
                rhs=words[:].bitcast(FP8X4),
                rhs_scale=scales[:],
                start=(g == 0),
                stop=(g == 1),
            )

        def score(c, nt):
            scores = held("scores%d%d" % (c, nt), [P, HALF], F32)
            bank = bank_at("y_ps%d%d" % (c, nt), [P, HALF], (nt + 2) % 4 if c == 0 else (nt + 4) % 8)
            y_pass(bank, c, 0, nt)
            y_pass(bank, c, 1, nt)
            if c == 1 and nt % 2 == 0:
                nc.vector.tensor_scalar_add(scores[:], bank[:], bias[:, nt : nt + 1])
            else:
                nc.scalar.activation(scores[:], bank[:], IDENTITY, bias=bias[:, nt : nt + 1])
            nc.sync.dma_start(out_tiles[:, nt, HALF * c : HALF * (c + 1)], scores[:])

        units = HALF // UNIT
        for c in range(2):
            low = at("h_bf10", [P, 4 * HALF], BF16, H_BF10_AT) if c == 1 else held("h_bf00", [P, 4 * HALF], BF16)
            if c == 0:
                for u in range(2):
                    join(c, 0, u, low[:, 4 * UNIT * u : 4 * UNIT * (u + 1)])
                hb00_woven = at("hb00_woven", [P, 2 * HALF], BF16, HB00_WOVEN_AT)
                for u in range(2):
                    part = hb00_woven[:, 4 * UNIT * u : 4 * UNIT * (u + 1)]
                    nc.scalar.copy(part.rearrange("p (j i t) -> p j t i", t=4, i=2), project_b(0, 0, 2 + u))
            else:
                nc.vector.tensor_tensor(low[:], hb10_woven[:], ha10_woven[:], MAX)
            for g in range(2):
                words = at("h00", [P, HALF], U32, H00_AT) if (c, g) == (0, 0) else held("h%d%d" % (c, g), [P, HALF], U32)
                h[c, g] = (words, shifted("h_sc%d%d" % (c, g), [P, HALF], U8, 128))
            high = held("h_bf%d1" % c, [P, 4 * HALF], BF16)
            if c == 0:
                wbq.append(quantise_wb(1, wb_bf[1]))
                quantise_h(c, 0, low, 0, 2)
                nc.vector.tensor_tensor(low[:, 2 * HALF : 4 * HALF], hb00_woven[:], ha00_woven[:], MAX)
                project_a(1, 1, range(2, 4))
                hb10_woven = held("hb10_woven", [P, 4 * HALF], BF16)
            for u in range(units):
                join(c, 1, u, high[:, 4 * UNIT * u : 4 * UNIT * (u + 1)])
                if u == 0:
                    quantise_h(c, 0, low, 2 - 2 * c, 2 + 2 * c)
            quantise_h(c, 1, high, 0, 2)
            quantise_h(c, 1, high, 2, 2)
            if c == 0:
                for u in range(units):
                    part = hb10_woven[:, 4 * UNIT * u : 4 * UNIT * (u + 1)]
                    nc.scalar.copy(part.rearrange("p (j i t) -> p j t i", t=4, i=2), project_b(1, 0, u))
                score(0, 0)

        for c, nt in [(c, nt) for c in range(2) for nt in range(N // P)][1:]:
            score(c, nt)
